import numpy as np
import ml_dtypes


def mxq(x, axis, fmt="e4m3"):
    dtype, down = {"e4m3": (ml_dtypes.float8_e4m3fn, 7), "e5m2": (ml_dtypes.float8_e5m2, 14)}[fmt]
    v = np.moveaxis(np.asarray(x, np.float32).astype(ml_dtypes.bfloat16).astype(np.float64), axis, -1)
    blocks = v.reshape(v.shape[:-1] + (-1, 32))
    amax = np.abs(blocks).max(-1, keepdims=True)
    byte = np.maximum(np.where(amax > 0, np.frexp(amax)[1] - 1 + 127, 0) - down, 1)
    scale = np.exp2(byte - 127.0)
    codes = (blocks / scale).astype(np.float32).astype(dtype).astype(np.float64)
    return np.moveaxis((codes * scale).reshape(v.shape), -1, axis)


WIDE = False


def mx_kscale(k):
    if not WIDE:
        return np.ones(k)
    levels = np.array([24, -24, 12, -12, 0])
    if k % 512:
        return np.exp2(np.random.permutation(np.resize(levels, k // 32))).repeat(32)
    a = np.empty((k // 512, 16))
    for p in range(k // 512):
        a[p, :8] = np.random.permutation(np.resize(levels, 8))
        for g in range(8):
            far = levels[np.abs(levels - a[p, g]) >= 10]
            a[p, g + 8] = far[np.random.randint(len(far))]
    return np.exp2(a.ravel()).repeat(32)


def f64(x):
    return np.asarray(x).astype(np.float64)


def striped(idx):
    return np.tile(idx.reshape(-1, 16).T, (8, 1)).astype(np.uint16)


def unstriped(offs):
    return offs[:16].T.reshape(-1).astype(np.int64)


E2M1 = np.array([0.0, 0.5, 1.0, 1.5, 2.0, 3.0, 4.0, 6.0, -0.0, -0.5, -1.0, -1.5, -2.0, -3.0, -4.0, -6.0])


def pack_weight(w, fmt):
    k, n = w.shape
    w = f64(np.asarray(w, np.float32).astype(ml_dtypes.bfloat16)).reshape(k // 32, 32, n)
    amax = np.abs(w).max(1)
    if fmt == "e4m3":
        byte = np.frexp(amax)[1] - 1 + 127 - 7
    else:
        mant, ex = np.frexp(amax / 6.0)
        byte = np.where(mant > 0.5, ex, ex - 1) + 127
    byte = np.clip(np.where(amax > 0, byte, 1), 1, 254)
    scaled = (w * np.exp2(127.0 - byte)[:, None, :]).reshape(k, n).astype(np.float32)
    by_word = np.ascontiguousarray(scaled.reshape(k // 512, 128, 4, n).transpose(0, 1, 3, 2))
    if fmt == "e4m3":
        words = by_word.astype(ml_dtypes.float8_e4m3fn).view(np.uint8)
    else:
        c = by_word.astype(ml_dtypes.float4_e2m1fn).view(np.uint8) & 0xF
        words = (c[..., 0::2] | (c[..., 1::2] << 4)).reshape(k // 512, 128, 2 * n)
    return np.ascontiguousarray(words), np.ascontiguousarray(byte.astype(np.uint8).reshape(k // 512, 16, n))


def unpack_weight(words, scales, fmt):
    g, _, n = scales.shape
    words = np.ascontiguousarray(words).reshape(g, 128, n, -1)
    if fmt == "e4m3":
        vals = words.view(ml_dtypes.float8_e4m3fn).astype(np.float64)
    else:
        nib = np.empty((g, 128, n, 4), np.uint8)
        nib[..., 0::2] = words & 0xF
        nib[..., 1::2] = words >> 4
        vals = E2M1[nib]
    vals = vals * np.repeat(np.exp2(scales.astype(np.float64) - 127.0), 8, axis=1)[..., None]
    return vals.transpose(0, 1, 3, 2).reshape(g * 512, n)


def planes(y):
    n, m = y.shape
    v = y.astype(np.float32).astype(ml_dtypes.bfloat16).astype(np.float64).reshape(n // 32, 32, m)
    top = np.abs(v).max(1)
    byte = np.clip(np.where(top > 0, np.frexp(top)[1] - 1 + 127 - 7, 1), 1, 254)
    codes = (v * np.exp2(127.0 - byte)[:, None, :]).reshape(n, m).astype(np.float32).astype(ml_dtypes.float8_e4m3fn).view(np.uint8)
    words = codes.reshape(n // 512, 128, 4, m).transpose(0, 1, 3, 2)
    return np.ascontiguousarray(words), np.ascontiguousarray(byte.astype(np.uint8).reshape(n // 512, 16, m))


def silu(f):
    return f / (1.0 + np.exp(-np.maximum(f, -700.0)))


K, R, N, T, J = 512, 1024, 512, 2048, 1024


def setup_inputs():
    n = np.random.standard_normal
    s = mx_kscale(K)[:, None]
    u = mx_kscale(R)[:, None]
    wd = n((R, N)) / np.sqrt(R) / u
    p_tab = pack_weight(n((K, T)) * s, "e4m3")
    p_wd8 = pack_weight(wd[:512], "e4m3")
    p_wd4 = pack_weight(wd[512:], "e2m1")
    return {
        "tab_words": p_tab[0],
        "tab_scales": p_tab[1],
        "wg": (n((K, R)) / np.sqrt(K) / s).astype(np.float32),
        "wu": (n((K, R)) / np.sqrt(K) / s * u.T).astype(np.float32),
        "wd8_words": p_wd8[0],
        "wd8_scales": p_wd8[1],
        "wd4_words": p_wd4[0],
        "wd4_scales": p_wd4[1],
        "gT": (n((N, T))).astype(np.float32),
        "offs": striped(np.random.permutation(T)[:J]),
    }


def reference(tab_words, tab_scales, wg, wu, wd8_words, wd8_scales, wd4_words, wd4_scales, gT, offs):
    idx = unstriped(offs)
    tab_ = unpack_weight(tab_words, tab_scales, "e4m3")[:, idx]
    wg_ = mxq(f64(wg), 0, "e4m3")
    wu_ = mxq(f64(wu), 0, "e4m3")
    ga = wg_.T @ tab_
    ub = wu_.T @ tab_
    h = silu(ga) * ub
    h_ = mxq(h, 0, "e4m3")
    wd8_ = unpack_weight(wd8_words, wd8_scales, "e4m3")
    wd4_ = unpack_weight(wd4_words, wd4_scales, "e2m1")
    y = wd8_.T @ h_[:512] + wd4_.T @ h_[512:]
    out_0 = y * f64(gT)[:, idx]
    return (out_0,) + planes(out_0)

@@ -1,0 +1,261 @@
+from contextlib import ExitStack
+
+import concourse.mybir as mybir
+
+K, R, N, T, J = 512, 1024, 512, 2048, 1024
+FLOPS = 2 * K * R * J * 2 + 2 * R * N * J
+
+F32 = mybir.dt.float32
+BF16 = mybir.dt.bfloat16
+I32 = mybir.dt.int32
+U32 = mybir.dt.uint32
+U16 = mybir.dt.uint16
+U8 = mybir.dt.uint8
+FP8X4 = mybir.dt.float8_e4m3fn_x4
+FP4X4 = mybir.dt.float4_e2m1fn_x4
+MULT = mybir.AluOpType.mult
+SILU = mybir.ActivationFunctionType.Silu
+
+P = 128
+PACK = 4
+GROUP = P * PACK
+CHUNK = 128
+CHUNKS = J // CHUNK
+STORE = 256
+
+
+def tile_list_gmlpt_silu_mix_gateP_kernel(
+    tc, tab_words, tab_scales, wg, wu, wd8_words, wd8_scales, wd4_words, wd4_scales, gT, offs, out_0, out_1, out_2
+):
+    nc = tc.nc
+    with ExitStack() as ctx:
+        held = ctx.enter_context(tc.tile_pool(name="held", bufs=1))
+        ring = ctx.enter_context(tc.tile_pool(name="ring", bufs=8))
+        psum = ctx.enter_context(tc.psum_pool(name="psum", bufs=1))
+
+        offsets = held.tile([P, J // 16], U16, name="offsets")
+        nc.sync.dma_start(offsets[:], offs)
+
+        tab_s = held.tile([P, T], U8, name="tab_s", align_bytes=64)
+        tab_rows = tab_scales[0].bitcast(I32)
+        for q in range(4):
+            nc.sync.dma_start(
+                tab_s[32 * q : 32 * q + 32, :].bitcast(I32),
+                tab_rows[4 * q : 4 * q + 4, :].unsqueeze(0).to_broadcast([8, 4, T // 4]),
+            )
+
+        wd_s = held.tile([P, N], U8, name="wd_s", align_bytes=64)
+        nc.vector.memset(wd_s[:].bitcast(I32), 0)
+
+        def load_scale_rows(scales, first):
+            for q in range(4):
+                nc.sync.dma_start(
+                    wd_s[32 * q + first : 32 * q + first + 4, :].bitcast(I32), scales[0].bitcast(I32)[4 * q : 4 * q + 4, :]
+                )
+
+        wd4_w = held.tile([P, 2 * N], U8, name="wd4_w", align_bytes=64)
+        nc.sync.dma_start(wd4_w[:].bitcast(I32), wd4_words[0].bitcast(I32))
+
+        def load_weight(w, b, name):
+            raw = held.tile([P, PACK, GROUP], F32, name=name)
+            nc.sync.dma_start(raw[:], w.rearrange("(p i) r -> p i r", i=PACK)[:, :, b * GROUP : (b + 1) * GROUP])
+            return raw
+
+        wg_raw, wu_raw = [None, None], [None, None]
+        wg_raw[0] = load_weight(wg, 0, "wg_raw0")
+        tab_w = held.tile([P, T], I32, name="tab_w", align_bytes=64)
+        nc.sync.dma_start(tab_w[:], tab_words[0].rearrange("p t i -> p (t i)").bitcast(I32))
+        wu_raw[0] = load_weight(wu, 0, "wu_raw0")
+        wg_raw[1] = load_weight(wg, 1, "wg_raw1")
+        load_scale_rows(wd4_scales, 0)
+        wu_raw[1] = load_weight(wu, 1, "wu_raw1")
+        wd8_w = held.tile([P, N], I32, name="wd8_w", align_bytes=64)
+        nc.sync.dma_start(wd8_w[:], wd8_words[0].rearrange("p n i -> p (n i)").bitcast(I32))
+        gate_rows = []
+        for t in range(PACK):
+            rows = held.tile([P, T], F32, name=f"gate_rows{t}")
+            nc.sync.dma_start(rows[:], gT.rearrange("(p t) c -> p t c", t=PACK)[:, t, :])
+            gate_rows.append(rows)
+            if t == 0:
+                load_scale_rows(wd8_scales, 4)
+
+        warm = held.tile([P, 1], F32, name="warm")
+        nc.vector.memset(warm[:], 0.0)
+        warm_out = held.tile([P, 1], F32, name="warm_out")
+        nc.scalar.activation(warm_out[:], warm[:], SILU)
+
+        v_s = held.tile([P, J], U8, name="v_s", align_bytes=64)
+        nc.vector.tensor_copy(v_s[:], tab_s[:].indirect(offsets[:]))
+
+        wd4_d = held.tile([P, 2 * N], U8, name="wd4_d", align_bytes=64)
+        nc.vector.tensor_copy(
+            wd4_d[:].rearrange("p (t m e) -> p m t e", t=PACK, e=2),
+            wd4_w[:].rearrange("p (m t e) -> p m t e", t=PACK, e=2),
+        )
+
+        def quantize_weight(raw, name, copies):
+            codes = held.tile([P, GROUP], U32, name=name + "_c", align_bytes=64)
+            scales = held.tile([P, GROUP], U8, name=name + "_s", align_bytes=64)
+            n = len(copies)
+            ts = PACK // n
+            halves = []
+            for u, copy in enumerate(copies):
+                dealt = held.tile([P, ts * P * PACK], BF16, name=f"{name}_b{u}", align_bytes=64)
+                copy(
+                    dealt[:].rearrange("p (t m i) -> p m i t", t=ts, i=PACK),
+                    raw[:].rearrange("p i (m t) -> p m i t", t=PACK)[:, :, :, u * ts : (u + 1) * ts],
+                )
+                halves.append(dealt)
+            for u, dealt in enumerate(halves):
+                cols = slice(u * ts * P, (u + 1) * ts * P)
+                nc.vector.quantize_mx(out=codes[:, cols].bitcast(FP8X4), scales=scales[:, cols], in_=dealt[:])
+            return codes, scales
+
+        on_scalar, on_vector = nc.scalar.copy, nc.vector.tensor_copy
+        wg_q, wu_q = [None, None], [None, None]
+        wg_q[0] = quantize_weight(wg_raw[0], "wg0", [on_scalar, on_vector])
+
+        v_w = held.tile([P, J], U32, name="v_w", align_bytes=64)
+        for half in range(2):
+            nc.vector.tensor_copy(
+                v_w[:, half * 512 : (half + 1) * 512],
+                tab_w[:].bitcast(U32).indirect(offsets[:, half * 32 : (half + 1) * 32]),
+            )
+        wu_q[0] = quantize_weight(wu_raw[0], "wu0", [on_scalar, on_vector])
+
+        h_bf = [held.tile([P, J * PACK], BF16, name=f"h_bf{b}", align_bytes=64) for b in range(2)]
+        h_c = [held.tile([P, J], U32, name=f"h_c{b}", align_bytes=64) for b in range(2)]
+        h_s = [held.tile([P, J], U8, name=f"h_s{b}", align_bytes=64) for b in range(2)]
+
+        def up_product(wq, c, tag):
+            codes, scales = wq
+            acc = psum.tile([P, PACK, CHUNK], F32, name=tag, bufs=3 if tag == "ub" else 2)
+            cols = slice(c * CHUNK, (c + 1) * CHUNK)
+            for t in range(PACK):
+                ms = slice(t * P, (t + 1) * P)
+                nc.tensor.matmul_mx(
+                    out=acc[:, t, :],
+                    lhsT=codes[:, ms].bitcast(FP8X4),
+                    lhsT_scale=scales[:, ms],
+                    rhs=v_w[:, cols].bitcast(FP8X4),
+                    rhs_scale=v_s[:, cols],
+                    start=True,
+                    stop=True,
+                )
+            return acc
+
+        def hidden(b, c):
+            ga = up_product(wg_q[b], c, "ga")
+            act = ring.tile([P, CHUNK, PACK], F32, name="act")
+            nc.scalar.activation(act[:], ga[:].rearrange("p t j -> p j t"), SILU)
+            ub = up_product(wu_q[b], c, "ub")
+            nc.vector.tensor_tensor(
+                h_bf[b][:, c * GROUP : (c + 1) * GROUP].rearrange("p (j t) -> p j t", t=PACK),
+                ub[:].rearrange("p t j -> p j t"),
+                act[:],
+                MULT,
+            )
+
+        def quantize_hidden(b, c0, c1):
+            cols = slice(c0 * CHUNK, c1 * CHUNK)
+            nc.vector.quantize_mx(
+                out=h_c[b][:, cols].bitcast(FP8X4), scales=h_s[b][:, cols], in_=h_bf[b][:, c0 * GROUP : c1 * GROUP]
+            )
+
+        for c in range(CHUNKS):
+            hidden(0, c)
+            if c == 1:
+                wg_q[1] = quantize_weight(wg_raw[1], "wg1", [on_scalar])
+            if c == 4:
+                quantize_hidden(0, 0, 4)
+                wu_q[1] = quantize_weight(wu_raw[1], "wu1", [on_scalar])
+
+        wd8_d = held.tile([P, N], I32, name="wd8_d", align_bytes=64)
+        nc.vector.tensor_copy(
+            wd8_d[:].rearrange("p (t m) -> p m t", t=PACK), wd8_w[:].rearrange("p (m t) -> p m t", t=PACK)
+        )
+        wd_sd = held.tile([P, N], U8, name="wd_sd", align_bytes=64)
+        nc.vector.tensor_copy(
+            wd_sd[:].rearrange("p (t m) -> p m t", t=PACK), wd_s[:].rearrange("p (m t) -> p m t", t=PACK)
+        )
+        quantize_hidden(0, 4, 8)
+
+        gate = held.tile([P, PACK, J], F32, name="gate")
+
+        def gather_gate(t, half):
+            nc.vector.tensor_copy(
+                gate[:, t, half * 512 : (half + 1) * 512],
+                gate_rows[t][:].indirect(offsets[:, half * 32 : (half + 1) * 32]),
+            )
+
+        out_f = [held.tile([P, PACK, STORE], F32, name=f"out_f{s}") for s in range(J // STORE)]
+        out_bf = held.tile([P, J * PACK], BF16, name="out_bf", align_bytes=64)
+        out_c = held.tile([P, J], U32, name="out_c", align_bytes=64)
+        out_s = held.tile([P, J], U8, name="out_s", align_bytes=64)
+
+        def down_product(c):
+            cols = slice(c * CHUNK, (c + 1) * CHUNK)
+            y = psum.tile([P, PACK, CHUNK], F32, name="y", bufs=3)
+            for t in range(PACK):
+                ms = slice(t * P, (t + 1) * P)
+                nc.tensor.matmul_mx(
+                    out=y[:, t, :],
+                    lhsT=wd8_d[:, ms].bitcast(FP8X4),
+                    lhsT_scale=wd_sd[4:P, ms],
+                    rhs=h_c[0][:, cols].bitcast(FP8X4),
+                    rhs_scale=h_s[0][:, cols],
+                    start=True,
+                    stop=False,
+                )
+                nc.tensor.matmul_mx(
+                    out=y[:, t, :],
+                    lhsT=wd4_d[:, 2 * t * P : 2 * (t + 1) * P].bitcast(FP4X4),
+                    lhsT_scale=wd_sd[:, ms],
+                    rhs=h_c[1][:, cols].bitcast(FP8X4),
+                    rhs_scale=h_s[1][:, cols],
+                    start=False,
+                    stop=True,
+                )
+            return y
+
+        def gate_output(c, y):
+            s, part = divmod(c * CHUNK, STORE)
+            piece = out_f[s][:, :, part : part + CHUNK]
+            nc.vector.tensor_tensor(piece, y[:], gate[:, :, c * CHUNK : (c + 1) * CHUNK], MULT)
+            nc.scalar.copy(
+                out_bf[:, c * GROUP : (c + 1) * GROUP].rearrange("p (j t) -> p j t", t=PACK),
+                piece.rearrange("p t j -> p j t"),
+            )
+            if part + CHUNK == STORE:
+                nc.sync.dma_start(
+                    out_0.rearrange("(p t) j -> p t j", t=PACK)[:, :, s * STORE : (s + 1) * STORE], out_f[s][:]
+                )
+
+        def quantize_output(c0, c1):
+            cols = slice(c0 * CHUNK, c1 * CHUNK)
+            nc.vector.quantize_mx(
+                out=out_c[:, cols].bitcast(FP8X4), scales=out_s[:, cols], in_=out_bf[:, c0 * GROUP : c1 * GROUP]
+            )
+            nc.sync.dma_start(
+                out_1[0].rearrange("p j i -> p (j i)").bitcast(I32)[:, cols], out_c[:, cols].bitcast(I32)
+            )
+
+        for c in range(CHUNKS):
+            hidden(1, c)
+            if c < PACK:
+                gather_gate(c, 0)
+            if c > 0:
+                quantize_hidden(1, c - 1, c)
+        quantize_hidden(1, CHUNKS - 1, CHUNKS)
+        for c in range(CHUNKS):
+            gate_output(c, down_product(c))
+            if c < PACK:
+                gather_gate(c, 1)
+            if c in (2, 4, 6):
+                quantize_output(c - 2, c)
+            if c == 7:
+                quantize_output(6, 7)
+        quantize_output(7, 8)
+        for q in range(4):
+            queue = nc.scalar if q % 2 else nc.sync
+            queue.dma_start(out_2[0].bitcast(I32)[4 * q : 4 * q + 4, :], out_s[32 * q : 32 * q + 4, :].bitcast(I32))

@@ -21,7 +21,6 @@ PACK = 4
 GROUP = P * PACK
 CHUNK = 128
 CHUNKS = J // CHUNK
-STORE = 256
 
 
 def tile_list_gmlpt_silu_mix_gateP_kernel(
@@ -45,7 +44,7 @@ def tile_list_gmlpt_silu_mix_gateP_kernel(
             )
 
         wd_s = held.tile([P, N], U8, name="wd_s", align_bytes=64)
-        nc.vector.memset(wd_s[:].bitcast(I32), 0)
+        nc.gpsimd.memset(wd_s[:].bitcast(I32), 0)
 
         def load_scale_rows(scales, first):
             for q in range(4):
@@ -56,16 +55,21 @@ def tile_list_gmlpt_silu_mix_gateP_kernel(
         wd4_w = held.tile([P, 2 * N], U8, name="wd4_w", align_bytes=64)
         nc.sync.dma_start(wd4_w[:].bitcast(I32), wd4_words[0].bitcast(I32))
 
-        def load_weight(w, b, name):
-            raw = held.tile([P, PACK, GROUP], F32, name=name)
-            nc.sync.dma_start(raw[:], w.rearrange("(p i) r -> p i r", i=PACK)[:, :, b * GROUP : (b + 1) * GROUP])
-            return raw
+        def load_weight(w, b, name, pieces=1):
+            width = GROUP // pieces
+            raws = []
+            for k in range(pieces):
+                raw = held.tile([P, PACK, width], F32, name=f"{name}_{k}")
+                first = b * GROUP + k * width
+                nc.sync.dma_start(raw[:], w.rearrange("(p i) r -> p i r", i=PACK)[:, :, first : first + width])
+                raws.append(raw)
+            return raws
 
         wg_raw, wu_raw = [None, None], [None, None]
         wg_raw[0] = load_weight(wg, 0, "wg_raw0")
         tab_w = held.tile([P, T], I32, name="tab_w", align_bytes=64)
         nc.sync.dma_start(tab_w[:], tab_words[0].rearrange("p t i -> p (t i)").bitcast(I32))
-        wu_raw[0] = load_weight(wu, 0, "wu_raw0")
+        wu_raw[0] = load_weight(wu, 0, "wu_raw0", pieces=2)
         wg_raw[1] = load_weight(wg, 1, "wg_raw1")
         load_scale_rows(wd4_scales, 0)
         wu_raw[1] = load_weight(wu, 1, "wu_raw1")
@@ -93,7 +97,7 @@ def tile_list_gmlpt_silu_mix_gateP_kernel(
             wd4_w[:].rearrange("p (m t e) -> p m t e", t=PACK, e=2),
         )
 
-        def quantize_weight(raw, name, copies):
+        def quantize_weight(raws, name, copies):
             codes = held.tile([P, GROUP], U32, name=name + "_c", align_bytes=64)
             scales = held.tile([P, GROUP], U8, name=name + "_s", align_bytes=64)
             n = len(copies)
@@ -101,10 +105,12 @@ def tile_list_gmlpt_silu_mix_gateP_kernel(
             halves = []
             for u, copy in enumerate(copies):
                 dealt = held.tile([P, ts * P * PACK], BF16, name=f"{name}_b{u}", align_bytes=64)
-                copy(
-                    dealt[:].rearrange("p (t m i) -> p m i t", t=ts, i=PACK),
-                    raw[:].rearrange("p i (m t) -> p m i t", t=PACK)[:, :, :, u * ts : (u + 1) * ts],
-                )
+                ms = P // len(raws)
+                for k, raw in enumerate(raws):
+                    copy(
+                        dealt[:].rearrange("p (t m i) -> p m i t", t=ts, i=PACK)[:, k * ms : (k + 1) * ms],
+                        raw[:].rearrange("p i (m t) -> p m i t", t=PACK)[:, :, :, u * ts : (u + 1) * ts],
+                    )
                 halves.append(dealt)
             for u, dealt in enumerate(halves):
                 cols = slice(u * ts * P, (u + 1) * ts * P)
@@ -164,11 +170,9 @@ def tile_list_gmlpt_silu_mix_gateP_kernel(
 
         for c in range(CHUNKS):
             hidden(0, c)
-            if c == 1:
-                wg_q[1] = quantize_weight(wg_raw[1], "wg1", [on_scalar])
-            if c == 4:
-                quantize_hidden(0, 0, 4)
-                wu_q[1] = quantize_weight(wu_raw[1], "wu1", [on_scalar])
+        wg_q[1] = quantize_weight(wg_raw[1], "wg1", [on_scalar])
+        wu_q[1] = quantize_weight(wu_raw[1], "wu1", [on_scalar, on_vector])
+        quantize_hidden(0, 0, 4)
 
         wd8_d = held.tile([P, N], I32, name="wd8_d", align_bytes=64)
         nc.vector.tensor_copy(
@@ -180,15 +184,9 @@ def tile_list_gmlpt_silu_mix_gateP_kernel(
         )
         quantize_hidden(0, 4, 8)
 
-        gate = held.tile([P, PACK, J], F32, name="gate")
-
-        def gather_gate(t, half):
-            nc.vector.tensor_copy(
-                gate[:, t, half * 512 : (half + 1) * 512],
-                gate_rows[t][:].indirect(offsets[:, half * 32 : (half + 1) * 32]),
-            )
-
-        out_f = [held.tile([P, PACK, STORE], F32, name=f"out_f{s}") for s in range(J // STORE)]
+        spans = [(0, 2), (2, 4), (4, 6), (6, 7), (7, 8)]
+        y_f = {}
+        out_f = [held.tile([P, PACK, (c1 - c0) * CHUNK], F32, name=f"out_f{c0}") for c0, c1 in spans]
         out_bf = held.tile([P, J * PACK], BF16, name="out_bf", align_bytes=64)
         out_c = held.tile([P, J], U32, name="out_c", align_bytes=64)
         out_s = held.tile([P, J], U8, name="out_s", align_bytes=64)
@@ -218,18 +216,23 @@ def tile_list_gmlpt_silu_mix_gateP_kernel(
                 )
             return y
 
-        def gate_output(c, y):
-            s, part = divmod(c * CHUNK, STORE)
-            piece = out_f[s][:, :, part : part + CHUNK]
-            nc.vector.tensor_tensor(piece, y[:], gate[:, :, c * CHUNK : (c + 1) * CHUNK], MULT)
-            nc.scalar.copy(
-                out_bf[:, c * GROUP : (c + 1) * GROUP].rearrange("p (j t) -> p j t", t=PACK),
-                piece.rearrange("p t j -> p j t"),
-            )
-            if part + CHUNK == STORE:
-                nc.sync.dma_start(
-                    out_0.rearrange("(p t) j -> p t j", t=PACK)[:, :, s * STORE : (s + 1) * STORE], out_f[s][:]
+        def gate_output(s):
+            c0, c1 = spans[s]
+            for t in range(PACK):
+                nc.vector.tensor_tensor(
+                    out_f[s][:, t, :],
+                    gate_rows[t][:].indirect(offsets[:, c0 * CHUNK // 16 : c1 * CHUNK // 16]),
+                    y_f[s][:, t, :],
+                    MULT,
                 )
+            nc.sync.dma_start(out_0.rearrange("(p t) j -> p t j", t=PACK)[:, :, c0 * CHUNK : c1 * CHUNK], out_f[s][:])
+
+        def round_output(s):
+            c0, c1 = spans[s]
+            nc.scalar.copy(
+                out_bf[:, c0 * GROUP : c1 * GROUP].rearrange("p (j t) -> p j t", t=PACK),
+                out_f[s][:].rearrange("p t j -> p j t"),
+            )
 
         def quantize_output(c0, c1):
             cols = slice(c0 * CHUNK, c1 * CHUNK)
@@ -240,22 +243,28 @@ def tile_list_gmlpt_silu_mix_gateP_kernel(
                 out_1[0].rearrange("p j i -> p (j i)").bitcast(I32)[:, cols], out_c[:, cols].bitcast(I32)
             )
 
+        def down_span(s):
+            c0, c1 = spans[s]
+            y_f[s] = ring.tile([P, PACK, (c1 - c0) * CHUNK], F32, name="y_f", bufs=2)
+            for c in range(c0, c1):
+                part = (c - c0) * CHUNK
+                nc.scalar.copy(y_f[s][:, :, part : part + CHUNK], down_product(c)[:])
+
         for c in range(CHUNKS):
             hidden(1, c)
-            if c < PACK:
-                gather_gate(c, 0)
-            if c > 0:
-                quantize_hidden(1, c - 1, c)
-        quantize_hidden(1, CHUNKS - 1, CHUNKS)
-        for c in range(CHUNKS):
-            gate_output(c, down_product(c))
-            if c < PACK:
-                gather_gate(c, 1)
             if c in (2, 4, 6):
-                quantize_output(c - 2, c)
-            if c == 7:
-                quantize_output(6, 7)
-        quantize_output(7, 8)
+                quantize_hidden(1, c - 2, c)
+        quantize_hidden(1, 6, 8)
+        down_span(0)
+        down_span(1)
+        for s in range(len(spans)):
+            gate_output(s)
+            if s + 2 < len(spans):
+                down_span(s + 2)
+            round_output(s)
+            if s > 0:
+                quantize_output(*spans[s - 1])
+        quantize_output(*spans[-1])
         for q in range(4):
             queue = nc.scalar if q % 2 else nc.sync
             queue.dma_start(out_2[0].bitcast(I32)[4 * q : 4 * q + 4, :], out_s[32 * q : 32 * q + 4, :].bitcast(I32))

@@ -14,6 +14,7 @@ U8 = mybir.dt.uint8
 FP8X4 = mybir.dt.float8_e4m3fn_x4
 FP4X4 = mybir.dt.float4_e2m1fn_x4
 MULT = mybir.AluOpType.mult
+ADD = mybir.AluOpType.add
 SILU = mybir.ActivationFunctionType.Silu
 
 P = 128
@@ -93,23 +94,23 @@ def tile_list_gmlpt_silu_mix_gateP_kernel(
 
         wd4_d = held.tile([P, 2 * N], U8, name="wd4_d", align_bytes=64)
         nc.vector.tensor_copy(
-            wd4_d[:].rearrange("p (t m e) -> p m t e", t=PACK, e=2),
-            wd4_w[:].rearrange("p (m t e) -> p m t e", t=PACK, e=2),
+            wd4_d[:].bitcast(U16).rearrange("p (t a m) -> p a t m", t=PACK, m=8),
+            wd4_w[:].bitcast(U16).rearrange("p (a m t) -> p a t m", t=PACK, m=8),
         )
 
-        def quantize_weight(raws, name, copies):
+        def quantize_weight(raws, name, copies, tag=""):
             codes = held.tile([P, GROUP], U32, name=name + "_c", align_bytes=64)
             scales = held.tile([P, GROUP], U8, name=name + "_s", align_bytes=64)
             n = len(copies)
             ts = PACK // n
             halves = []
             for u, copy in enumerate(copies):
-                dealt = held.tile([P, ts * P * PACK], BF16, name=f"{name}_b{u}", align_bytes=64)
+                dealt = held.tile([P, ts * P * PACK], BF16, name=f"{name}_b{u}", tag=tag or f"{name}_b{u}", align_bytes=64)
                 ms = P // len(raws)
                 for k, raw in enumerate(raws):
                     copy(
-                        dealt[:].rearrange("p (t m i) -> p m i t", t=ts, i=PACK)[:, k * ms : (k + 1) * ms],
-                        raw[:].rearrange("p i (m t) -> p m i t", t=PACK)[:, :, :, u * ts : (u + 1) * ts],
+                        dealt[:].rearrange("p (t m i) -> p m t i", t=ts, i=PACK)[:, k * ms : (k + 1) * ms],
+                        raw[:].rearrange("p i (m t) -> p m t i", t=PACK)[:, :, u * ts : (u + 1) * ts, :],
                     )
                 halves.append(dealt)
             for u, dealt in enumerate(halves):
@@ -118,6 +119,10 @@ def tile_list_gmlpt_silu_mix_gateP_kernel(
             return codes, scales
 
         on_scalar, on_vector = nc.scalar.copy, nc.vector.tensor_copy
+
+        def on_gpsimd(out, in_):
+            nc.gpsimd.tensor_scalar(out, in_, 1.0, 0.0, MULT, ADD)
+
         wg_q, wu_q = [None, None], [None, None]
         wg_q[0] = quantize_weight(wg_raw[0], "wg0", [on_scalar, on_vector])
 
@@ -127,7 +132,7 @@ def tile_list_gmlpt_silu_mix_gateP_kernel(
                 v_w[:, half * 512 : (half + 1) * 512],
                 tab_w[:].bitcast(U32).indirect(offsets[:, half * 32 : (half + 1) * 32]),
             )
-        wu_q[0] = quantize_weight(wu_raw[0], "wu0", [on_scalar, on_vector])
+        wu_q[0] = quantize_weight(wu_raw[0], "wu0", [on_vector], tag="shared_bf")
 
         h_bf = [held.tile([P, J * PACK], BF16, name=f"h_bf{b}", align_bytes=64) for b in range(2)]
         h_c = [held.tile([P, J], U32, name=f"h_c{b}", align_bytes=64) for b in range(2)]
@@ -152,7 +157,7 @@ def tile_list_gmlpt_silu_mix_gateP_kernel(
 
         def hidden(b, c):
             ga = up_product(wg_q[b], c, "ga")
-            act = ring.tile([P, CHUNK, PACK], F32, name="act")
+            act = ring.tile([P, CHUNK, PACK], F32, name="act", bufs=3)
             nc.scalar.activation(act[:], ga[:].rearrange("p t j -> p j t"), SILU)
             ub = up_product(wu_q[b], c, "ub")
             nc.vector.tensor_tensor(
@@ -170,19 +175,21 @@ def tile_list_gmlpt_silu_mix_gateP_kernel(
 
         for c in range(CHUNKS):
             hidden(0, c)
-        wg_q[1] = quantize_weight(wg_raw[1], "wg1", [on_scalar])
-        wu_q[1] = quantize_weight(wu_raw[1], "wu1", [on_scalar, on_vector])
+        wg_q[1] = quantize_weight(wg_raw[1], "wg1", [on_gpsimd], tag="shared_bf")
+        wu_q[1] = quantize_weight(wu_raw[1], "wu1", [on_scalar, on_scalar])
         quantize_hidden(0, 0, 4)
+        quantize_hidden(0, 4, 8)
 
         wd8_d = held.tile([P, N], I32, name="wd8_d", align_bytes=64)
         nc.vector.tensor_copy(
-            wd8_d[:].rearrange("p (t m) -> p m t", t=PACK), wd8_w[:].rearrange("p (m t) -> p m t", t=PACK)
+            wd8_d[:].rearrange("p (t a m) -> p a t m", t=PACK, m=4),
+            wd8_w[:].rearrange("p (a m t) -> p a t m", t=PACK, m=4),
         )
         wd_sd = held.tile([P, N], U8, name="wd_sd", align_bytes=64)
         nc.vector.tensor_copy(
-            wd_sd[:].rearrange("p (t m) -> p m t", t=PACK), wd_s[:].rearrange("p (m t) -> p m t", t=PACK)
+            wd_sd[:].rearrange("p (t a m) -> p a t m", t=PACK, m=16),
+            wd_s[:].rearrange("p (a m t) -> p a t m", t=PACK, m=16),
         )
-        quantize_hidden(0, 4, 8)
 
         spans = [(0, 2), (2, 4), (4, 6), (6, 7), (7, 8)]
         y_f = {}
@@ -230,8 +237,8 @@ def tile_list_gmlpt_silu_mix_gateP_kernel(
         def round_output(s):
             c0, c1 = spans[s]
             nc.scalar.copy(
-                out_bf[:, c0 * GROUP : c1 * GROUP].rearrange("p (j t) -> p j t", t=PACK),
-                out_f[s][:].rearrange("p t j -> p j t"),
+                out_bf[:, c0 * GROUP : c1 * GROUP].rearrange("p (a j t) -> p a t j", t=PACK, j=4),
+                out_f[s][:].rearrange("p t (a j) -> p a t j", j=4),
             )
 
         def quantize_output(c0, c1):

@@ -22,6 +22,7 @@ PACK = 4
 GROUP = P * PACK
 CHUNK = 128
 CHUNKS = J // CHUNK
+ACT_SLOTS = 3
 
 
 def tile_list_gmlpt_silu_mix_gateP_kernel(
@@ -30,7 +31,7 @@ def tile_list_gmlpt_silu_mix_gateP_kernel(
     nc = tc.nc
     with ExitStack() as ctx:
         held = ctx.enter_context(tc.tile_pool(name="held", bufs=1))
-        ring = ctx.enter_context(tc.tile_pool(name="ring", bufs=8))
+        ring = ctx.enter_context(tc.tile_pool(name="ring", bufs=3))
         psum = ctx.enter_context(tc.psum_pool(name="psum", bufs=1))
 
         offsets = held.tile([P, J // 16], U16, name="offsets")
@@ -53,27 +54,26 @@ def tile_list_gmlpt_silu_mix_gateP_kernel(
                     wd_s[32 * q + first : 32 * q + first + 4, :].bitcast(I32), scales[0].bitcast(I32)[4 * q : 4 * q + 4, :]
                 )
 
-        wd4_w = held.tile([P, 2 * N], U8, name="wd4_w", align_bytes=64)
-        nc.sync.dma_start(wd4_w[:].bitcast(I32), wd4_words[0].bitcast(I32))
-
         def load_weight(w, b, name, pieces=1):
             width = GROUP // pieces
             raws = []
             for k in range(pieces):
-                raw = held.tile([P, PACK, width], F32, name=f"{name}_{k}")
+                raw = held.tile([P, PACK, width], F32, name=f"{name}_{k}", tag=f"{name}_{k}")
                 first = b * GROUP + k * width
                 nc.sync.dma_start(raw[:], w.rearrange("(p i) r -> p i r", i=PACK)[:, :, first : first + width])
                 raws.append(raw)
             return raws
 
         wg_raw, wu_raw = [None, None], [None, None]
-        wg_raw[0] = load_weight(wg, 0, "wg_raw0")
         tab_w = held.tile([P, T], I32, name="tab_w", align_bytes=64)
         nc.sync.dma_start(tab_w[:], tab_words[0].rearrange("p t i -> p (t i)").bitcast(I32))
+        wg_raw[0] = load_weight(wg, 0, "wg_raw0")
         wu_raw[0] = load_weight(wu, 0, "wu_raw0", pieces=2)
         wg_raw[1] = load_weight(wg, 1, "wg_raw1")
-        load_scale_rows(wd4_scales, 0)
         wu_raw[1] = load_weight(wu, 1, "wu_raw1")
+        load_scale_rows(wd4_scales, 0)
+        wd4_w = held.tile([P, 2 * N], U8, name="wd4_w", align_bytes=64)
+        nc.sync.dma_start(wd4_w[:].bitcast(I32), wd4_words[0].bitcast(I32))
         wd8_w = held.tile([P, N], I32, name="wd8_w", align_bytes=64)
         nc.sync.dma_start(wd8_w[:], wd8_words[0].rearrange("p n i -> p (n i)").bitcast(I32))
         gate_rows = []
@@ -92,23 +92,17 @@ def tile_list_gmlpt_silu_mix_gateP_kernel(
         v_s = held.tile([P, J], U8, name="v_s", align_bytes=64)
         nc.vector.tensor_copy(v_s[:], tab_s[:].indirect(offsets[:]))
 
-        wd4_d = held.tile([P, 2 * N], U8, name="wd4_d", align_bytes=64)
-        nc.vector.tensor_copy(
-            wd4_d[:].bitcast(U16).rearrange("p (t a m) -> p a t m", t=PACK, m=8),
-            wd4_w[:].bitcast(U16).rearrange("p (a m t) -> p a t m", t=PACK, m=8),
-        )
-
-        def quantize_weight(raws, name, copies, tag=""):
+        def quantize_weight(raws, name, copies, tags=None):
             codes = held.tile([P, GROUP], U32, name=name + "_c", align_bytes=64)
             scales = held.tile([P, GROUP], U8, name=name + "_s", align_bytes=64)
             n = len(copies)
             ts = PACK // n
             halves = []
             for u, copy in enumerate(copies):
-                dealt = held.tile([P, ts * P * PACK], BF16, name=f"{name}_b{u}", tag=tag or f"{name}_b{u}", align_bytes=64)
+                dealt = held.tile([P, ts * P * PACK], BF16, name=f"{name}_b{u}", tag=tags[u] if tags else f"{name}_b{u}", align_bytes=64)
                 ms = P // len(raws)
                 for k, raw in enumerate(raws):
-                    copy(
+                    (copy[k] if isinstance(copy, list) else copy)(
                         dealt[:].rearrange("p (t m i) -> p m t i", t=ts, i=PACK)[:, k * ms : (k + 1) * ms],
                         raw[:].rearrange("p i (m t) -> p m t i", t=PACK)[:, :, u * ts : (u + 1) * ts, :],
                     )
@@ -124,15 +118,15 @@ def tile_list_gmlpt_silu_mix_gateP_kernel(
             nc.gpsimd.tensor_scalar(out, in_, 1.0, 0.0, MULT, ADD)
 
         wg_q, wu_q = [None, None], [None, None]
-        wg_q[0] = quantize_weight(wg_raw[0], "wg0", [on_scalar, on_vector])
-
         v_w = held.tile([P, J], U32, name="v_w", align_bytes=64)
         for half in range(2):
             nc.vector.tensor_copy(
                 v_w[:, half * 512 : (half + 1) * 512],
                 tab_w[:].bitcast(U32).indirect(offsets[:, half * 32 : (half + 1) * 32]),
             )
-        wu_q[0] = quantize_weight(wu_raw[0], "wu0", [on_vector], tag="shared_bf")
+        wg_q[0] = quantize_weight(wg_raw[0], "wg0", [on_scalar, on_vector])
+
+        wu_q[0] = quantize_weight(wu_raw[0], "wu0", [[on_scalar, on_vector]], tags=["wu0_bf"])
 
         h_bf = [held.tile([P, J * PACK], BF16, name=f"h_bf{b}", align_bytes=64) for b in range(2)]
         h_c = [held.tile([P, J], U32, name=f"h_c{b}", align_bytes=64) for b in range(2)]
@@ -140,7 +134,7 @@ def tile_list_gmlpt_silu_mix_gateP_kernel(
 
         def up_product(wq, c, tag):
             codes, scales = wq
-            acc = psum.tile([P, PACK, CHUNK], F32, name=tag, bufs=3 if tag == "ub" else 2)
+            acc = psum.tile([P, PACK, CHUNK], F32, name=tag, bufs=3)
             cols = slice(c * CHUNK, (c + 1) * CHUNK)
             for t in range(PACK):
                 ms = slice(t * P, (t + 1) * P)
@@ -157,13 +151,16 @@ def tile_list_gmlpt_silu_mix_gateP_kernel(
 
         def hidden(b, c):
             ga = up_product(wg_q[b], c, "ga")
-            act = ring.tile([P, CHUNK, PACK], F32, name="act", bufs=3)
-            nc.scalar.activation(act[:], ga[:].rearrange("p t j -> p j t"), SILU)
+            if (b, c) == (0, 4):
+                act = held.tile([P, CHUNK, PACK], F32, name="act_apart", tag="wu1_b1", align_bytes=64)[:]
+            else:
+                act = acts[b][:, c % ACT_SLOTS]
+            nc.scalar.activation(act, ga[:].rearrange("p t j -> p j t"), SILU)
             ub = up_product(wu_q[b], c, "ub")
             nc.vector.tensor_tensor(
                 h_bf[b][:, c * GROUP : (c + 1) * GROUP].rearrange("p (j t) -> p j t", t=PACK),
                 ub[:].rearrange("p t j -> p j t"),
-                act[:],
+                act,
                 MULT,
             )
 
@@ -173,20 +170,29 @@ def tile_list_gmlpt_silu_mix_gateP_kernel(
                 out=h_c[b][:, cols].bitcast(FP8X4), scales=h_s[b][:, cols], in_=h_bf[b][:, c0 * GROUP : c1 * GROUP]
             )
 
+        acts = [held.tile([P, ACT_SLOTS, CHUNK, PACK], F32, name="act0", tag="wu0_bf", align_bytes=64)]
         for c in range(CHUNKS):
             hidden(0, c)
-        wg_q[1] = quantize_weight(wg_raw[1], "wg1", [on_gpsimd], tag="shared_bf")
-        wu_q[1] = quantize_weight(wu_raw[1], "wu1", [on_scalar, on_scalar])
+            if c == 4:
+                wg_q[1] = quantize_weight(wg_raw[1], "wg1", [on_gpsimd])
+        wu_q[1] = quantize_weight(wu_raw[1], "wu1", [on_gpsimd, on_scalar], tags=["wg1_b0", "wu1_b1"])
+        acts.append(held.tile([P, ACT_SLOTS, CHUNK, PACK], F32, name="act1", tag="wu1_b1", align_bytes=64))
         quantize_hidden(0, 0, 4)
         quantize_hidden(0, 4, 8)
 
-        wd8_d = held.tile([P, N], I32, name="wd8_d", align_bytes=64)
+        wd4_d = held.tile([P, 2 * N], U8, name="wd4_d", align_bytes=64)
         nc.vector.tensor_copy(
+            wd4_d[:].bitcast(U16).rearrange("p (t a m) -> p a t m", t=PACK, m=8),
+            wd4_w[:].bitcast(U16).rearrange("p (a m t) -> p a t m", t=PACK, m=8),
+        )
+
+        wd8_d = held.tile([P, N], I32, name="wd8_d", align_bytes=64)
+        nc.gpsimd.tensor_copy(
             wd8_d[:].rearrange("p (t a m) -> p a t m", t=PACK, m=4),
             wd8_w[:].rearrange("p (a m t) -> p a t m", t=PACK, m=4),
         )
         wd_sd = held.tile([P, N], U8, name="wd_sd", align_bytes=64)
-        nc.vector.tensor_copy(
+        nc.gpsimd.tensor_copy(
             wd_sd[:].rearrange("p (t a m) -> p a t m", t=PACK, m=16),
             wd_s[:].rearrange("p (a m t) -> p a t m", t=PACK, m=16),
         )
@@ -200,7 +206,7 @@ def tile_list_gmlpt_silu_mix_gateP_kernel(
 
         def down_product(c):
             cols = slice(c * CHUNK, (c + 1) * CHUNK)
-            y = psum.tile([P, PACK, CHUNK], F32, name="y", bufs=3)
+            y = psum.tile([P, PACK, CHUNK], F32, name="y", bufs=2)
             for t in range(PACK):
                 ms = slice(t * P, (t + 1) * P)
                 nc.tensor.matmul_mx(
@@ -252,7 +258,7 @@ def tile_list_gmlpt_silu_mix_gateP_kernel(
 
         def down_span(s):
             c0, c1 = spans[s]
-            y_f[s] = ring.tile([P, PACK, (c1 - c0) * CHUNK], F32, name="y_f", bufs=2)
+            y_f[s] = ring.tile([P, PACK, (c1 - c0) * CHUNK], F32, name="y_f", bufs=3)
             for c in range(c0, c1):
                 part = (c - c0) * CHUNK
                 nc.scalar.copy(y_f[s][:, :, part : part + CHUNK], down_product(c)[:])
@@ -264,10 +270,11 @@ def tile_list_gmlpt_silu_mix_gateP_kernel(
         quantize_hidden(1, 6, 8)
         down_span(0)
         down_span(1)
+        down_span(2)
         for s in range(len(spans)):
             gate_output(s)
-            if s + 2 < len(spans):
-                down_span(s + 2)
+            if s + 3 < len(spans):
+                down_span(s + 3)
             round_output(s)
             if s > 0:
                 quantize_output(*spans[s - 1])

@@ -23,6 +23,7 @@ GROUP = P * PACK
 CHUNK = 128
 CHUNKS = J // CHUNK
 ACT_SLOTS = 3
+HALF = J // 2
 
 
 def tile_list_gmlpt_silu_mix_gateP_kernel(
@@ -31,7 +32,7 @@ def tile_list_gmlpt_silu_mix_gateP_kernel(
     nc = tc.nc
     with ExitStack() as ctx:
         held = ctx.enter_context(tc.tile_pool(name="held", bufs=1))
-        ring = ctx.enter_context(tc.tile_pool(name="ring", bufs=3))
+        reused = ctx.enter_context(tc.tile_pool(name="reused", bufs=1))
         psum = ctx.enter_context(tc.psum_pool(name="psum", bufs=1))
 
         offsets = held.tile([P, J // 16], U16, name="offsets")
@@ -197,88 +198,87 @@ def tile_list_gmlpt_silu_mix_gateP_kernel(
             wd_s[:].rearrange("p (a m t) -> p a t m", t=PACK, m=16),
         )
 
-        spans = [(0, 2), (2, 4), (4, 6), (6, 7), (7, 8)]
-        y_f = {}
-        out_f = [held.tile([P, PACK, (c1 - c0) * CHUNK], F32, name=f"out_f{c0}") for c0, c1 in spans]
+        spans = [(0, 512), (512, 768), (768, 896), (896, 1024)]
+        y_f = [reused.tile([P, PACK, HALF], F32, name="y_f0", offset=0), held.tile([P, PACK, HALF], F32, name="y_f1")]
+        out_f = [held.tile([P, PACK, HALF], F32, name="out_f0")[:]]
         out_bf = held.tile([P, J * PACK], BF16, name="out_bf", align_bytes=64)
         out_c = held.tile([P, J], U32, name="out_c", align_bytes=64)
         out_s = held.tile([P, J], U8, name="out_s", align_bytes=64)
 
-        def down_product(c):
-            cols = slice(c * CHUNK, (c + 1) * CHUNK)
-            y = psum.tile([P, PACK, CHUNK], F32, name="y", bufs=2)
-            for t in range(PACK):
-                ms = slice(t * P, (t + 1) * P)
-                nc.tensor.matmul_mx(
-                    out=y[:, t, :],
-                    lhsT=wd8_d[:, ms].bitcast(FP8X4),
-                    lhsT_scale=wd_sd[4:P, ms],
-                    rhs=h_c[0][:, cols].bitcast(FP8X4),
-                    rhs_scale=h_s[0][:, cols],
-                    start=True,
-                    stop=False,
-                )
-                nc.tensor.matmul_mx(
-                    out=y[:, t, :],
-                    lhsT=wd4_d[:, 2 * t * P : 2 * (t + 1) * P].bitcast(FP4X4),
-                    lhsT_scale=wd_sd[:, ms],
-                    rhs=h_c[1][:, cols].bitcast(FP8X4),
-                    rhs_scale=h_s[1][:, cols],
-                    start=False,
-                    stop=True,
-                )
-            return y
+        def down_product(half, t):
+            cols = slice(half * HALF, (half + 1) * HALF)
+            ms = slice(t * P, (t + 1) * P)
+            y = psum.tile([P, HALF], F32, name="y", bufs=2)
+            nc.tensor.matmul_mx(
+                out=y[:],
+                lhsT=wd8_d[:, ms].bitcast(FP8X4),
+                lhsT_scale=wd_sd[4:P, ms],
+                rhs=h_c[0][:, cols].bitcast(FP8X4),
+                rhs_scale=h_s[0][:, cols],
+                start=True,
+                stop=False,
+            )
+            nc.tensor.matmul_mx(
+                out=y[:],
+                lhsT=wd4_d[:, 2 * t * P : 2 * (t + 1) * P].bitcast(FP4X4),
+                lhsT_scale=wd_sd[:, ms],
+                rhs=h_c[1][:, cols].bitcast(FP8X4),
+                rhs_scale=h_s[1][:, cols],
+                start=False,
+                stop=True,
+            )
+            nc.scalar.copy(y_f[half][:, t, :], y[:])
 
-        def gate_output(s):
-            c0, c1 = spans[s]
-            for t in range(PACK):
-                nc.vector.tensor_tensor(
-                    out_f[s][:, t, :],
-                    gate_rows[t][:].indirect(offsets[:, c0 * CHUNK // 16 : c1 * CHUNK // 16]),
-                    y_f[s][:, t, :],
-                    MULT,
-                )
-            nc.sync.dma_start(out_0.rearrange("(p t) j -> p t j", t=PACK)[:, :, c0 * CHUNK : c1 * CHUNK], out_f[s][:])
+        def gate_plane(s, t):
+            j0, j1 = spans[s]
+            half = j0 // HALF
+            nc.vector.tensor_tensor(
+                out_f[s][:, t, :],
+                gate_rows[t][:].indirect(offsets[:, j0 // 16 : j1 // 16]),
+                y_f[half][:, t, j0 - half * HALF : j1 - half * HALF],
+                MULT,
+            )
 
-        def round_output(s):
-            c0, c1 = spans[s]
+        def finish_span(s):
+            j0, j1 = spans[s]
+            nc.sync.dma_start(out_0.rearrange("(p t) j -> p t j", t=PACK)[:, :, j0:j1], out_f[s])
             nc.scalar.copy(
-                out_bf[:, c0 * GROUP : c1 * GROUP].rearrange("p (a j t) -> p a t j", t=PACK, j=4),
-                out_f[s][:].rearrange("p t (a j) -> p a t j", j=4),
+                out_bf[:, j0 * PACK : j1 * PACK].rearrange("p (a j t) -> p a t j", t=PACK, j=4),
+                out_f[s].rearrange("p t (a j) -> p a t j", j=4),
             )
 
-        def quantize_output(c0, c1):
-            cols = slice(c0 * CHUNK, c1 * CHUNK)
+        def quantize_output(s):
+            j0, j1 = spans[s]
             nc.vector.quantize_mx(
-                out=out_c[:, cols].bitcast(FP8X4), scales=out_s[:, cols], in_=out_bf[:, c0 * GROUP : c1 * GROUP]
+                out=out_c[:, j0:j1].bitcast(FP8X4), scales=out_s[:, j0:j1], in_=out_bf[:, j0 * PACK : j1 * PACK]
             )
-            nc.sync.dma_start(
-                out_1[0].rearrange("p j i -> p (j i)").bitcast(I32)[:, cols], out_c[:, cols].bitcast(I32)
-            )
-
-        def down_span(s):
-            c0, c1 = spans[s]
-            y_f[s] = ring.tile([P, PACK, (c1 - c0) * CHUNK], F32, name="y_f", bufs=3)
-            for c in range(c0, c1):
-                part = (c - c0) * CHUNK
-                nc.scalar.copy(y_f[s][:, :, part : part + CHUNK], down_product(c)[:])
 
         for c in range(CHUNKS):
             hidden(1, c)
-            if c in (2, 4, 6):
-                quantize_hidden(1, c - 2, c)
-        quantize_hidden(1, 6, 8)
-        down_span(0)
-        down_span(1)
-        down_span(2)
-        for s in range(len(spans)):
-            gate_output(s)
-            if s + 3 < len(spans):
-                down_span(s + 3)
-            round_output(s)
-            if s > 0:
-                quantize_output(*spans[s - 1])
-        quantize_output(*spans[-1])
+            if c == 4:
+                quantize_hidden(1, 0, 4)
+                for t in range(PACK):
+                    down_product(0, t)
+        gate_plane(0, 0)
+        quantize_hidden(1, 4, 8)
+        for t in range(PACK):
+            down_product(1, t)
+        for t in range(1, PACK):
+            gate_plane(0, t)
+        finish_span(0)
+        for j0, j1 in spans[1:]:
+            late = reused.tile([P, PACK, j1 - j0], F32, name=f"out_f{j0}", offset=(j0 - HALF) * PACK * 4)
+            out_f.append(late[:])
+        for s in range(1, len(spans)):
+            for t in range(PACK):
+                gate_plane(s, t)
+            finish_span(s)
+            quantize_output(s - 1)
+        quantize_output(len(spans) - 1)
+        for j0, j1 in spans:
+            nc.sync.dma_start(
+                out_1[0].rearrange("p j i -> p (j i)").bitcast(I32)[:, j0:j1], out_c[:, j0:j1].bitcast(I32)
+            )
         for q in range(4):
             queue = nc.scalar if q % 2 else nc.sync
             queue.dma_start(out_2[0].bitcast(I32)[4 * q : 4 * q + 4, :], out_s[32 * q : 32 * q + 4, :].bitcast(I32))

@@ -22,7 +22,7 @@ PACK = 4
 GROUP = P * PACK
 CHUNK = 128
 CHUNKS = J // CHUNK
-ACT_SLOTS = 3
+ACT_SLOTS = 4
 HALF = J // 2
 
 
@@ -55,21 +55,16 @@ def tile_list_gmlpt_silu_mix_gateP_kernel(
                     wd_s[32 * q + first : 32 * q + first + 4, :].bitcast(I32), scales[0].bitcast(I32)[4 * q : 4 * q + 4, :]
                 )
 
-        def load_weight(w, b, name, pieces=1):
-            width = GROUP // pieces
-            raws = []
-            for k in range(pieces):
-                raw = held.tile([P, PACK, width], F32, name=f"{name}_{k}", tag=f"{name}_{k}")
-                first = b * GROUP + k * width
-                nc.sync.dma_start(raw[:], w.rearrange("(p i) r -> p i r", i=PACK)[:, :, first : first + width])
-                raws.append(raw)
-            return raws
+        def load_weight(w, b, name):
+            raw = held.tile([P, PACK, GROUP], F32, name=name, tag=name, align_bytes=64)
+            nc.sync.dma_start(raw[:], w.rearrange("(p i) r -> p i r", i=PACK)[:, :, b * GROUP : (b + 1) * GROUP])
+            return raw
 
         wg_raw, wu_raw = [None, None], [None, None]
         tab_w = held.tile([P, T], I32, name="tab_w", align_bytes=64)
         nc.sync.dma_start(tab_w[:], tab_words[0].rearrange("p t i -> p (t i)").bitcast(I32))
         wg_raw[0] = load_weight(wg, 0, "wg_raw0")
-        wu_raw[0] = load_weight(wu, 0, "wu_raw0", pieces=2)
+        wu_raw[0] = load_weight(wu, 0, "wu_raw0")
         wg_raw[1] = load_weight(wg, 1, "wg_raw1")
         wu_raw[1] = load_weight(wu, 1, "wu_raw1")
         load_scale_rows(wd4_scales, 0)
@@ -93,24 +88,20 @@ def tile_list_gmlpt_silu_mix_gateP_kernel(
         v_s = held.tile([P, J], U8, name="v_s", align_bytes=64)
         nc.vector.tensor_copy(v_s[:], tab_s[:].indirect(offsets[:]))
 
-        def quantize_weight(raws, name, copies, tags=None):
+        def round_weight(copy, raw, u, parts, rounded):
+            ts = PACK // parts
+            copy(
+                rounded.rearrange("p (t m i) -> p m t i", t=ts, i=PACK),
+                raw[:].rearrange("p i (m t) -> p m t i", t=PACK)[:, :, u * ts : (u + 1) * ts, :],
+            )
+
+        def quantize_weight(name, parts):
             codes = held.tile([P, GROUP], U32, name=name + "_c", align_bytes=64)
             scales = held.tile([P, GROUP], U8, name=name + "_s", align_bytes=64)
-            n = len(copies)
-            ts = PACK // n
-            halves = []
-            for u, copy in enumerate(copies):
-                dealt = held.tile([P, ts * P * PACK], BF16, name=f"{name}_b{u}", tag=tags[u] if tags else f"{name}_b{u}", align_bytes=64)
-                ms = P // len(raws)
-                for k, raw in enumerate(raws):
-                    (copy[k] if isinstance(copy, list) else copy)(
-                        dealt[:].rearrange("p (t m i) -> p m t i", t=ts, i=PACK)[:, k * ms : (k + 1) * ms],
-                        raw[:].rearrange("p i (m t) -> p m t i", t=PACK)[:, :, u * ts : (u + 1) * ts, :],
-                    )
-                halves.append(dealt)
-            for u, dealt in enumerate(halves):
-                cols = slice(u * ts * P, (u + 1) * ts * P)
-                nc.vector.quantize_mx(out=codes[:, cols].bitcast(FP8X4), scales=scales[:, cols], in_=dealt[:])
+            width = GROUP // len(parts)
+            for u, rounded in enumerate(parts):
+                cols = slice(u * width, (u + 1) * width)
+                nc.vector.quantize_mx(out=codes[:, cols].bitcast(FP8X4), scales=scales[:, cols], in_=rounded)
             return codes, scales
 
         on_scalar, on_vector = nc.scalar.copy, nc.vector.tensor_copy
@@ -120,16 +111,17 @@ def tile_list_gmlpt_silu_mix_gateP_kernel(
 
         wg_q, wu_q = [None, None], [None, None]
         v_w = held.tile([P, J], U32, name="v_w", align_bytes=64)
-        for half in range(2):
-            nc.vector.tensor_copy(
-                v_w[:, half * 512 : (half + 1) * 512],
-                tab_w[:].bitcast(U32).indirect(offsets[:, half * 32 : (half + 1) * 32]),
-            )
-        wg_q[0] = quantize_weight(wg_raw[0], "wg0", [on_scalar, on_vector])
+        nc.vector.tensor_copy(v_w[:], tab_w[:].bitcast(U32).indirect(offsets[:]))
+        wg0_bf = held.tile([P, GROUP * PACK], BF16, name="wg0_bf", align_bytes=64)
+        round_weight(on_scalar, wg_raw[0], 0, 2, wg0_bf[:, : 2 * GROUP])
+        round_weight(on_vector, wg_raw[0], 1, 2, wg0_bf[:, 2 * GROUP :])
+        wg_q[0] = quantize_weight("wg0", [wg0_bf[:]])
+        wu0_bf = held.tile([P, GROUP * PACK], BF16, name="wu0_bf", tag="wu0_bf", align_bytes=64)
+        round_weight(on_vector, wu_raw[0], 0, 2, wu0_bf[:, : 2 * GROUP])
+        round_weight(on_scalar, wu_raw[0], 1, 2, wu0_bf[:, 2 * GROUP :])
+        wu_q[0] = quantize_weight("wu0", [wu0_bf[:, : 2 * GROUP], wu0_bf[:, 2 * GROUP :]])
 
-        wu_q[0] = quantize_weight(wu_raw[0], "wu0", [[on_scalar, on_vector]], tags=["wu0_bf"])
-
-        h_bf = [held.tile([P, J * PACK], BF16, name=f"h_bf{b}", align_bytes=64) for b in range(2)]
+        h_bf = [held.tile([P, J * PACK], BF16, name=f"h_bf{b}", tag=f"h_bf{b}", align_bytes=64) for b in range(2)]
         h_c = [held.tile([P, J], U32, name=f"h_c{b}", align_bytes=64) for b in range(2)]
         h_s = [held.tile([P, J], U8, name=f"h_s{b}", align_bytes=64) for b in range(2)]
 
@@ -153,9 +145,9 @@ def tile_list_gmlpt_silu_mix_gateP_kernel(
         def hidden(b, c):
             ga = up_product(wg_q[b], c, "ga")
             if (b, c) == (0, 4):
-                act = held.tile([P, CHUNK, PACK], F32, name="act_apart", tag="wu1_b1", align_bytes=64)[:]
+                act = held.tile([P, CHUNK, PACK], F32, name="act_apart", tag="wu1_late", align_bytes=64)[:]
             else:
-                act = acts[b][:, c % ACT_SLOTS]
+                act = acts[b][:, c % ACT_SLOTS if b == 0 else c]
             nc.scalar.activation(act, ga[:].rearrange("p t j -> p j t"), SILU)
             ub = up_product(wu_q[b], c, "ub")
             nc.vector.tensor_tensor(
@@ -175,9 +167,15 @@ def tile_list_gmlpt_silu_mix_gateP_kernel(
         for c in range(CHUNKS):
             hidden(0, c)
             if c == 4:
-                wg_q[1] = quantize_weight(wg_raw[1], "wg1", [on_gpsimd])
-        wu_q[1] = quantize_weight(wu_raw[1], "wu1", [on_gpsimd, on_scalar], tags=["wg1_b0", "wu1_b1"])
-        acts.append(held.tile([P, ACT_SLOTS, CHUNK, PACK], F32, name="act1", tag="wu1_b1", align_bytes=64))
+                wg1_bf = held.tile([P, GROUP * PACK], BF16, name="wg1_bf", tag="wg1_bf", align_bytes=64)
+                round_weight(on_gpsimd, wg_raw[1], 0, 1, wg1_bf[:])
+                wg_q[1] = quantize_weight("wg1", [wg1_bf[:]])
+        wu1_early = held.tile([P, 2 * GROUP], BF16, name="wu1_early", tag="wg1_bf", align_bytes=64)
+        round_weight(on_gpsimd, wu_raw[1], 0, 2, wu1_early[:])
+        wu1_late = held.tile([P, 2 * GROUP], BF16, name="wu1_late", tag="wu1_late", align_bytes=64)
+        round_weight(on_scalar, wu_raw[1], 1, 2, wu1_late[:])
+        wu_q[1] = quantize_weight("wu1", [wu1_early[:], wu1_late[:]])
+        acts.append(held.tile([P, CHUNKS, CHUNK, PACK], F32, name="act1", tag="wu_raw1", align_bytes=64))
         quantize_hidden(0, 0, 4)
         quantize_hidden(0, 4, 8)
 
@@ -187,18 +185,20 @@ def tile_list_gmlpt_silu_mix_gateP_kernel(
             wd4_w[:].bitcast(U16).rearrange("p (a m t) -> p a t m", t=PACK, m=8),
         )
 
-        wd8_d = held.tile([P, N], I32, name="wd8_d", align_bytes=64)
+        dealt_wd = held.tile([P, N + N // 4], I32, name="dealt_wd", tag="h_bf0", align_bytes=64)
+        wd8_d = dealt_wd[:, :N]
         nc.gpsimd.tensor_copy(
-            wd8_d[:].rearrange("p (t a m) -> p a t m", t=PACK, m=4),
+            wd8_d.rearrange("p (t a m) -> p a t m", t=PACK, m=4),
             wd8_w[:].rearrange("p (a m t) -> p a t m", t=PACK, m=4),
         )
-        wd_sd = held.tile([P, N], U8, name="wd_sd", align_bytes=64)
+        wd_sd = dealt_wd[:, N:].bitcast(U8)
         nc.gpsimd.tensor_copy(
-            wd_sd[:].rearrange("p (t a m) -> p a t m", t=PACK, m=16),
+            wd_sd.rearrange("p (t a m) -> p a t m", t=PACK, m=16),
             wd_s[:].rearrange("p (a m t) -> p a t m", t=PACK, m=16),
         )
 
-        spans = [(0, 512), (512, 768), (768, 896), (896, 1024)]
+        spans = [(0, 512), (512, 832), (832, 1024)]
+        coded = [(0, 512), (512, 768), (768, 1024)]
         y_f = [reused.tile([P, PACK, HALF], F32, name="y_f0", offset=0), held.tile([P, PACK, HALF], F32, name="y_f1")]
         out_f = [held.tile([P, PACK, HALF], F32, name="out_f0")[:]]
         out_bf = held.tile([P, J * PACK], BF16, name="out_bf", align_bytes=64)
@@ -247,8 +247,7 @@ def tile_list_gmlpt_silu_mix_gateP_kernel(
                 out_f[s].rearrange("p t (a j) -> p a t j", j=4),
             )
 
-        def quantize_output(s):
-            j0, j1 = spans[s]
+        def quantize_output(j0, j1):
             nc.vector.quantize_mx(
                 out=out_c[:, j0:j1].bitcast(FP8X4), scales=out_s[:, j0:j1], in_=out_bf[:, j0 * PACK : j1 * PACK]
             )
@@ -273,9 +272,8 @@ def tile_list_gmlpt_silu_mix_gateP_kernel(
             for t in range(PACK):
                 gate_plane(s, t)
             finish_span(s)
-            quantize_output(s - 1)
-        quantize_output(len(spans) - 1)
-        for j0, j1 in spans:
+        for j0, j1 in coded:
+            quantize_output(j0, j1)
             nc.sync.dma_start(
                 out_1[0].rearrange("p j i -> p (j i)").bitcast(I32)[:, j0:j1], out_c[:, j0:j1].bitcast(I32)
             )

@@ -38,13 +38,16 @@ def tile_list_gmlpt_silu_mix_gateP_kernel(
         offsets = held.tile([P, J // 16], U16, name="offsets")
         nc.sync.dma_start(offsets[:], offs)
 
+        wd4_w = held.tile([P, 2 * N], U8, name="wd4_w", align_bytes=64)
+        nc.sync.dma_start(wd4_w[:].bitcast(I32), wd4_words[0].bitcast(I32))
+        wd8_w = held.tile([P, N], I32, name="wd8_w", align_bytes=64)
+        nc.sync.dma_start(wd8_w[:], wd8_words[0].rearrange("p n i -> p (n i)").bitcast(I32))
+
         tab_s = held.tile([P, T], U8, name="tab_s", align_bytes=64)
+        nc.gpsimd.memset(tab_s[:].bitcast(I32), 0)
         tab_rows = tab_scales[0].bitcast(I32)
         for q in range(4):
-            nc.sync.dma_start(
-                tab_s[32 * q : 32 * q + 32, :].bitcast(I32),
-                tab_rows[4 * q : 4 * q + 4, :].unsqueeze(0).to_broadcast([8, 4, T // 4]),
-            )
+            nc.sync.dma_start(tab_s[32 * q : 32 * q + 4, :].bitcast(I32), tab_rows[4 * q : 4 * q + 4, :])
 
         wd_s = held.tile([P, N], U8, name="wd_s", align_bytes=64)
         nc.gpsimd.memset(wd_s[:].bitcast(I32), 0)
@@ -68,10 +71,6 @@ def tile_list_gmlpt_silu_mix_gateP_kernel(
         wg_raw[1] = load_weight(wg, 1, "wg_raw1")
         wu_raw[1] = load_weight(wu, 1, "wu_raw1")
         load_scale_rows(wd4_scales, 0)
-        wd4_w = held.tile([P, 2 * N], U8, name="wd4_w", align_bytes=64)
-        nc.sync.dma_start(wd4_w[:].bitcast(I32), wd4_words[0].bitcast(I32))
-        wd8_w = held.tile([P, N], I32, name="wd8_w", align_bytes=64)
-        nc.sync.dma_start(wd8_w[:], wd8_words[0].rearrange("p n i -> p (n i)").bitcast(I32))
         gate_rows = []
         for t in range(PACK):
             rows = held.tile([P, T], F32, name=f"gate_rows{t}")
@@ -84,6 +83,18 @@ def tile_list_gmlpt_silu_mix_gateP_kernel(
         nc.vector.memset(warm[:], 0.0)
         warm_out = held.tile([P, 1], F32, name="warm_out")
         nc.scalar.activation(warm_out[:], warm[:], SILU)
+
+        wd4_d = held.tile([P, 2 * N], U8, name="wd4_d", align_bytes=64)
+        nc.vector.tensor_copy(
+            wd4_d[:].bitcast(U16).rearrange("p (t a m) -> p a t m", t=PACK, m=8),
+            wd4_w[:].bitcast(U16).rearrange("p (a m t) -> p a t m", t=PACK, m=8),
+        )
+
+        wd8_d = held.tile([P, N], I32, name="wd8_d", align_bytes=64)
+        nc.vector.tensor_copy(
+            wd8_d[:].rearrange("p (t a m) -> p a t m", t=PACK, m=4),
+            wd8_w[:].rearrange("p (a m t) -> p a t m", t=PACK, m=4),
+        )
 
         v_s = held.tile([P, J], U8, name="v_s", align_bytes=64)
         nc.vector.tensor_copy(v_s[:], tab_s[:].indirect(offsets[:]))
@@ -116,7 +127,7 @@ def tile_list_gmlpt_silu_mix_gateP_kernel(
         round_weight(on_scalar, wg_raw[0], 0, 2, wg0_bf[:, : 2 * GROUP])
         round_weight(on_vector, wg_raw[0], 1, 2, wg0_bf[:, 2 * GROUP :])
         wg_q[0] = quantize_weight("wg0", [wg0_bf[:]])
-        wu0_bf = held.tile([P, GROUP * PACK], BF16, name="wu0_bf", tag="wu0_bf", align_bytes=64)
+        wu0_bf = held.tile([P, GROUP * PACK], BF16, name="wu0_bf", align_bytes=64)
         round_weight(on_vector, wu_raw[0], 0, 2, wu0_bf[:, : 2 * GROUP])
         round_weight(on_scalar, wu_raw[0], 1, 2, wu0_bf[:, 2 * GROUP :])
         wu_q[0] = quantize_weight("wu0", [wu0_bf[:, : 2 * GROUP], wu0_bf[:, 2 * GROUP :]])
@@ -163,7 +174,7 @@ def tile_list_gmlpt_silu_mix_gateP_kernel(
                 out=h_c[b][:, cols].bitcast(FP8X4), scales=h_s[b][:, cols], in_=h_bf[b][:, c0 * GROUP : c1 * GROUP]
             )
 
-        acts = [held.tile([P, ACT_SLOTS, CHUNK, PACK], F32, name="act0", tag="wu0_bf", align_bytes=64)]
+        acts = [held.tile([P, ACT_SLOTS, CHUNK, PACK], F32, name="act0", tag="wu_raw0", align_bytes=64)]
         for c in range(CHUNKS):
             hidden(0, c)
             if c == 4:
@@ -179,21 +190,9 @@ def tile_list_gmlpt_silu_mix_gateP_kernel(
         quantize_hidden(0, 0, 4)
         quantize_hidden(0, 4, 8)
 
-        wd4_d = held.tile([P, 2 * N], U8, name="wd4_d", align_bytes=64)
-        nc.vector.tensor_copy(
-            wd4_d[:].bitcast(U16).rearrange("p (t a m) -> p a t m", t=PACK, m=8),
-            wd4_w[:].bitcast(U16).rearrange("p (a m t) -> p a t m", t=PACK, m=8),
-        )
-
-        dealt_wd = held.tile([P, N + N // 4], I32, name="dealt_wd", tag="h_bf0", align_bytes=64)
-        wd8_d = dealt_wd[:, :N]
+        wd_sd = held.tile([P, N], U8, name="wd_sd", tag="h_bf0", align_bytes=64)
         nc.gpsimd.tensor_copy(
-            wd8_d.rearrange("p (t a m) -> p a t m", t=PACK, m=4),
-            wd8_w[:].rearrange("p (a m t) -> p a t m", t=PACK, m=4),
-        )
-        wd_sd = dealt_wd[:, N:].bitcast(U8)
-        nc.gpsimd.tensor_copy(
-            wd_sd.rearrange("p (t a m) -> p a t m", t=PACK, m=16),
+            wd_sd[:].rearrange("p (t a m) -> p a t m", t=PACK, m=16),
             wd_s[:].rearrange("p (a m t) -> p a t m", t=PACK, m=16),
         )
 

@@ -67,7 +67,13 @@ def tile_list_gmlpt_silu_mix_gateP_kernel(
         tab_w = held.tile([P, T], I32, name="tab_w", align_bytes=64)
         nc.sync.dma_start(tab_w[:], tab_words[0].rearrange("p t i -> p (t i)").bitcast(I32))
         wg_raw[0] = load_weight(wg, 0, "wg_raw0")
-        wu_raw[0] = load_weight(wu, 0, "wu_raw0")
+        wu0_parts = []
+        for k in range(2):
+            part = held.tile([P, PACK, GROUP // 2], F32, name=f"wu0_part{k}", tag=f"wu0_part{k}", align_bytes=64)
+            nc.sync.dma_start(
+                part[:], wu.rearrange("(p i) r -> p i r", i=PACK)[:, :, k * GROUP // 2 : (k + 1) * GROUP // 2]
+            )
+            wu0_parts.append(part)
         wg_raw[1] = load_weight(wg, 1, "wg_raw1")
         wu_raw[1] = load_weight(wu, 1, "wu_raw1")
         load_scale_rows(wd4_scales, 0)
@@ -124,12 +130,15 @@ def tile_list_gmlpt_silu_mix_gateP_kernel(
         v_w = held.tile([P, J], U32, name="v_w", align_bytes=64)
         nc.vector.tensor_copy(v_w[:], tab_w[:].bitcast(U32).indirect(offsets[:]))
         wg0_bf = held.tile([P, GROUP * PACK], BF16, name="wg0_bf", align_bytes=64)
-        round_weight(on_scalar, wg_raw[0], 0, 2, wg0_bf[:, : 2 * GROUP])
-        round_weight(on_vector, wg_raw[0], 1, 2, wg0_bf[:, 2 * GROUP :])
-        wg_q[0] = quantize_weight("wg0", [wg0_bf[:]])
+        round_weight(on_vector, wg_raw[0], 0, 2, wg0_bf[:, : 2 * GROUP])
+        round_weight(on_scalar, wg_raw[0], 1, 2, wg0_bf[:, 2 * GROUP :])
+        wg_q[0] = quantize_weight("wg0", [wg0_bf[:, : 2 * GROUP], wg0_bf[:, 2 * GROUP :]])
         wu0_bf = held.tile([P, GROUP * PACK], BF16, name="wu0_bf", align_bytes=64)
-        round_weight(on_vector, wu_raw[0], 0, 2, wu0_bf[:, : 2 * GROUP])
-        round_weight(on_scalar, wu_raw[0], 1, 2, wu0_bf[:, 2 * GROUP :])
+        wu0_dealt = wu0_bf[:].rearrange("p (t m i) -> p m t i", t=PACK, i=PACK)
+        wu0_read = [part[:].rearrange("p i (m t) -> p m t i", t=PACK) for part in wu0_parts]
+        on_scalar(wu0_dealt[:, : P // 2], wu0_read[0])
+        on_vector(wu0_dealt[:, P // 2 :, 0:2], wu0_read[1][:, :, 0:2])
+        on_scalar(wu0_dealt[:, P // 2 :, 2:4], wu0_read[1][:, :, 2:4])
         wu_q[0] = quantize_weight("wu0", [wu0_bf[:, : 2 * GROUP], wu0_bf[:, 2 * GROUP :]])
 
         h_bf = [held.tile([P, J * PACK], BF16, name=f"h_bf{b}", tag=f"h_bf{b}", align_bytes=64) for b in range(2)]
@@ -157,6 +166,8 @@ def tile_list_gmlpt_silu_mix_gateP_kernel(
             ga = up_product(wg_q[b], c, "ga")
             if (b, c) == (0, 4):
                 act = held.tile([P, CHUNK, PACK], F32, name="act_apart", tag="wu1_late", align_bytes=64)[:]
+            elif (b, c) == (0, 5):
+                act = held.tile([P, CHUNK, PACK], F32, name="act_fifth", tag="act1", align_bytes=64)[:]
             else:
                 act = acts[b][:, c % ACT_SLOTS if b == 0 else c]
             nc.scalar.activation(act, ga[:].rearrange("p t j -> p j t"), SILU)
@@ -174,7 +185,7 @@ def tile_list_gmlpt_silu_mix_gateP_kernel(
                 out=h_c[b][:, cols].bitcast(FP8X4), scales=h_s[b][:, cols], in_=h_bf[b][:, c0 * GROUP : c1 * GROUP]
             )
 
-        acts = [held.tile([P, ACT_SLOTS, CHUNK, PACK], F32, name="act0", tag="wu_raw0", align_bytes=64)]
+        acts = [held.tile([P, ACT_SLOTS, CHUNK, PACK], F32, name="act0", tag="wu0_part1", align_bytes=64)]
         for c in range(CHUNKS):
             hidden(0, c)
             if c == 4:
@@ -186,7 +197,7 @@ def tile_list_gmlpt_silu_mix_gateP_kernel(
         wu1_late = held.tile([P, 2 * GROUP], BF16, name="wu1_late", tag="wu1_late", align_bytes=64)
         round_weight(on_scalar, wu_raw[1], 1, 2, wu1_late[:])
         wu_q[1] = quantize_weight("wu1", [wu1_early[:], wu1_late[:]])
-        acts.append(held.tile([P, CHUNKS, CHUNK, PACK], F32, name="act1", tag="wu_raw1", align_bytes=64))
+        acts.append(held.tile([P, CHUNKS, CHUNK, PACK], F32, name="act1", tag="act1", align_bytes=64))
         quantize_hidden(0, 0, 4)
         quantize_hidden(0, 4, 8)
 

@@ -40,8 +40,9 @@ def tile_list_gmlpt_silu_mix_gateP_kernel(
 
         wd4_w = held.tile([P, 2 * N], U8, name="wd4_w", align_bytes=64)
         nc.sync.dma_start(wd4_w[:].bitcast(I32), wd4_words[0].bitcast(I32))
-        wd8_w = held.tile([P, N], I32, name="wd8_w", align_bytes=64)
-        nc.sync.dma_start(wd8_w[:], wd8_words[0].rearrange("p n i -> p (n i)").bitcast(I32))
+        tab_w = held.tile([P, T], I32, name="tab_w", align_bytes=64)
+        tab_cols = tab_words[0].rearrange("p t i -> p (t i)").bitcast(I32)
+        nc.sync.dma_start(tab_w[:, : T // 4], tab_cols[:, : T // 4])
 
         tab_s = held.tile([P, T], U8, name="tab_s", align_bytes=64)
         nc.gpsimd.memset(tab_s[:].bitcast(I32), 0)
@@ -64,19 +65,25 @@ def tile_list_gmlpt_silu_mix_gateP_kernel(
             return raw
 
         wg_raw, wu_raw = [None, None], [None, None]
-        tab_w = held.tile([P, T], I32, name="tab_w", align_bytes=64)
-        nc.sync.dma_start(tab_w[:], tab_words[0].rearrange("p t i -> p (t i)").bitcast(I32))
-        wg_raw[0] = load_weight(wg, 0, "wg_raw0")
-        wu0_parts = []
-        for k in range(2):
-            part = held.tile([P, PACK, GROUP // 2], F32, name=f"wu0_part{k}", tag=f"wu0_part{k}", align_bytes=64)
-            nc.sync.dma_start(
-                part[:], wu.rearrange("(p i) r -> p i r", i=PACK)[:, :, k * GROUP // 2 : (k + 1) * GROUP // 2]
-            )
-            wu0_parts.append(part)
+        nc.sync.dma_start(tab_w[:, T // 4 :], tab_cols[:, T // 4 :])
+
+        def load_halves(w, name):
+            parts = []
+            for k in range(2):
+                part = held.tile([P, PACK, GROUP // 2], F32, name=f"{name}{k}", tag=f"{name}{k}", align_bytes=64)
+                nc.sync.dma_start(
+                    part[:], w.rearrange("(p i) r -> p i r", i=PACK)[:, :, k * GROUP // 2 : (k + 1) * GROUP // 2]
+                )
+                parts.append(part)
+            return parts
+
+        wg0_parts = load_halves(wg, "wg0_part")
+        wu0_parts = load_halves(wu, "wu0_part")
         wg_raw[1] = load_weight(wg, 1, "wg_raw1")
         wu_raw[1] = load_weight(wu, 1, "wu_raw1")
         load_scale_rows(wd4_scales, 0)
+        wd8_w = held.tile([P, N], I32, name="wd8_w", align_bytes=64)
+        nc.sync.dma_start(wd8_w[:], wd8_words[0].rearrange("p n i -> p (n i)").bitcast(I32))
         gate_rows = []
         for t in range(PACK):
             rows = held.tile([P, T], F32, name=f"gate_rows{t}")
@@ -94,12 +101,6 @@ def tile_list_gmlpt_silu_mix_gateP_kernel(
         nc.vector.tensor_copy(
             wd4_d[:].bitcast(U16).rearrange("p (t a m) -> p a t m", t=PACK, m=8),
             wd4_w[:].bitcast(U16).rearrange("p (a m t) -> p a t m", t=PACK, m=8),
-        )
-
-        wd8_d = held.tile([P, N], I32, name="wd8_d", align_bytes=64)
-        nc.vector.tensor_copy(
-            wd8_d[:].rearrange("p (t a m) -> p a t m", t=PACK, m=4),
-            wd8_w[:].rearrange("p (a m t) -> p a t m", t=PACK, m=4),
         )
 
         v_s = held.tile([P, J], U8, name="v_s", align_bytes=64)
@@ -127,19 +128,28 @@ def tile_list_gmlpt_silu_mix_gateP_kernel(
             nc.gpsimd.tensor_scalar(out, in_, 1.0, 0.0, MULT, ADD)
 
         wg_q, wu_q = [None, None], [None, None]
-        v_w = held.tile([P, J], U32, name="v_w", align_bytes=64)
-        nc.vector.tensor_copy(v_w[:], tab_w[:].bitcast(U32).indirect(offsets[:]))
-        wg0_bf = held.tile([P, GROUP * PACK], BF16, name="wg0_bf", align_bytes=64)
-        round_weight(on_vector, wg_raw[0], 0, 2, wg0_bf[:, : 2 * GROUP])
-        round_weight(on_scalar, wg_raw[0], 1, 2, wg0_bf[:, 2 * GROUP :])
-        wg_q[0] = quantize_weight("wg0", [wg0_bf[:, : 2 * GROUP], wg0_bf[:, 2 * GROUP :]])
-        wu0_bf = held.tile([P, GROUP * PACK], BF16, name="wu0_bf", align_bytes=64)
-        wu0_dealt = wu0_bf[:].rearrange("p (t m i) -> p m t i", t=PACK, i=PACK)
-        wu0_read = [part[:].rearrange("p i (m t) -> p m t i", t=PACK) for part in wu0_parts]
-        on_scalar(wu0_dealt[:, : P // 2], wu0_read[0])
-        on_vector(wu0_dealt[:, P // 2 :, 0:2], wu0_read[1][:, :, 0:2])
-        on_scalar(wu0_dealt[:, P // 2 :, 2:4], wu0_read[1][:, :, 2:4])
-        wu_q[0] = quantize_weight("wu0", [wu0_bf[:, : 2 * GROUP], wu0_bf[:, 2 * GROUP :]])
+        v_w = []
+
+        def gather_words(half, tag):
+            words = held.tile([P, HALF], U32, name=f"v_w{half}", tag=tag, align_bytes=64)
+            picks = offsets[:, half * HALF // 16 : (half + 1) * HALF // 16]
+            nc.vector.tensor_copy(words[:], tab_w[:].bitcast(U32).indirect(picks))
+            v_w.append(words)
+
+        gather_words(0, "v_w0")
+
+        def quantize_halves(parts, name):
+            rounded = held.tile([P, GROUP * PACK], BF16, name=name + "_bf", tag=name + "_bf", align_bytes=64)
+            dealt = rounded[:].rearrange("p (t m i) -> p m t i", t=PACK, i=PACK)
+            read = [part[:].rearrange("p i (m t) -> p m t i", t=PACK) for part in parts]
+            on_scalar(dealt[:, : P // 2], read[0])
+            on_vector(dealt[:, P // 2 :, 0:2], read[1][:, :, 0:2])
+            on_scalar(dealt[:, P // 2 :, 2:4], read[1][:, :, 2:4])
+            return quantize_weight(name, [rounded[:, : 2 * GROUP], rounded[:, 2 * GROUP :]])
+
+        wg_q[0] = quantize_halves(wg0_parts, "wg0")
+        gather_words(1, "wg0_bf")
+        wu_q[0] = quantize_halves(wu0_parts, "wu0")
 
         h_bf = [held.tile([P, J * PACK], BF16, name=f"h_bf{b}", tag=f"h_bf{b}", align_bytes=64) for b in range(2)]
         h_c = [held.tile([P, J], U32, name=f"h_c{b}", align_bytes=64) for b in range(2)]
@@ -155,7 +165,7 @@ def tile_list_gmlpt_silu_mix_gateP_kernel(
                     out=acc[:, t, :],
                     lhsT=codes[:, ms].bitcast(FP8X4),
                     lhsT_scale=scales[:, ms],
-                    rhs=v_w[:, cols].bitcast(FP8X4),
+                    rhs=v_w[c * CHUNK // HALF][:, c * CHUNK % HALF : c * CHUNK % HALF + CHUNK].bitcast(FP8X4),
                     rhs_scale=v_s[:, cols],
                     start=True,
                     stop=True,
@@ -201,9 +211,15 @@ def tile_list_gmlpt_silu_mix_gateP_kernel(
         quantize_hidden(0, 0, 4)
         quantize_hidden(0, 4, 8)
 
-        wd_sd = held.tile([P, N], U8, name="wd_sd", tag="h_bf0", align_bytes=64)
+        dealt_wd = held.tile([P, N + N // 4], I32, name="dealt_wd", tag="h_bf0", align_bytes=64)
+        wd8_d = dealt_wd[:, :N]
         nc.gpsimd.tensor_copy(
-            wd_sd[:].rearrange("p (t a m) -> p a t m", t=PACK, m=16),
+            wd8_d.rearrange("p (t a m) -> p a t m", t=PACK, m=4),
+            wd8_w[:].rearrange("p (a m t) -> p a t m", t=PACK, m=4),
+        )
+        wd_sd = dealt_wd[:, N:].bitcast(U8)
+        nc.gpsimd.tensor_copy(
+            wd_sd.rearrange("p (t a m) -> p a t m", t=PACK, m=16),
             wd_s[:].rearrange("p (a m t) -> p a t m", t=PACK, m=16),
         )
 

@@ -38,11 +38,15 @@ def tile_list_gmlpt_silu_mix_gateP_kernel(
         offsets = held.tile([P, J // 16], U16, name="offsets")
         nc.sync.dma_start(offsets[:], offs)
 
-        wd4_w = held.tile([P, 2 * N], U8, name="wd4_w", align_bytes=64)
-        nc.sync.dma_start(wd4_w[:].bitcast(I32), wd4_words[0].bitcast(I32))
-        tab_w = held.tile([P, T], I32, name="tab_w", align_bytes=64)
-        tab_cols = tab_words[0].rearrange("p t i -> p (t i)").bitcast(I32)
-        nc.sync.dma_start(tab_w[:, : T // 4], tab_cols[:, : T // 4])
+        def load_half(w, k, name, pieces):
+            part = held.tile([P, PACK, GROUP // 2], F32, name=name, tag=name, align_bytes=64)
+            rows = w.rearrange("(p i) r -> p i r", i=PACK)[:, :, k * GROUP // 2 : (k + 1) * GROUP // 2]
+            for u in range(pieces):
+                planes = slice(u * PACK // pieces, (u + 1) * PACK // pieces)
+                nc.sync.dma_start(part[:, planes], rows[:, planes])
+            return part
+
+        wg0_parts = [load_half(wg, 0, "wg0_part0", 2)]
 
         tab_s = held.tile([P, T], U8, name="tab_s", align_bytes=64)
         nc.gpsimd.memset(tab_s[:].bitcast(I32), 0)
@@ -65,21 +69,13 @@ def tile_list_gmlpt_silu_mix_gateP_kernel(
             return raw
 
         wg_raw, wu_raw = [None, None], [None, None]
-        nc.sync.dma_start(tab_w[:, T // 4 :], tab_cols[:, T // 4 :])
-
-        def load_halves(w, name):
-            parts = []
-            for k in range(2):
-                part = held.tile([P, PACK, GROUP // 2], F32, name=f"{name}{k}", tag=f"{name}{k}", align_bytes=64)
-                nc.sync.dma_start(
-                    part[:], w.rearrange("(p i) r -> p i r", i=PACK)[:, :, k * GROUP // 2 : (k + 1) * GROUP // 2]
-                )
-                parts.append(part)
-            return parts
-
-        wg0_parts = load_halves(wg, "wg0_part")
-        wu0_parts = load_halves(wu, "wu0_part")
-        wg_raw[1] = load_weight(wg, 1, "wg_raw1")
+        wg0_parts.append(load_half(wg, 1, "wg0_part1", 1))
+        tab_w = held.tile([P, T], I32, name="tab_w", align_bytes=64)
+        nc.sync.dma_start(tab_w[:], tab_words[0].rearrange("p t i -> p (t i)").bitcast(I32))
+        wu0_parts = [load_half(wu, k, f"wu0_part{k}", 1) for k in range(2)]
+        wd4_w = held.tile([P, 2 * N], U8, name="wd4_w", align_bytes=64)
+        nc.sync.dma_start(wd4_w[:].bitcast(I32), wd4_words[0].bitcast(I32))
+        wg1_parts = [load_half(wg, 2 + k, f"wg1_part{k}", 1) for k in range(2)]
         wu_raw[1] = load_weight(wu, 1, "wu_raw1")
         load_scale_rows(wd4_scales, 0)
         wd8_w = held.tile([P, N], I32, name="wd8_w", align_bytes=64)
@@ -97,12 +93,6 @@ def tile_list_gmlpt_silu_mix_gateP_kernel(
         warm_out = held.tile([P, 1], F32, name="warm_out")
         nc.scalar.activation(warm_out[:], warm[:], SILU)
 
-        wd4_d = held.tile([P, 2 * N], U8, name="wd4_d", align_bytes=64)
-        nc.vector.tensor_copy(
-            wd4_d[:].bitcast(U16).rearrange("p (t a m) -> p a t m", t=PACK, m=8),
-            wd4_w[:].bitcast(U16).rearrange("p (a m t) -> p a t m", t=PACK, m=8),
-        )
-
         v_s = held.tile([P, J], U8, name="v_s", align_bytes=64)
         nc.vector.tensor_copy(v_s[:], tab_s[:].indirect(offsets[:]))
 
@@ -113,11 +103,13 @@ def tile_list_gmlpt_silu_mix_gateP_kernel(
                 raw[:].rearrange("p i (m t) -> p m t i", t=PACK)[:, :, u * ts : (u + 1) * ts, :],
             )
 
-        def quantize_weight(name, parts):
+        def quantize_weight(name, parts, between=None):
             codes = held.tile([P, GROUP], U32, name=name + "_c", align_bytes=64)
             scales = held.tile([P, GROUP], U8, name=name + "_s", align_bytes=64)
             width = GROUP // len(parts)
             for u, rounded in enumerate(parts):
+                if u and between:
+                    between()
                 cols = slice(u * width, (u + 1) * width)
                 nc.vector.quantize_mx(out=codes[:, cols].bitcast(FP8X4), scales=scales[:, cols], in_=rounded)
             return codes, scales
@@ -128,28 +120,34 @@ def tile_list_gmlpt_silu_mix_gateP_kernel(
             nc.gpsimd.tensor_scalar(out, in_, 1.0, 0.0, MULT, ADD)
 
         wg_q, wu_q = [None, None], [None, None]
-        v_w = []
+        v_w = {}
 
-        def gather_words(half, tag):
-            words = held.tile([P, HALF], U32, name=f"v_w{half}", tag=tag, align_bytes=64)
-            picks = offsets[:, half * HALF // 16 : (half + 1) * HALF // 16]
-            nc.vector.tensor_copy(words[:], tab_w[:].bitcast(U32).indirect(picks))
-            v_w.append(words)
+        def gather_words(j0, j1, tag):
+            words = held.tile([P, j1 - j0], U32, name=f"v_w{j0}", tag=tag, align_bytes=64)
+            nc.vector.tensor_copy(words[:], tab_w[:].bitcast(U32).indirect(offsets[:, j0 // 16 : j1 // 16]))
+            for j in range(j0, j1, CHUNK):
+                v_w[j // CHUNK] = words[:, j - j0 : j - j0 + CHUNK]
 
-        gather_words(0, "v_w0")
 
-        def quantize_halves(parts, name):
+        def quantize_halves(parts, name, late_pair):
             rounded = held.tile([P, GROUP * PACK], BF16, name=name + "_bf", tag=name + "_bf", align_bytes=64)
             dealt = rounded[:].rearrange("p (t m i) -> p m t i", t=PACK, i=PACK)
             read = [part[:].rearrange("p i (m t) -> p m t i", t=PACK) for part in parts]
             on_scalar(dealt[:, : P // 2], read[0])
-            on_vector(dealt[:, P // 2 :, 0:2], read[1][:, :, 0:2])
+            late_pair(dealt[:, P // 2 :, 0:2], read[1][:, :, 0:2])
             on_scalar(dealt[:, P // 2 :, 2:4], read[1][:, :, 2:4])
             return quantize_weight(name, [rounded[:, : 2 * GROUP], rounded[:, 2 * GROUP :]])
 
-        wg_q[0] = quantize_halves(wg0_parts, "wg0")
-        gather_words(1, "wg0_bf")
-        wu_q[0] = quantize_halves(wu0_parts, "wu0")
+        wg_q[0] = quantize_halves(wg0_parts, "wg0", on_scalar)
+        gather_words(0, 256, "v_w0")
+        gather_words(256, J, "v_w1")
+        wu_q[0] = quantize_halves(wu0_parts, "wu0", on_vector)
+
+        wd4_d = held.tile([P, 2 * N], U8, name="wd4_d", tag="wu0_bf", align_bytes=64)
+        nc.vector.tensor_copy(
+            wd4_d[:].bitcast(U16).rearrange("p (t a m) -> p a t m", t=PACK, m=8),
+            wd4_w[:].bitcast(U16).rearrange("p (a m t) -> p a t m", t=PACK, m=8),
+        )
 
         h_bf = [held.tile([P, J * PACK], BF16, name=f"h_bf{b}", tag=f"h_bf{b}", align_bytes=64) for b in range(2)]
         h_c = [held.tile([P, J], U32, name=f"h_c{b}", align_bytes=64) for b in range(2)]
@@ -165,7 +163,7 @@ def tile_list_gmlpt_silu_mix_gateP_kernel(
                     out=acc[:, t, :],
                     lhsT=codes[:, ms].bitcast(FP8X4),
                     lhsT_scale=scales[:, ms],
-                    rhs=v_w[c * CHUNK // HALF][:, c * CHUNK % HALF : c * CHUNK % HALF + CHUNK].bitcast(FP8X4),
+                    rhs=v_w[c].bitcast(FP8X4),
                     rhs_scale=v_s[:, cols],
                     start=True,
                     stop=True,
@@ -200,15 +198,16 @@ def tile_list_gmlpt_silu_mix_gateP_kernel(
             hidden(0, c)
             if c == 4:
                 wg1_bf = held.tile([P, GROUP * PACK], BF16, name="wg1_bf", tag="wg1_bf", align_bytes=64)
-                round_weight(on_gpsimd, wg_raw[1], 0, 1, wg1_bf[:])
+                dealt = wg1_bf[:].rearrange("p (t m i) -> p m t i", t=PACK, i=PACK)
+                for k, part in enumerate(wg1_parts):
+                    on_gpsimd(dealt[:, k * P // 2 : (k + 1) * P // 2], part[:].rearrange("p i (m t) -> p m t i", t=PACK))
                 wg_q[1] = quantize_weight("wg1", [wg1_bf[:]])
         wu1_early = held.tile([P, 2 * GROUP], BF16, name="wu1_early", tag="wg1_bf", align_bytes=64)
         round_weight(on_gpsimd, wu_raw[1], 0, 2, wu1_early[:])
         wu1_late = held.tile([P, 2 * GROUP], BF16, name="wu1_late", tag="wu1_late", align_bytes=64)
         round_weight(on_scalar, wu_raw[1], 1, 2, wu1_late[:])
-        wu_q[1] = quantize_weight("wu1", [wu1_early[:], wu1_late[:]])
+        wu_q[1] = quantize_weight("wu1", [wu1_early[:], wu1_late[:]], lambda: quantize_hidden(0, 0, 4))
         acts.append(held.tile([P, CHUNKS, CHUNK, PACK], F32, name="act1", tag="act1", align_bytes=64))
-        quantize_hidden(0, 0, 4)
         quantize_hidden(0, 4, 8)
 
         dealt_wd = held.tile([P, N + N // 4], I32, name="dealt_wd", tag="h_bf0", align_bytes=64)

@@ -129,13 +129,12 @@ def tile_list_gmlpt_silu_mix_gateP_kernel(
                 v_w[j // CHUNK] = words[:, j - j0 : j - j0 + CHUNK]
 
 
-        def quantize_halves(parts, name, late_pair):
+        def quantize_halves(parts, name, second_half):
             rounded = held.tile([P, GROUP * PACK], BF16, name=name + "_bf", tag=name + "_bf", align_bytes=64)
             dealt = rounded[:].rearrange("p (t m i) -> p m t i", t=PACK, i=PACK)
             read = [part[:].rearrange("p i (m t) -> p m t i", t=PACK) for part in parts]
             on_scalar(dealt[:, : P // 2], read[0])
-            late_pair(dealt[:, P // 2 :, 0:2], read[1][:, :, 0:2])
-            on_scalar(dealt[:, P // 2 :, 2:4], read[1][:, :, 2:4])
+            second_half(dealt[:, P // 2 :], read[1])
             return quantize_weight(name, [rounded[:, : 2 * GROUP], rounded[:, 2 * GROUP :]])
 
         wg_q[0] = quantize_halves(wg0_parts, "wg0", on_scalar)
@@ -177,7 +176,7 @@ def tile_list_gmlpt_silu_mix_gateP_kernel(
             elif (b, c) == (0, 5):
                 act = held.tile([P, CHUNK, PACK], F32, name="act_fifth", tag="act1", align_bytes=64)[:]
             else:
-                act = acts[b][:, c % ACT_SLOTS if b == 0 else c]
+                act = acts[b][:, c % (ACT_SLOTS + 2) if b == 0 else c]
             nc.scalar.activation(act, ga[:].rearrange("p t j -> p j t"), SILU)
             ub = up_product(wu_q[b], c, "ub")
             nc.vector.tensor_tensor(
@@ -193,7 +192,7 @@ def tile_list_gmlpt_silu_mix_gateP_kernel(
                 out=h_c[b][:, cols].bitcast(FP8X4), scales=h_s[b][:, cols], in_=h_bf[b][:, c0 * GROUP : c1 * GROUP]
             )
 
-        acts = [held.tile([P, ACT_SLOTS, CHUNK, PACK], F32, name="act0", tag="wu0_part1", align_bytes=64)]
+        acts = [held.tile([P, ACT_SLOTS, CHUNK, PACK], F32, name="act0", tag="wu0_part0", align_bytes=64)]
         for c in range(CHUNKS):
             hidden(0, c)
             if c == 4:

@@ -73,7 +73,7 @@ def tile_list_gmlpt_silu_mix_gateP_kernel(
         tab_w = held.tile([P, T], I32, name="tab_w", align_bytes=64)
         nc.sync.dma_start(tab_w[:], tab_words[0].rearrange("p t i -> p (t i)").bitcast(I32))
         wu0_parts = [load_half(wu, k, f"wu0_part{k}", 1) for k in range(2)]
-        wd4_w = held.tile([P, 2 * N], U8, name="wd4_w", align_bytes=64)
+        wd4_w = held.tile([P, 2 * N], U8, name="wd4_w", tag="wd4_w", align_bytes=64)
         nc.sync.dma_start(wd4_w[:].bitcast(I32), wd4_words[0].bitcast(I32))
         wg1_parts = [load_half(wg, 2 + k, f"wg1_part{k}", 1) for k in range(2)]
         wu_raw[1] = load_weight(wu, 1, "wu_raw1")
@@ -196,12 +196,12 @@ def tile_list_gmlpt_silu_mix_gateP_kernel(
         for c in range(CHUNKS):
             hidden(0, c)
             if c == 4:
-                wg1_bf = held.tile([P, GROUP * PACK], BF16, name="wg1_bf", tag="wg1_bf", align_bytes=64)
+                wg1_bf = held.tile([P, GROUP * PACK], BF16, name="wg1_bf", tag="wd4_w", align_bytes=64)
                 dealt = wg1_bf[:].rearrange("p (t m i) -> p m t i", t=PACK, i=PACK)
                 for k, part in enumerate(wg1_parts):
                     on_gpsimd(dealt[:, k * P // 2 : (k + 1) * P // 2], part[:].rearrange("p i (m t) -> p m t i", t=PACK))
                 wg_q[1] = quantize_weight("wg1", [wg1_bf[:]])
-        wu1_early = held.tile([P, 2 * GROUP], BF16, name="wu1_early", tag="wg1_bf", align_bytes=64)
+        wu1_early = held.tile([P, 2 * GROUP], BF16, name="wu1_early", tag="wd4_w", align_bytes=64)
         round_weight(on_gpsimd, wu_raw[1], 0, 2, wu1_early[:])
         wu1_late = held.tile([P, 2 * GROUP], BF16, name="wu1_late", tag="wu1_late", align_bytes=64)
         round_weight(on_scalar, wu_raw[1], 1, 2, wu1_late[:])

@@ -262,10 +262,10 @@ def tile_list_gmlpt_silu_mix_gateP_kernel(
                 y_f[half][:, t, j0 - half * HALF : j1 - half * HALF],
                 MULT,
             )
+            nc.sync.dma_start(out_0.rearrange("(p t) j -> p t j", t=PACK)[:, t, j0:j1], out_f[s][:, t, :])
 
         def finish_span(s):
             j0, j1 = spans[s]
-            nc.sync.dma_start(out_0.rearrange("(p t) j -> p t j", t=PACK)[:, :, j0:j1], out_f[s])
             nc.scalar.copy(
                 out_bf[:, j0 * PACK : j1 * PACK].rearrange("p (a j t) -> p a t j", t=PACK, j=4),
                 out_f[s].rearrange("p t (a j) -> p a t j", j=4),

@@ -24,6 +24,9 @@ CHUNK = 128
 CHUNKS = J // CHUNK
 ACT_SLOTS = 4
 HALF = J // 2
+LOW = 8192
+HIGH = LOW + 4096
+NEXT = HIGH + 4096
 
 
 def tile_list_gmlpt_silu_mix_gateP_kernel(
@@ -73,10 +76,10 @@ def tile_list_gmlpt_silu_mix_gateP_kernel(
         tab_w = held.tile([P, T], I32, name="tab_w", align_bytes=64)
         nc.sync.dma_start(tab_w[:], tab_words[0].rearrange("p t i -> p (t i)").bitcast(I32))
         wu0_parts = [load_half(wu, k, f"wu0_part{k}", 1) for k in range(2)]
-        wd4_w = held.tile([P, 2 * N], U8, name="wd4_w", tag="wd4_w", align_bytes=64)
+        wd4_w = reused.tile([P, 2 * N], U8, name="wd4_w", offset=LOW)
         nc.sync.dma_start(wd4_w[:].bitcast(I32), wd4_words[0].bitcast(I32))
         wg1_parts = [load_half(wg, 2 + k, f"wg1_part{k}", 1) for k in range(2)]
-        wu_raw[1] = load_weight(wu, 1, "wu_raw1")
+        wu1_parts = [load_half(wu, 2 + k, f"wu1_part{k}", 1) for k in range(2)]
         load_scale_rows(wd4_scales, 0)
         wd8_w = held.tile([P, N], I32, name="wd8_w", align_bytes=64)
         nc.sync.dma_start(wd8_w[:], wd8_words[0].rearrange("p n i -> p (n i)").bitcast(I32))
@@ -103,16 +106,11 @@ def tile_list_gmlpt_silu_mix_gateP_kernel(
                 raw[:].rearrange("p i (m t) -> p m t i", t=PACK)[:, :, u * ts : (u + 1) * ts, :],
             )
 
-        def quantize_weight(name, parts, between=None):
-            codes = held.tile([P, GROUP], U32, name=name + "_c", align_bytes=64)
-            scales = held.tile([P, GROUP], U8, name=name + "_s", align_bytes=64)
-            width = GROUP // len(parts)
-            for u, rounded in enumerate(parts):
-                if u and between:
-                    between()
-                cols = slice(u * width, (u + 1) * width)
-                nc.vector.quantize_mx(out=codes[:, cols].bitcast(FP8X4), scales=scales[:, cols], in_=rounded)
-            return codes, scales
+        def quantize_part(name, rounded, planes, tag=None):
+            codes = held.tile([P, planes * P], U32, name=name + "_c", tag=tag or name + "_c", align_bytes=64)
+            scales = held.tile([P, planes * P], U8, name=name + "_s", align_bytes=64)
+            nc.vector.quantize_mx(out=codes[:].bitcast(FP8X4), scales=scales[:], in_=rounded)
+            return [(codes[:, t * P : (t + 1) * P], scales[:, t * P : (t + 1) * P]) for t in range(planes)]
 
         on_scalar, on_vector = nc.scalar.copy, nc.vector.tensor_copy
 
@@ -129,18 +127,23 @@ def tile_list_gmlpt_silu_mix_gateP_kernel(
                 v_w[j // CHUNK] = words[:, j - j0 : j - j0 + CHUNK]
 
 
-        def quantize_halves(parts, name, second_half):
-            rounded = held.tile([P, GROUP * PACK], BF16, name=name + "_bf", tag=name + "_bf", align_bytes=64)
-            dealt = rounded[:].rearrange("p (t m i) -> p m t i", t=PACK, i=PACK)
+        def quantize_halves(parts, name, first_half, second_half, rounded, calls):
+            dealt = rounded.rearrange("p (t m i) -> p m t i", t=PACK, i=PACK)
             read = [part[:].rearrange("p i (m t) -> p m t i", t=PACK) for part in parts]
-            on_scalar(dealt[:, : P // 2], read[0])
+            first_half(dealt[:, : P // 2], read[0])
             second_half(dealt[:, P // 2 :], read[1])
-            return quantize_weight(name, [rounded[:, : 2 * GROUP], rounded[:, 2 * GROUP :]])
+            planes = PACK // calls
+            quantised = []
+            for u in range(calls):
+                quantised += quantize_part(f"{name}_{u}", rounded[:, u * planes * GROUP : (u + 1) * planes * GROUP], planes)
+            return quantised
 
-        wg_q[0] = quantize_halves(wg0_parts, "wg0", on_scalar)
+        wg0_bf = held.tile([P, GROUP * PACK], BF16, name="wg0_bf", align_bytes=64)
+        wg_q[0] = quantize_halves(wg0_parts, "wg0", on_scalar, on_scalar, wg0_bf[:], 2)
         gather_words(0, 256, "v_w0")
         gather_words(256, J, "v_w1")
-        wu_q[0] = quantize_halves(wu0_parts, "wu0", on_vector)
+        wu0_bf = held.tile([P, GROUP * PACK], BF16, name="wu0_bf", tag="wu0_bf", align_bytes=64)
+        wu_q[0] = quantize_halves(wu0_parts, "wu0", on_scalar, on_vector, wu0_bf[:], 2)
 
         wd4_d = held.tile([P, 2 * N], U8, name="wd4_d", tag="wu0_bf", align_bytes=64)
         nc.vector.tensor_copy(
@@ -148,20 +151,20 @@ def tile_list_gmlpt_silu_mix_gateP_kernel(
             wd4_w[:].bitcast(U16).rearrange("p (a m t) -> p a t m", t=PACK, m=8),
         )
 
-        h_bf = [held.tile([P, J * PACK], BF16, name=f"h_bf{b}", tag=f"h_bf{b}", align_bytes=64) for b in range(2)]
-        h_c = [held.tile([P, J], U32, name=f"h_c{b}", align_bytes=64) for b in range(2)]
-        h_s = [held.tile([P, J], U8, name=f"h_s{b}", align_bytes=64) for b in range(2)]
+        h_bf10 = held.tile([P, HALF * PACK], BF16, name="h_bf10", align_bytes=64)
+        h_bf00 = reused.tile([P, J * PACK], BF16, name="h_bf00", offset=NEXT)
+        h_bf = {(0, 0): h_bf00[:, : HALF * PACK], (1, 0): h_bf10[:]}
+        h_q = {}
 
         def up_product(wq, c, tag):
-            codes, scales = wq
             acc = psum.tile([P, PACK, CHUNK], F32, name=tag, bufs=3)
             cols = slice(c * CHUNK, (c + 1) * CHUNK)
             for t in range(PACK):
-                ms = slice(t * P, (t + 1) * P)
+                codes, scales = wq[t]
                 nc.tensor.matmul_mx(
                     out=acc[:, t, :],
-                    lhsT=codes[:, ms].bitcast(FP8X4),
-                    lhsT_scale=scales[:, ms],
+                    lhsT=codes.bitcast(FP8X4),
+                    lhsT_scale=scales,
                     rhs=v_w[c].bitcast(FP8X4),
                     rhs_scale=v_s[:, cols],
                     start=True,
@@ -171,51 +174,43 @@ def tile_list_gmlpt_silu_mix_gateP_kernel(
 
         def hidden(b, c):
             ga = up_product(wg_q[b], c, "ga")
-            if (b, c) == (0, 4):
-                act = held.tile([P, CHUNK, PACK], F32, name="act_apart", tag="wu1_late", align_bytes=64)[:]
-            elif (b, c) == (0, 5):
-                act = held.tile([P, CHUNK, PACK], F32, name="act_fifth", tag="act1", align_bytes=64)[:]
+            if (b, c) == (0, 5):
+                act = held.tile([P, CHUNK, PACK], F32, name="act_apart", tag="wg1_part1", align_bytes=64)[:]
             else:
-                act = acts[b][:, c % (ACT_SLOTS + 2) if b == 0 else c]
+                act = acts[b][:, c]
             nc.scalar.activation(act, ga[:].rearrange("p t j -> p j t"), SILU)
             ub = up_product(wu_q[b], c, "ub")
-            nc.vector.tensor_tensor(
-                h_bf[b][:, c * GROUP : (c + 1) * GROUP].rearrange("p (j t) -> p j t", t=PACK),
-                ub[:].rearrange("p t j -> p j t"),
-                act,
-                MULT,
-            )
+            rounded = h_bf[b, c // 4][:, c % 4 * GROUP : (c % 4 + 1) * GROUP].rearrange("p (j t) -> p j t", t=PACK)
+            if (b, c) == (1, CHUNKS - 1):
+                ub_f = held.tile([P, CHUNK, PACK], F32, name="ub_f", align_bytes=64)
+                nc.scalar.copy(ub_f[:], ub[:].rearrange("p t j -> p j t"))
+                nc.gpsimd.tensor_tensor(rounded, ub_f[:], act, MULT)
+            else:
+                nc.vector.tensor_tensor(rounded, ub[:].rearrange("p t j -> p j t"), act, MULT)
 
-        def quantize_hidden(b, c0, c1):
-            cols = slice(c0 * CHUNK, c1 * CHUNK)
-            nc.vector.quantize_mx(
-                out=h_c[b][:, cols].bitcast(FP8X4), scales=h_s[b][:, cols], in_=h_bf[b][:, c0 * GROUP : c1 * GROUP]
-            )
+        def quantize_hidden(b, half, codes=None):
+            if codes is None:
+                codes = held.tile([P, HALF], U32, name=f"h_c{b}{half}", align_bytes=64)
+            scales = held.tile([P, HALF], U8, name=f"h_s{b}{half}", align_bytes=64)
+            nc.vector.quantize_mx(out=codes[:].bitcast(FP8X4), scales=scales[:], in_=h_bf[b, half])
+            h_q[b, half] = codes[:].bitcast(FP8X4), scales[:]
 
-        acts = [held.tile([P, ACT_SLOTS, CHUNK, PACK], F32, name="act0", tag="wu0_part0", align_bytes=64)]
-        for c in range(CHUNKS):
+        acts = [held.tile([P, CHUNKS, CHUNK, PACK], F32, name="act0", tag="wu0_part0", align_bytes=64)]
+        for c in (0, 1, 2, 4, 5, 6, 7, 3):
             hidden(0, c)
-            if c == 4:
-                wg1_bf = held.tile([P, GROUP * PACK], BF16, name="wg1_bf", tag="wd4_w", align_bytes=64)
-                dealt = wg1_bf[:].rearrange("p (t m i) -> p m t i", t=PACK, i=PACK)
-                for k, part in enumerate(wg1_parts):
-                    on_gpsimd(dealt[:, k * P // 2 : (k + 1) * P // 2], part[:].rearrange("p i (m t) -> p m t i", t=PACK))
-                wg_q[1] = quantize_weight("wg1", [wg1_bf[:]])
-        wu1_early = held.tile([P, 2 * GROUP], BF16, name="wu1_early", tag="wd4_w", align_bytes=64)
-        round_weight(on_gpsimd, wu_raw[1], 0, 2, wu1_early[:])
-        wu1_late = held.tile([P, 2 * GROUP], BF16, name="wu1_late", tag="wu1_late", align_bytes=64)
-        round_weight(on_scalar, wu_raw[1], 1, 2, wu1_late[:])
-        wu_q[1] = quantize_weight("wu1", [wu1_early[:], wu1_late[:]], lambda: quantize_hidden(0, 0, 4))
+            if c == 2:
+                wg1_bf = reused.tile([P, 2 * GROUP * PACK], BF16, name="wg1_bf", offset=LOW)
+                wg_q[1] = quantize_halves(wg1_parts, "wg1", on_gpsimd, on_scalar, wg1_bf[:, : GROUP * PACK], 1)
+                h_bf[0, 1] = reused.tile([P, HALF * PACK], BF16, name="h_bf01", offset=HIGH)[:]
+        wu1_bf = reused.tile([P, GROUP * PACK], BF16, name="wu1_bf", offset=LOW)
+        wu_q[1] = quantize_halves(wu1_parts, "wu1", on_gpsimd, on_gpsimd, wu1_bf[:], 1)
         acts.append(held.tile([P, CHUNKS, CHUNK, PACK], F32, name="act1", tag="act1", align_bytes=64))
-        quantize_hidden(0, 4, 8)
+        quantize_hidden(0, 1)
+        quantize_hidden(0, 0, reused.tile([P, HALF], U32, name="h_c00", offset=LOW))
 
-        dealt_wd = held.tile([P, N + N // 4], I32, name="dealt_wd", tag="h_bf0", align_bytes=64)
-        wd8_d = dealt_wd[:, :N]
-        nc.gpsimd.tensor_copy(
-            wd8_d.rearrange("p (t a m) -> p a t m", t=PACK, m=4),
-            wd8_w[:].rearrange("p (a m t) -> p a t m", t=PACK, m=4),
-        )
-        wd_sd = dealt_wd[:, N:].bitcast(U8)
+        h_bf[1, 1] = reused.tile([P, HALF * PACK], BF16, name="h_bf11", offset=NEXT + 4096)[:]
+        wd8_d = held.tile([P, N], U32, name="wd8_d", align_bytes=64)
+        wd_sd = reused.tile([P, N], U8, name="wd_sd", offset=NEXT)[:]
         nc.gpsimd.tensor_copy(
             wd_sd.rearrange("p (t a m) -> p a t m", t=PACK, m=16),
             wd_s[:].rearrange("p (a m t) -> p a t m", t=PACK, m=16),
@@ -223,22 +218,21 @@ def tile_list_gmlpt_silu_mix_gateP_kernel(
 
         spans = [(0, 512), (512, 832), (832, 1024)]
         coded = [(0, 512), (512, 768), (768, 1024)]
-        y_f = [reused.tile([P, PACK, HALF], F32, name="y_f0", offset=0), held.tile([P, PACK, HALF], F32, name="y_f1")]
+        y_f = [reused.tile([P, PACK, HALF], F32, name="y_f0", offset=0, align_bytes=64), held.tile([P, PACK, HALF], F32, name="y_f1")]
         out_f = [held.tile([P, PACK, HALF], F32, name="out_f0")[:]]
         out_bf = held.tile([P, J * PACK], BF16, name="out_bf", align_bytes=64)
         out_c = held.tile([P, J], U32, name="out_c", align_bytes=64)
         out_s = held.tile([P, J], U8, name="out_s", align_bytes=64)
 
         def down_product(half, t):
-            cols = slice(half * HALF, (half + 1) * HALF)
             ms = slice(t * P, (t + 1) * P)
             y = psum.tile([P, HALF], F32, name="y", bufs=2)
             nc.tensor.matmul_mx(
                 out=y[:],
                 lhsT=wd8_d[:, ms].bitcast(FP8X4),
                 lhsT_scale=wd_sd[4:P, ms],
-                rhs=h_c[0][:, cols].bitcast(FP8X4),
-                rhs_scale=h_s[0][:, cols],
+                rhs=h_q[0, half][0],
+                rhs_scale=h_q[0, half][1],
                 start=True,
                 stop=False,
             )
@@ -246,8 +240,8 @@ def tile_list_gmlpt_silu_mix_gateP_kernel(
                 out=y[:],
                 lhsT=wd4_d[:, 2 * t * P : 2 * (t + 1) * P].bitcast(FP4X4),
                 lhsT_scale=wd_sd[:, ms],
-                rhs=h_c[1][:, cols].bitcast(FP8X4),
-                rhs_scale=h_s[1][:, cols],
+                rhs=h_q[1, half][0],
+                rhs_scale=h_q[1, half][1],
                 start=False,
                 stop=True,
             )
@@ -262,7 +256,9 @@ def tile_list_gmlpt_silu_mix_gateP_kernel(
                 y_f[half][:, t, j0 - half * HALF : j1 - half * HALF],
                 MULT,
             )
-            nc.sync.dma_start(out_0.rearrange("(p t) j -> p t j", t=PACK)[:, t, j0:j1], out_f[s][:, t, :])
+            if t % 2:
+                pair = slice(t - 1, t + 1)
+                nc.sync.dma_start(out_0.rearrange("(p t) j -> p t j", t=PACK)[:, pair, j0:j1], out_f[s][:, pair, :])
 
         def finish_span(s):
             j0, j1 = spans[s]
@@ -276,14 +272,18 @@ def tile_list_gmlpt_silu_mix_gateP_kernel(
                 out=out_c[:, j0:j1].bitcast(FP8X4), scales=out_s[:, j0:j1], in_=out_bf[:, j0 * PACK : j1 * PACK]
             )
 
-        for c in range(CHUNKS):
+        for c in (7, 0, 1, 2, 3, 4, 5, 6):
             hidden(1, c)
             if c == 4:
-                quantize_hidden(1, 0, 4)
+                nc.scalar.copy(
+                    wd8_d[:].rearrange("p (t a m) -> p a t m", t=PACK, m=4),
+                    wd8_w[:].bitcast(U32).rearrange("p (a m t) -> p a t m", t=PACK, m=4),
+                )
+                quantize_hidden(1, 0)
                 for t in range(PACK):
                     down_product(0, t)
         gate_plane(0, 0)
-        quantize_hidden(1, 4, 8)
+        quantize_hidden(1, 1)
         for t in range(PACK):
             down_product(1, t)
         for t in range(1, PACK):

@@ -55,16 +55,14 @@ def tile_list_gmlpt_silu_mix_gateP_kernel(
         nc.gpsimd.memset(tab_s[:].bitcast(I32), 0)
         tab_rows = tab_scales[0].bitcast(I32)
         for q in range(4):
-            nc.sync.dma_start(tab_s[32 * q : 32 * q + 4, :].bitcast(I32), tab_rows[4 * q : 4 * q + 4, :])
+            nc.sync.dma_start(tab_s[q:P:32, :].bitcast(I32), tab_rows[q:16:4, :])
 
         wd_s = held.tile([P, N], U8, name="wd_s", align_bytes=64)
         nc.gpsimd.memset(wd_s[:].bitcast(I32), 0)
 
         def load_scale_rows(scales, first):
             for q in range(4):
-                nc.sync.dma_start(
-                    wd_s[32 * q + first : 32 * q + first + 4, :].bitcast(I32), scales[0].bitcast(I32)[4 * q : 4 * q + 4, :]
-                )
+                nc.sync.dma_start(wd_s[first + q : P : 32, :].bitcast(I32), scales[0].bitcast(I32)[q:16:4, :])
 
         def load_weight(w, b, name):
             raw = held.tile([P, PACK, GROUP], F32, name=name, tag=name, align_bytes=64)
@@ -129,9 +127,13 @@ def tile_list_gmlpt_silu_mix_gateP_kernel(
 
         def quantize_halves(parts, name, first_half, second_half, rounded, calls):
             dealt = rounded.rearrange("p (t m i) -> p m t i", t=PACK, i=PACK)
-            read = [part[:].rearrange("p i (m t) -> p m t i", t=PACK) for part in parts]
-            first_half(dealt[:, : P // 2], read[0])
-            second_half(dealt[:, P // 2 :], read[1])
+            paired = rounded.rearrange("p (t m u e) -> p m u t e", t=PACK, u=2, e=2)
+            for k, copy in enumerate((first_half, second_half)):
+                ms = slice(k * P // 2, (k + 1) * P // 2)
+                if copy is on_gpsimd:
+                    copy(dealt[:, ms], parts[k][:].rearrange("p i (m t) -> p m t i", t=PACK))
+                else:
+                    copy(paired[:, ms], parts[k][:].rearrange("p (u e) (m t) -> p m u t e", e=2, t=PACK))
             planes = PACK // calls
             quantised = []
             for u in range(calls):
@@ -157,7 +159,7 @@ def tile_list_gmlpt_silu_mix_gateP_kernel(
         h_q = {}
 
         def up_product(wq, c, tag):
-            acc = psum.tile([P, PACK, CHUNK], F32, name=tag, bufs=3)
+            acc = psum.tile([P, PACK, CHUNK], F32, name=tag, tag=tag, bufs=2 if tag == "y" else 3)
             cols = slice(c * CHUNK, (c + 1) * CHUNK)
             for t in range(PACK):
                 codes, scales = wq[t]
@@ -179,7 +181,7 @@ def tile_list_gmlpt_silu_mix_gateP_kernel(
             else:
                 act = acts[b][:, c]
             nc.scalar.activation(act, ga[:].rearrange("p t j -> p j t"), SILU)
-            ub = up_product(wu_q[b], c, "ub")
+            ub = up_product(wu_q[b], c, "y" if (b, c) == (1, CHUNKS - 1) else "ub")
             rounded = h_bf[b, c // 4][:, c % 4 * GROUP : (c % 4 + 1) * GROUP].rearrange("p (j t) -> p j t", t=PACK)
             if (b, c) == (1, CHUNKS - 1):
                 ub_f = held.tile([P, CHUNK, PACK], F32, name="ub_f", align_bytes=64)
@@ -193,7 +195,7 @@ def tile_list_gmlpt_silu_mix_gateP_kernel(
                 codes = held.tile([P, HALF], U32, name=f"h_c{b}{half}", align_bytes=64)
             scales = held.tile([P, HALF], U8, name=f"h_s{b}{half}", align_bytes=64)
             nc.vector.quantize_mx(out=codes[:].bitcast(FP8X4), scales=scales[:], in_=h_bf[b, half])
-            h_q[b, half] = codes[:].bitcast(FP8X4), scales[:]
+            h_q[b, half] = codes, scales
 
         acts = [held.tile([P, CHUNKS, CHUNK, PACK], F32, name="act0", tag="wu0_part0", align_bytes=64)]
         for c in (0, 1, 2, 4, 5, 6, 7, 3):
@@ -216,23 +218,24 @@ def tile_list_gmlpt_silu_mix_gateP_kernel(
             wd_s[:].rearrange("p (a m t) -> p a t m", t=PACK, m=16),
         )
 
-        spans = [(0, 512), (512, 832), (832, 1024)]
-        coded = [(0, 512), (512, 768), (768, 1024)]
+        spans = [(0, 512), (512, 896), (896, 1024)]
         y_f = [reused.tile([P, PACK, HALF], F32, name="y_f0", offset=0, align_bytes=64), held.tile([P, PACK, HALF], F32, name="y_f1")]
         out_f = [held.tile([P, PACK, HALF], F32, name="out_f0")[:]]
         out_bf = held.tile([P, J * PACK], BF16, name="out_bf", align_bytes=64)
         out_c = held.tile([P, J], U32, name="out_c", align_bytes=64)
         out_s = held.tile([P, J], U8, name="out_s", align_bytes=64)
 
-        def down_product(half, t):
+        def down_product(t, j0, j1):
+            half = j0 // HALF
             ms = slice(t * P, (t + 1) * P)
-            y = psum.tile([P, HALF], F32, name="y", bufs=2)
+            cols = slice(j0 - half * HALF, j1 - half * HALF)
+            y = psum.tile([P, j1 - j0], F32, name="y", tag="y", bufs=2)
             nc.tensor.matmul_mx(
                 out=y[:],
                 lhsT=wd8_d[:, ms].bitcast(FP8X4),
                 lhsT_scale=wd_sd[4:P, ms],
-                rhs=h_q[0, half][0],
-                rhs_scale=h_q[0, half][1],
+                rhs=h_q[0, half][0][:, cols].bitcast(FP8X4),
+                rhs_scale=h_q[0, half][1][:, cols],
                 start=True,
                 stop=False,
             )
@@ -240,25 +243,34 @@ def tile_list_gmlpt_silu_mix_gateP_kernel(
                 out=y[:],
                 lhsT=wd4_d[:, 2 * t * P : 2 * (t + 1) * P].bitcast(FP4X4),
                 lhsT_scale=wd_sd[:, ms],
-                rhs=h_q[1, half][0],
-                rhs_scale=h_q[1, half][1],
+                rhs=h_q[1, half][0][:, cols].bitcast(FP8X4),
+                rhs_scale=h_q[1, half][1][:, cols],
                 start=False,
                 stop=True,
             )
-            nc.scalar.copy(y_f[half][:, t, :], y[:])
+            nc.scalar.copy(y_f[half][:, t, cols], y[:])
 
-        def gate_plane(s, t):
-            j0, j1 = spans[s]
+        def gate_columns(s, t, j0, j1):
             half = j0 // HALF
+            first = spans[s][0]
             nc.vector.tensor_tensor(
-                out_f[s][:, t, :],
+                out_f[s][:, t, j0 - first : j1 - first],
                 gate_rows[t][:].indirect(offsets[:, j0 // 16 : j1 // 16]),
                 y_f[half][:, t, j0 - half * HALF : j1 - half * HALF],
                 MULT,
             )
+
+        def gate_plane(s, t):
+            j0, j1 = spans[s]
+            gate_columns(s, t, j0, j1)
             if t % 2:
                 pair = slice(t - 1, t + 1)
                 nc.sync.dma_start(out_0.rearrange("(p t) j -> p t j", t=PACK)[:, pair, j0:j1], out_f[s][:, pair, :])
+                if s == 1:
+                    nc.scalar.copy(
+                        out_bf[:, j0 * PACK : j1 * PACK].rearrange("p (j t) -> p j t", t=PACK)[:, :, pair],
+                        out_f[s][:, pair, :].rearrange("p t j -> p j t"),
+                    )
 
         def finish_span(s):
             j0, j1 = spans[s]
@@ -280,12 +292,15 @@ def tile_list_gmlpt_silu_mix_gateP_kernel(
                     wd8_w[:].bitcast(U32).rearrange("p (a m t) -> p a t m", t=PACK, m=4),
                 )
                 quantize_hidden(1, 0)
-                for t in range(PACK):
-                    down_product(0, t)
-        gate_plane(0, 0)
+                down_product(0, 0, HALF // 2)
+                down_product(0, HALF // 2, HALF)
+                for t in range(1, PACK):
+                    down_product(t, 0, HALF)
+        gate_columns(0, 0, 0, HALF // 2)
+        gate_columns(0, 0, HALF // 2, HALF)
         quantize_hidden(1, 1)
         for t in range(PACK):
-            down_product(1, t)
+            down_product(t, HALF, J)
         for t in range(1, PACK):
             gate_plane(0, t)
         finish_span(0)
@@ -295,12 +310,13 @@ def tile_list_gmlpt_silu_mix_gateP_kernel(
         for s in range(1, len(spans)):
             for t in range(PACK):
                 gate_plane(s, t)
-            finish_span(s)
-        for j0, j1 in coded:
+            if s != 1:
+                finish_span(s)
+        for j0, j1 in spans:
             quantize_output(j0, j1)
             nc.sync.dma_start(
                 out_1[0].rearrange("p j i -> p (j i)").bitcast(I32)[:, j0:j1], out_c[:, j0:j1].bitcast(I32)
             )
         for q in range(4):
             queue = nc.scalar if q % 2 else nc.sync
-            queue.dma_start(out_2[0].bitcast(I32)[4 * q : 4 * q + 4, :], out_s[32 * q : 32 * q + 4, :].bitcast(I32))
+            queue.dma_start(out_2[0].bitcast(I32)[q:16:4, :], out_s[q:P:32, :].bitcast(I32))

@@ -225,11 +225,11 @@ def tile_list_gmlpt_silu_mix_gateP_kernel(
         out_c = held.tile([P, J], U32, name="out_c", align_bytes=64)
         out_s = held.tile([P, J], U8, name="out_s", align_bytes=64)
 
-        def down_product(t, j0, j1):
+        def down_product(t, j0, j1, bank):
             half = j0 // HALF
             ms = slice(t * P, (t + 1) * P)
             cols = slice(j0 - half * HALF, j1 - half * HALF)
-            y = psum.tile([P, j1 - j0], F32, name="y", tag="y", bufs=2)
+            y = psum.tile([P, j1 - j0], F32, name="y", tag=bank, bufs=2 if bank == "y" else 3)
             nc.tensor.matmul_mx(
                 out=y[:],
                 lhsT=wd8_d[:, ms].bitcast(FP8X4),
@@ -292,15 +292,14 @@ def tile_list_gmlpt_silu_mix_gateP_kernel(
                     wd8_w[:].bitcast(U32).rearrange("p (a m t) -> p a t m", t=PACK, m=4),
                 )
                 quantize_hidden(1, 0)
-                down_product(0, 0, HALF // 2)
-                down_product(0, HALF // 2, HALF)
-                for t in range(1, PACK):
-                    down_product(t, 0, HALF)
-        gate_columns(0, 0, 0, HALF // 2)
-        gate_columns(0, 0, HALF // 2, HALF)
-        quantize_hidden(1, 1)
+                down_product(0, 0, HALF // 2, "y")
+                down_product(0, HALF // 2, HALF, "y")
+        for t in range(1, PACK):
+            down_product(t, 0, HALF, "ga")
+        gate_plane(0, 0)
+        quantize_hidden(1, 1, reused.tile([P, HALF], U32, name="h_c11", offset=LOW))
         for t in range(PACK):
-            down_product(t, HALF, J)
+            down_product(t, HALF, J, "ub" if t < 3 else "y")
         for t in range(1, PACK):
             gate_plane(0, t)
         finish_span(0)

@@ -20,13 +20,30 @@ SILU = mybir.ActivationFunctionType.Silu
 P = 128
 PACK = 4
 GROUP = P * PACK
+QUADRANT = 32
+SCALE_ROWS = GROUP // 32
+WD8_SCALES_AT = 4
 CHUNK = 128
 CHUNKS = J // CHUNK
-ACT_SLOTS = 4
 HALF = J // 2
-LOW = 8192
-HIGH = LOW + 4096
-NEXT = HIGH + 4096
+HALF_CHUNKS = CHUNKS // 2
+HALF_M = P // 2
+BANKS = {"ga": 3, "ub": 3, "y": 2}
+
+FIRST_WORDS = 2 * CHUNK
+WU1_SPLIT = 96
+EARLY_CHUNKS = HALF_CHUNKS - 1
+GROUP0_TURNS = [*range(EARLY_CHUNKS), *range(HALF_CHUNKS, CHUNKS), EARLY_CHUNKS]
+AFTER_ROUNDING = HALF_CHUNKS + 1
+ON_GPSIMD = CHUNKS - 1
+GROUP1_TURNS = [ON_GPSIMD, *range(ON_GPSIMD)]
+SPANS = [(0, HALF), (HALF, J - CHUNK), (J - CHUNK, J)]
+MIDDLE = 1
+
+ROUNDED_BYTES = GROUP * PACK * 2
+LOW = PACK * HALF * 4
+HIGH = LOW + ROUNDED_BYTES
+NEXT = HIGH + ROUNDED_BYTES
 
 
 def tile_list_gmlpt_silu_mix_gateP_kernel(
@@ -45,31 +62,26 @@ def tile_list_gmlpt_silu_mix_gateP_kernel(
             part = held.tile([P, PACK, GROUP // 2], F32, name=name, tag=name, align_bytes=64)
             rows = w.rearrange("(p i) r -> p i r", i=PACK)[:, :, k * GROUP // 2 : (k + 1) * GROUP // 2]
             for u in range(pieces):
-                planes = slice(u * PACK // pieces, (u + 1) * PACK // pieces)
-                nc.sync.dma_start(part[:, planes], rows[:, planes])
+                some = slice(u * PACK // pieces, (u + 1) * PACK // pieces)
+                nc.sync.dma_start(part[:, some], rows[:, some])
             return part
+
+        def scale_rows(tile, first, r):
+            return tile[first + r : P : QUADRANT, :].bitcast(I32)
+
+        def load_scale_rows(tile, first, scales):
+            for r in range(PACK):
+                nc.sync.dma_start(scale_rows(tile, first, r), scales[0].bitcast(I32)[r:SCALE_ROWS:PACK, :])
 
         wg0_parts = [load_half(wg, 0, "wg0_part0", 2)]
 
         tab_s = held.tile([P, T], U8, name="tab_s", align_bytes=64)
         nc.gpsimd.memset(tab_s[:].bitcast(I32), 0)
-        tab_rows = tab_scales[0].bitcast(I32)
-        for q in range(4):
-            nc.sync.dma_start(tab_s[q:P:32, :].bitcast(I32), tab_rows[q:16:4, :])
+        load_scale_rows(tab_s, 0, tab_scales)
 
         wd_s = held.tile([P, N], U8, name="wd_s", align_bytes=64)
         nc.gpsimd.memset(wd_s[:].bitcast(I32), 0)
 
-        def load_scale_rows(scales, first):
-            for q in range(4):
-                nc.sync.dma_start(wd_s[first + q : P : 32, :].bitcast(I32), scales[0].bitcast(I32)[q:16:4, :])
-
-        def load_weight(w, b, name):
-            raw = held.tile([P, PACK, GROUP], F32, name=name, tag=name, align_bytes=64)
-            nc.sync.dma_start(raw[:], w.rearrange("(p i) r -> p i r", i=PACK)[:, :, b * GROUP : (b + 1) * GROUP])
-            return raw
-
-        wg_raw, wu_raw = [None, None], [None, None]
         wg0_parts.append(load_half(wg, 1, "wg0_part1", 1))
         tab_w = held.tile([P, T], I32, name="tab_w", align_bytes=64)
         nc.sync.dma_start(tab_w[:], tab_words[0].rearrange("p t i -> p (t i)").bitcast(I32))
@@ -78,7 +90,7 @@ def tile_list_gmlpt_silu_mix_gateP_kernel(
         nc.sync.dma_start(wd4_w[:].bitcast(I32), wd4_words[0].bitcast(I32))
         wg1_parts = [load_half(wg, 2 + k, f"wg1_part{k}", 1) for k in range(2)]
         wu1_parts = [load_half(wu, 2 + k, f"wu1_part{k}", 1) for k in range(2)]
-        load_scale_rows(wd4_scales, 0)
+        load_scale_rows(wd_s, 0, wd4_scales)
         wd8_w = held.tile([P, N], I32, name="wd8_w", align_bytes=64)
         nc.sync.dma_start(wd8_w[:], wd8_words[0].rearrange("p n i -> p (n i)").bitcast(I32))
         gate_rows = []
@@ -87,7 +99,7 @@ def tile_list_gmlpt_silu_mix_gateP_kernel(
             nc.sync.dma_start(rows[:], gT.rearrange("(p t) c -> p t c", t=PACK)[:, t, :])
             gate_rows.append(rows)
             if t == 0:
-                load_scale_rows(wd8_scales, 4)
+                load_scale_rows(wd_s, WD8_SCALES_AT, wd8_scales)
 
         warm = held.tile([P, 1], F32, name="warm")
         nc.vector.memset(warm[:], 0.0)
@@ -97,55 +109,45 @@ def tile_list_gmlpt_silu_mix_gateP_kernel(
         v_s = held.tile([P, J], U8, name="v_s", align_bytes=64)
         nc.vector.tensor_copy(v_s[:], tab_s[:].indirect(offsets[:]))
 
-        def round_weight(copy, raw, u, parts, rounded):
-            ts = PACK // parts
-            copy(
-                rounded.rearrange("p (t m i) -> p m t i", t=ts, i=PACK),
-                raw[:].rearrange("p i (m t) -> p m t i", t=PACK)[:, :, u * ts : (u + 1) * ts, :],
-            )
-
-        def quantize_part(name, rounded, planes, tag=None):
-            codes = held.tile([P, planes * P], U32, name=name + "_c", tag=tag or name + "_c", align_bytes=64)
-            scales = held.tile([P, planes * P], U8, name=name + "_s", align_bytes=64)
-            nc.vector.quantize_mx(out=codes[:].bitcast(FP8X4), scales=scales[:], in_=rounded)
-            return [(codes[:, t * P : (t + 1) * P], scales[:, t * P : (t + 1) * P]) for t in range(planes)]
-
-        on_scalar, on_vector = nc.scalar.copy, nc.vector.tensor_copy
-
-        def on_gpsimd(out, in_):
-            nc.gpsimd.tensor_scalar(out, in_, 1.0, 0.0, MULT, ADD)
-
-        wg_q, wu_q = [None, None], [None, None]
         v_w = {}
 
-        def gather_words(j0, j1, tag):
-            words = held.tile([P, j1 - j0], U32, name=f"v_w{j0}", tag=tag, align_bytes=64)
+        def gather_words(j0, j1):
+            words = held.tile([P, j1 - j0], U32, name=f"v_w{j0}", align_bytes=64)
             nc.vector.tensor_copy(words[:], tab_w[:].bitcast(U32).indirect(offsets[:, j0 // 16 : j1 // 16]))
             for j in range(j0, j1, CHUNK):
                 v_w[j // CHUNK] = words[:, j - j0 : j - j0 + CHUNK]
 
+        def round_places(engine, parts, rounded, m0, m1):
+            part = parts[m0 // HALF_M][:]
+            ms = slice(m0 % HALF_M, m0 % HALF_M + m1 - m0)
+            if engine == "gpsimd":
+                dealt = rounded.rearrange("p (t m i) -> p m t i", t=PACK, i=PACK)[:, m0:m1]
+                nc.gpsimd.tensor_scalar(dealt, part.rearrange("p i (m t) -> p m t i", t=PACK)[:, ms], 1.0, 0.0, MULT, ADD)
+            else:
+                dealt = rounded.rearrange("p (t m u e) -> p m u t e", t=PACK, u=2, e=2)[:, m0:m1]
+                copy = nc.scalar.copy if engine == "scalar" else nc.vector.tensor_copy
+                copy(dealt, part.rearrange("p (u e) (m t) -> p m u t e", e=2, t=PACK)[:, ms])
 
-        def quantize_halves(parts, name, first_half, second_half, rounded, calls):
-            dealt = rounded.rearrange("p (t m i) -> p m t i", t=PACK, i=PACK)
-            paired = rounded.rearrange("p (t m u e) -> p m u t e", t=PACK, u=2, e=2)
-            for k, copy in enumerate((first_half, second_half)):
-                ms = slice(k * P // 2, (k + 1) * P // 2)
-                if copy is on_gpsimd:
-                    copy(dealt[:, ms], parts[k][:].rearrange("p i (m t) -> p m t i", t=PACK))
-                else:
-                    copy(paired[:, ms], parts[k][:].rearrange("p (u e) (m t) -> p m u t e", e=2, t=PACK))
+        def quantize_weight(parts, name, shares, rounded, calls):
+            for engine, m0, m1 in shares:
+                round_places(engine, parts, rounded, m0, m1)
             planes = PACK // calls
             quantised = []
             for u in range(calls):
-                quantised += quantize_part(f"{name}_{u}", rounded[:, u * planes * GROUP : (u + 1) * planes * GROUP], planes)
+                codes = held.tile([P, planes * P], U32, name=f"{name}_{u}_c", align_bytes=64)
+                scales = held.tile([P, planes * P], U8, name=f"{name}_{u}_s", align_bytes=64)
+                values = rounded[:, u * planes * GROUP : (u + 1) * planes * GROUP]
+                nc.vector.quantize_mx(out=codes[:].bitcast(FP8X4), scales=scales[:], in_=values)
+                quantised += [(codes[:, t * P : (t + 1) * P], scales[:, t * P : (t + 1) * P]) for t in range(planes)]
             return quantised
 
+        wg_q, wu_q = {}, {}
         wg0_bf = held.tile([P, GROUP * PACK], BF16, name="wg0_bf", align_bytes=64)
-        wg_q[0] = quantize_halves(wg0_parts, "wg0", on_scalar, on_scalar, wg0_bf[:], 2)
-        gather_words(0, 256, "v_w0")
-        gather_words(256, J, "v_w1")
+        wg_q[0] = quantize_weight(wg0_parts, "wg0", [("scalar", 0, HALF_M), ("scalar", HALF_M, P)], wg0_bf[:], 2)
+        gather_words(0, FIRST_WORDS)
+        gather_words(FIRST_WORDS, J)
         wu0_bf = held.tile([P, GROUP * PACK], BF16, name="wu0_bf", tag="wu0_bf", align_bytes=64)
-        wu_q[0] = quantize_halves(wu0_parts, "wu0", on_scalar, on_vector, wu0_bf[:], 2)
+        wu_q[0] = quantize_weight(wu0_parts, "wu0", [("scalar", 0, HALF_M), ("vector", HALF_M, P)], wu0_bf[:], 2)
 
         wd4_d = held.tile([P, 2 * N], U8, name="wd4_d", tag="wu0_bf", align_bytes=64)
         nc.vector.tensor_copy(
@@ -158,9 +160,8 @@ def tile_list_gmlpt_silu_mix_gateP_kernel(
         h_bf = {(0, 0): h_bf00[:, : HALF * PACK], (1, 0): h_bf10[:]}
         h_q = {}
 
-        def up_product(wq, c, tag):
-            acc = psum.tile([P, PACK, CHUNK], F32, name=tag, tag=tag, bufs=2 if tag == "y" else 3)
-            cols = slice(c * CHUNK, (c + 1) * CHUNK)
+        def up_product(wq, c, bank):
+            acc = psum.tile([P, PACK, CHUNK], F32, name=bank, tag=bank, bufs=BANKS[bank])
             for t in range(PACK):
                 codes, scales = wq[t]
                 nc.tensor.matmul_mx(
@@ -168,49 +169,52 @@ def tile_list_gmlpt_silu_mix_gateP_kernel(
                     lhsT=codes.bitcast(FP8X4),
                     lhsT_scale=scales,
                     rhs=v_w[c].bitcast(FP8X4),
-                    rhs_scale=v_s[:, cols],
+                    rhs_scale=v_s[:, c * CHUNK : (c + 1) * CHUNK],
                     start=True,
                     stop=True,
                 )
-            return acc
+            return acc[:].rearrange("p t j -> p j t")
 
         def hidden(b, c):
             ga = up_product(wg_q[b], c, "ga")
-            if (b, c) == (0, 5):
+            if (b, c) == (0, AFTER_ROUNDING):
                 act = held.tile([P, CHUNK, PACK], F32, name="act_apart", tag="wg1_part1", align_bytes=64)[:]
             else:
                 act = acts[b][:, c]
-            nc.scalar.activation(act, ga[:].rearrange("p t j -> p j t"), SILU)
-            ub = up_product(wu_q[b], c, "y" if (b, c) == (1, CHUNKS - 1) else "ub")
-            rounded = h_bf[b, c // 4][:, c % 4 * GROUP : (c % 4 + 1) * GROUP].rearrange("p (j t) -> p j t", t=PACK)
-            if (b, c) == (1, CHUNKS - 1):
+            nc.scalar.activation(act, ga, SILU)
+            place = c % HALF_CHUNKS * GROUP
+            rounded = h_bf[b, c // HALF_CHUNKS][:, place : place + GROUP].rearrange("p (j t) -> p j t", t=PACK)
+            if (b, c) == (1, ON_GPSIMD):
+                ub = up_product(wu_q[b], c, "y")
                 ub_f = held.tile([P, CHUNK, PACK], F32, name="ub_f", align_bytes=64)
-                nc.scalar.copy(ub_f[:], ub[:].rearrange("p t j -> p j t"))
+                nc.scalar.copy(ub_f[:], ub)
                 nc.gpsimd.tensor_tensor(rounded, ub_f[:], act, MULT)
             else:
-                nc.vector.tensor_tensor(rounded, ub[:].rearrange("p t j -> p j t"), act, MULT)
+                nc.vector.tensor_tensor(rounded, up_product(wu_q[b], c, "ub"), act, MULT)
 
-        def quantize_hidden(b, half, codes=None):
-            if codes is None:
-                codes = held.tile([P, HALF], U32, name=f"h_c{b}{half}", align_bytes=64)
+        def quantize_hidden(b, half, codes):
             scales = held.tile([P, HALF], U8, name=f"h_s{b}{half}", align_bytes=64)
             nc.vector.quantize_mx(out=codes[:].bitcast(FP8X4), scales=scales[:], in_=h_bf[b, half])
             h_q[b, half] = codes, scales
 
         acts = [held.tile([P, CHUNKS, CHUNK, PACK], F32, name="act0", tag="wu0_part0", align_bytes=64)]
-        for c in (0, 1, 2, 4, 5, 6, 7, 3):
+        for c in GROUP0_TURNS[:EARLY_CHUNKS]:
             hidden(0, c)
-            if c == 2:
-                wg1_bf = reused.tile([P, 2 * GROUP * PACK], BF16, name="wg1_bf", offset=LOW)
-                wg_q[1] = quantize_halves(wg1_parts, "wg1", on_gpsimd, on_scalar, wg1_bf[:, : GROUP * PACK], 1)
-                h_bf[0, 1] = reused.tile([P, HALF * PACK], BF16, name="h_bf01", offset=HIGH)[:]
+        wg1_bf = reused.tile([P, 2 * GROUP * PACK], BF16, name="wg1_bf", offset=LOW)
+        wg_q[1] = quantize_weight(
+            wg1_parts, "wg1", [("gpsimd", 0, HALF_M), ("scalar", HALF_M, P)], wg1_bf[:, : GROUP * PACK], 1
+        )
+        h_bf[0, 1] = reused.tile([P, HALF * PACK], BF16, name="h_bf01", offset=HIGH)[:]
+        for c in GROUP0_TURNS[EARLY_CHUNKS:]:
+            hidden(0, c)
         wu1_bf = reused.tile([P, GROUP * PACK], BF16, name="wu1_bf", offset=LOW)
-        wu_q[1] = quantize_halves(wu1_parts, "wu1", on_gpsimd, on_gpsimd, wu1_bf[:], 1)
-        acts.append(held.tile([P, CHUNKS, CHUNK, PACK], F32, name="act1", tag="act1", align_bytes=64))
-        quantize_hidden(0, 1)
+        wu1_shares = [("gpsimd", 0, HALF_M), ("gpsimd", HALF_M, WU1_SPLIT), ("scalar", WU1_SPLIT, P)]
+        wu_q[1] = quantize_weight(wu1_parts, "wu1", wu1_shares, wu1_bf[:], 1)
+        acts.append(held.tile([P, CHUNKS, CHUNK, PACK], F32, name="act1", align_bytes=64))
+        quantize_hidden(0, 1, held.tile([P, HALF], U32, name="h_c01", align_bytes=64))
         quantize_hidden(0, 0, reused.tile([P, HALF], U32, name="h_c00", offset=LOW))
 
-        h_bf[1, 1] = reused.tile([P, HALF * PACK], BF16, name="h_bf11", offset=NEXT + 4096)[:]
+        h_bf[1, 1] = reused.tile([P, HALF * PACK], BF16, name="h_bf11", offset=NEXT + ROUNDED_BYTES)[:]
         wd8_d = held.tile([P, N], U32, name="wd8_d", align_bytes=64)
         wd_sd = reused.tile([P, N], U8, name="wd_sd", offset=NEXT)[:]
         nc.gpsimd.tensor_copy(
@@ -218,8 +222,10 @@ def tile_list_gmlpt_silu_mix_gateP_kernel(
             wd_s[:].rearrange("p (a m t) -> p a t m", t=PACK, m=16),
         )
 
-        spans = [(0, 512), (512, 896), (896, 1024)]
-        y_f = [reused.tile([P, PACK, HALF], F32, name="y_f0", offset=0, align_bytes=64), held.tile([P, PACK, HALF], F32, name="y_f1")]
+        y_f = [
+            reused.tile([P, PACK, HALF], F32, name="y_f0", offset=0, align_bytes=64),
+            held.tile([P, PACK, HALF], F32, name="y_f1"),
+        ]
         out_f = [held.tile([P, PACK, HALF], F32, name="out_f0")[:]]
         out_bf = held.tile([P, J * PACK], BF16, name="out_bf", align_bytes=64)
         out_c = held.tile([P, J], U32, name="out_c", align_bytes=64)
@@ -229,11 +235,11 @@ def tile_list_gmlpt_silu_mix_gateP_kernel(
             half = j0 // HALF
             ms = slice(t * P, (t + 1) * P)
             cols = slice(j0 - half * HALF, j1 - half * HALF)
-            y = psum.tile([P, j1 - j0], F32, name="y", tag=bank, bufs=2 if bank == "y" else 3)
+            y = psum.tile([P, j1 - j0], F32, name="y", tag=bank, bufs=BANKS[bank])
             nc.tensor.matmul_mx(
                 out=y[:],
                 lhsT=wd8_d[:, ms].bitcast(FP8X4),
-                lhsT_scale=wd_sd[4:P, ms],
+                lhsT_scale=wd_sd[WD8_SCALES_AT:P, ms],
                 rhs=h_q[0, half][0][:, cols].bitcast(FP8X4),
                 rhs_scale=h_q[0, half][1][:, cols],
                 start=True,
@@ -250,48 +256,39 @@ def tile_list_gmlpt_silu_mix_gateP_kernel(
             )
             nc.scalar.copy(y_f[half][:, t, cols], y[:])
 
-        def gate_columns(s, t, j0, j1):
+        def gate_plane(s, t):
+            j0, j1 = SPANS[s]
             half = j0 // HALF
-            first = spans[s][0]
             nc.vector.tensor_tensor(
-                out_f[s][:, t, j0 - first : j1 - first],
+                out_f[s][:, t, :],
                 gate_rows[t][:].indirect(offsets[:, j0 // 16 : j1 // 16]),
                 y_f[half][:, t, j0 - half * HALF : j1 - half * HALF],
                 MULT,
             )
-
-        def gate_plane(s, t):
-            j0, j1 = spans[s]
-            gate_columns(s, t, j0, j1)
             if t % 2:
                 pair = slice(t - 1, t + 1)
                 nc.sync.dma_start(out_0.rearrange("(p t) j -> p t j", t=PACK)[:, pair, j0:j1], out_f[s][:, pair, :])
-                if s == 1:
+                if s == MIDDLE:
                     nc.scalar.copy(
                         out_bf[:, j0 * PACK : j1 * PACK].rearrange("p (j t) -> p j t", t=PACK)[:, :, pair],
                         out_f[s][:, pair, :].rearrange("p t j -> p j t"),
                     )
 
-        def finish_span(s):
-            j0, j1 = spans[s]
+        def round_span(s):
+            j0, j1 = SPANS[s]
             nc.scalar.copy(
                 out_bf[:, j0 * PACK : j1 * PACK].rearrange("p (a j t) -> p a t j", t=PACK, j=4),
                 out_f[s].rearrange("p t (a j) -> p a t j", j=4),
             )
 
-        def quantize_output(j0, j1):
-            nc.vector.quantize_mx(
-                out=out_c[:, j0:j1].bitcast(FP8X4), scales=out_s[:, j0:j1], in_=out_bf[:, j0 * PACK : j1 * PACK]
-            )
-
-        for c in (7, 0, 1, 2, 3, 4, 5, 6):
+        for c in GROUP1_TURNS:
             hidden(1, c)
-            if c == 4:
+            if c == HALF_CHUNKS:
                 nc.scalar.copy(
                     wd8_d[:].rearrange("p (t a m) -> p a t m", t=PACK, m=4),
                     wd8_w[:].bitcast(U32).rearrange("p (a m t) -> p a t m", t=PACK, m=4),
                 )
-                quantize_hidden(1, 0)
+                quantize_hidden(1, 0, held.tile([P, HALF], U32, name="h_c10", align_bytes=64))
                 down_product(0, 0, HALF // 2, "y")
                 down_product(0, HALF // 2, HALF, "y")
         for t in range(1, PACK):
@@ -299,23 +296,24 @@ def tile_list_gmlpt_silu_mix_gateP_kernel(
         gate_plane(0, 0)
         quantize_hidden(1, 1, reused.tile([P, HALF], U32, name="h_c11", offset=LOW))
         for t in range(PACK):
-            down_product(t, HALF, J, "ub" if t < 3 else "y")
+            down_product(t, HALF, J, "ub" if t < BANKS["ub"] else "y")
         for t in range(1, PACK):
             gate_plane(0, t)
-        finish_span(0)
-        for j0, j1 in spans[1:]:
+        round_span(0)
+        for j0, j1 in SPANS[1:]:
             late = reused.tile([P, PACK, j1 - j0], F32, name=f"out_f{j0}", offset=(j0 - HALF) * PACK * 4)
             out_f.append(late[:])
-        for s in range(1, len(spans)):
+        for s in range(1, len(SPANS)):
             for t in range(PACK):
                 gate_plane(s, t)
-            if s != 1:
-                finish_span(s)
-        for j0, j1 in spans:
-            quantize_output(j0, j1)
+        round_span(len(SPANS) - 1)
+        for j0, j1 in SPANS:
+            nc.vector.quantize_mx(
+                out=out_c[:, j0:j1].bitcast(FP8X4), scales=out_s[:, j0:j1], in_=out_bf[:, j0 * PACK : j1 * PACK]
+            )
             nc.sync.dma_start(
                 out_1[0].rearrange("p j i -> p (j i)").bitcast(I32)[:, j0:j1], out_c[:, j0:j1].bitcast(I32)
             )
-        for q in range(4):
-            queue = nc.scalar if q % 2 else nc.sync
-            queue.dma_start(out_2[0].bitcast(I32)[q:16:4, :], out_s[q:P:32, :].bitcast(I32))
+        for r in range(PACK):
+            queue = nc.scalar if r % 2 else nc.sync
+            queue.dma_start(out_2[0].bitcast(I32)[r:SCALE_ROWS:PACK, :], scale_rows(out_s, 0, r))

@@ -28,22 +28,27 @@ CHUNKS = J // CHUNK
 HALF = J // 2
 HALF_CHUNKS = CHUNKS // 2
 HALF_M = P // 2
-BANKS = {"ga": 3, "ub": 3, "y": 2}
+UP_BANKS = 3
+GATE_BANKS = 5
 
-FIRST_WORDS = 2 * CHUNK
-WU1_SPLIT = 96
-EARLY_CHUNKS = HALF_CHUNKS - 1
-GROUP0_TURNS = [*range(EARLY_CHUNKS), *range(HALF_CHUNKS, CHUNKS), EARLY_CHUNKS]
-AFTER_ROUNDING = HALF_CHUNKS + 1
+WORD_PIECES = [(0, CHUNK), (CHUNK, HALF), (HALF, J)]
+EARLY_SILUS = 6
+WU1_SPLIT = 80
 ON_GPSIMD = CHUNKS - 1
 GROUP1_TURNS = [ON_GPSIMD, *range(ON_GPSIMD)]
 SPANS = [(0, HALF), (HALF, J - CHUNK), (J - CHUNK, J)]
 MIDDLE = 1
 
-ROUNDED_BYTES = GROUP * PACK * 2
-LOW = PACK * HALF * 4
-HIGH = LOW + ROUNDED_BYTES
-NEXT = HIGH + ROUNDED_BYTES
+ROUNDED = GROUP * PACK * 2
+CODES = HALF * 4
+AT_WU1_BF = PACK * HALF * 4
+AT_WG1_BF = AT_WU1_BF + ROUNDED // 2
+AT_H01 = AT_WU1_BF + ROUNDED
+AT_H11 = AT_H01 + N
+AT_WU1 = AT_H11 + ROUNDED
+AT_WU1_SCALAR = AT_WU1 + WU1_SPLIT * PACK * PACK * 4
+AT_H_CODES = [AT_WU1, AT_WU1_SCALAR - CODES // 2]
+AT_ACT1 = AT_WU1_SCALAR + CODES // 2
 
 
 def tile_list_gmlpt_silu_mix_gateP_kernel(
@@ -58,13 +63,15 @@ def tile_list_gmlpt_silu_mix_gateP_kernel(
         offsets = held.tile([P, J // 16], U16, name="offsets")
         nc.sync.dma_start(offsets[:], offs)
 
-        def load_half(w, k, name, pieces):
-            part = held.tile([P, PACK, GROUP // 2], F32, name=name, tag=name, align_bytes=64)
-            rows = w.rearrange("(p i) r -> p i r", i=PACK)[:, :, k * GROUP // 2 : (k + 1) * GROUP // 2]
+        def load_weight(part, w, c0, pieces):
+            rows = w.rearrange("(p i) r -> p i r", i=PACK)[:, :, c0 : c0 + part.shape[2]]
             for u in range(pieces):
                 some = slice(u * PACK // pieces, (u + 1) * PACK // pieces)
                 nc.sync.dma_start(part[:, some], rows[:, some])
             return part
+
+        def half_tile(name):
+            return held.tile([P, PACK, GROUP // 2], F32, name=name, align_bytes=64)
 
         def scale_rows(tile, first, r):
             return tile[first + r : P : QUADRANT, :].bitcast(I32)
@@ -73,7 +80,7 @@ def tile_list_gmlpt_silu_mix_gateP_kernel(
             for r in range(PACK):
                 nc.sync.dma_start(scale_rows(tile, first, r), scales[0].bitcast(I32)[r:SCALE_ROWS:PACK, :])
 
-        wg0_parts = [load_half(wg, 0, "wg0_part0", 2)]
+        wg0_parts = [load_weight(half_tile("wg0_low"), wg, 0, 2)]
 
         tab_s = held.tile([P, T], U8, name="tab_s", align_bytes=64)
         nc.gpsimd.memset(tab_s[:].bitcast(I32), 0)
@@ -82,24 +89,32 @@ def tile_list_gmlpt_silu_mix_gateP_kernel(
         wd_s = held.tile([P, N], U8, name="wd_s", align_bytes=64)
         nc.gpsimd.memset(wd_s[:].bitcast(I32), 0)
 
-        wg0_parts.append(load_half(wg, 1, "wg0_part1", 1))
+        wg0_parts.append(load_weight(half_tile("wg0_high"), wg, GROUP // 2, 1))
         tab_w = held.tile([P, T], I32, name="tab_w", align_bytes=64)
         nc.sync.dma_start(tab_w[:], tab_words[0].rearrange("p t i -> p (t i)").bitcast(I32))
-        wu0_parts = [load_half(wu, k, f"wu0_part{k}", 1) for k in range(2)]
-        wd4_w = reused.tile([P, 2 * N], U8, name="wd4_w", offset=LOW)
+        wu0_parts = [load_weight(half_tile(f"wu0_{k}"), wu, k * GROUP // 2, 1) for k in range(2)]
+        wd4_w = reused.tile([P, 2 * N], U8, name="wd4_w", offset=AT_WG1_BF)
         nc.sync.dma_start(wd4_w[:].bitcast(I32), wd4_words[0].bitcast(I32))
-        wg1_parts = [load_half(wg, 2 + k, f"wg1_part{k}", 1) for k in range(2)]
-        wu1_parts = [load_half(wu, 2 + k, f"wu1_part{k}", 1) for k in range(2)]
+        wg1 = held.tile([P, PACK, GROUP], F32, name="wg1", tag="wg1", align_bytes=64)
+        load_weight(wg1, wg, GROUP, 1)
+        wu1_gpsimd = reused.tile([P, PACK, WU1_SPLIT * PACK], F32, name="wu1_gpsimd", offset=AT_WU1)
+        load_weight(wu1_gpsimd, wu, GROUP, 1)
+        wu1_scalar = reused.tile([P, PACK, GROUP - WU1_SPLIT * PACK], F32, name="wu1_scalar", offset=AT_WU1_SCALAR)
+        load_weight(wu1_scalar, wu, GROUP + WU1_SPLIT * PACK, 1)
         load_scale_rows(wd_s, 0, wd4_scales)
         wd8_w = held.tile([P, N], I32, name="wd8_w", align_bytes=64)
         nc.sync.dma_start(wd8_w[:], wd8_words[0].rearrange("p n i -> p (n i)").bitcast(I32))
         gate_rows = []
         for t in range(PACK):
             rows = held.tile([P, T], F32, name=f"gate_rows{t}")
-            nc.sync.dma_start(rows[:], gT.rearrange("(p t) c -> p t c", t=PACK)[:, t, :])
-            gate_rows.append(rows)
+            plane = gT.rearrange("(p t) c -> p t c", t=PACK)[:, t, :]
             if t == 0:
+                nc.sync.dma_start(rows[:, : T // 2], plane[:, : T // 2])
                 load_scale_rows(wd_s, WD8_SCALES_AT, wd8_scales)
+                nc.sync.dma_start(rows[:, T // 2 :], plane[:, T // 2 :])
+            else:
+                nc.sync.dma_start(rows[:], plane)
+            gate_rows.append(rows)
 
         warm = held.tile([P, 1], F32, name="warm")
         nc.vector.memset(warm[:], 0.0)
@@ -109,17 +124,8 @@ def tile_list_gmlpt_silu_mix_gateP_kernel(
         v_s = held.tile([P, J], U8, name="v_s", align_bytes=64)
         nc.vector.tensor_copy(v_s[:], tab_s[:].indirect(offsets[:]))
 
-        v_w = {}
-
-        def gather_words(j0, j1):
-            words = held.tile([P, j1 - j0], U32, name=f"v_w{j0}", align_bytes=64)
-            nc.vector.tensor_copy(words[:], tab_w[:].bitcast(U32).indirect(offsets[:, j0 // 16 : j1 // 16]))
-            for j in range(j0, j1, CHUNK):
-                v_w[j // CHUNK] = words[:, j - j0 : j - j0 + CHUNK]
-
-        def round_places(engine, parts, rounded, m0, m1):
-            part = parts[m0 // HALF_M][:]
-            ms = slice(m0 % HALF_M, m0 % HALF_M + m1 - m0)
+        def round_places(engine, part, m_part, rounded, m0, m1):
+            ms = slice(m0 - m_part, m1 - m_part)
             if engine == "gpsimd":
                 dealt = rounded.rearrange("p (t m i) -> p m t i", t=PACK, i=PACK)[:, m0:m1]
                 nc.gpsimd.tensor_scalar(dealt, part.rearrange("p i (m t) -> p m t i", t=PACK)[:, ms], 1.0, 0.0, MULT, ADD)
@@ -128,9 +134,7 @@ def tile_list_gmlpt_silu_mix_gateP_kernel(
                 copy = nc.scalar.copy if engine == "scalar" else nc.vector.tensor_copy
                 copy(dealt, part.rearrange("p (u e) (m t) -> p m u t e", e=2, t=PACK)[:, ms])
 
-        def quantize_weight(parts, name, shares, rounded, calls):
-            for engine, m0, m1 in shares:
-                round_places(engine, parts, rounded, m0, m1)
+        def quantize_weight(name, rounded, calls):
             planes = PACK // calls
             quantised = []
             for u in range(calls):
@@ -143,25 +147,19 @@ def tile_list_gmlpt_silu_mix_gateP_kernel(
 
         wg_q, wu_q = {}, {}
         wg0_bf = held.tile([P, GROUP * PACK], BF16, name="wg0_bf", align_bytes=64)
-        wg_q[0] = quantize_weight(wg0_parts, "wg0", [("scalar", 0, HALF_M), ("scalar", HALF_M, P)], wg0_bf[:], 2)
-        gather_words(0, FIRST_WORDS)
-        gather_words(FIRST_WORDS, J)
-        wu0_bf = held.tile([P, GROUP * PACK], BF16, name="wu0_bf", tag="wu0_bf", align_bytes=64)
-        wu_q[0] = quantize_weight(wu0_parts, "wu0", [("scalar", 0, HALF_M), ("vector", HALF_M, P)], wu0_bf[:], 2)
+        for k in range(2):
+            round_places("scalar", wg0_parts[k][:], k * HALF_M, wg0_bf[:], k * HALF_M, (k + 1) * HALF_M)
+        wg_q[0] = quantize_weight("wg0", wg0_bf[:], 1)
 
-        wd4_d = held.tile([P, 2 * N], U8, name="wd4_d", tag="wu0_bf", align_bytes=64)
-        nc.vector.tensor_copy(
-            wd4_d[:].bitcast(U16).rearrange("p (t a m) -> p a t m", t=PACK, m=8),
-            wd4_w[:].bitcast(U16).rearrange("p (a m t) -> p a t m", t=PACK, m=8),
-        )
+        v_w = {}
+        for j0, j1 in WORD_PIECES:
+            words = held.tile([P, j1 - j0], U32, name=f"v_w{j0}", align_bytes=64)
+            nc.vector.tensor_copy(words[:], tab_w[:].bitcast(U32).indirect(offsets[:, j0 // 16 : j1 // 16]))
+            for j in range(j0, j1, CHUNK):
+                v_w[j // CHUNK] = words[:, j - j0 : j - j0 + CHUNK]
 
-        h_bf10 = held.tile([P, HALF * PACK], BF16, name="h_bf10", align_bytes=64)
-        h_bf00 = reused.tile([P, J * PACK], BF16, name="h_bf00", offset=NEXT)
-        h_bf = {(0, 0): h_bf00[:, : HALF * PACK], (1, 0): h_bf10[:]}
-        h_q = {}
-
-        def up_product(wq, c, bank):
-            acc = psum.tile([P, PACK, CHUNK], F32, name=bank, tag=bank, bufs=BANKS[bank])
+        def up_sums(wq, c, bank):
+            acc = psum.tile([P, PACK, CHUNK], F32, name="acc", tag=f"bank{bank}")
             for t in range(PACK):
                 codes, scales = wq[t]
                 nc.tensor.matmul_mx(
@@ -175,48 +173,72 @@ def tile_list_gmlpt_silu_mix_gateP_kernel(
                 )
             return acc[:].rearrange("p t j -> p j t")
 
-        def hidden(b, c):
-            ga = up_product(wg_q[b], c, "ga")
-            if (b, c) == (0, AFTER_ROUNDING):
-                act = held.tile([P, CHUNK, PACK], F32, name="act_apart", tag="wg1_part1", align_bytes=64)[:]
-            else:
-                act = acts[b][:, c]
-            nc.scalar.activation(act, ga, SILU)
+        acts = {}
+
+        def gate_bank(turn):
+            return UP_BANKS + turn % GATE_BANKS
+
+        def gate_silu(b, c, act, bank):
+            acts[b, c] = act
+            nc.scalar.activation(act, up_sums(wg_q[b], c, bank), SILU)
+
+        act_early = held.tile([P, EARLY_SILUS, CHUNK, PACK], F32, name="act_early", align_bytes=64)
+        for c in range(EARLY_SILUS):
+            gate_silu(0, c, act_early[:, c], gate_bank(c))
+
+        wu0_bf = held.tile([P, GROUP * PACK], BF16, name="wu0_bf", tag="wu0_bf", align_bytes=64)
+        for k in range(2):
+            round_places("vector", wu0_parts[k][:], k * HALF_M, wu0_bf[:], k * HALF_M, (k + 1) * HALF_M)
+        wu_q[0] = quantize_weight("wu0", wu0_bf[:], 2)
+
+        wd4_d = held.tile([P, 2 * N], U8, name="wd4_d", tag="wu0_bf", align_bytes=64)
+        nc.vector.tensor_copy(
+            wd4_d[:].bitcast(U16).rearrange("p (t a m) -> p a t m", t=PACK, m=8),
+            wd4_w[:].bitcast(U16).rearrange("p (a m t) -> p a t m", t=PACK, m=8),
+        )
+
+        h_bf00 = held.tile([P, HALF * PACK], BF16, name="h_bf00", align_bytes=64)
+        h_bf10 = held.tile([P, HALF * PACK], BF16, name="h_bf10", align_bytes=64)
+        h_bf = {(0, 0): h_bf00, (1, 0): h_bf10}
+        h_q = {}
+
+        def hidden(b, c, bank):
             place = c % HALF_CHUNKS * GROUP
             rounded = h_bf[b, c // HALF_CHUNKS][:, place : place + GROUP].rearrange("p (j t) -> p j t", t=PACK)
             if (b, c) == (1, ON_GPSIMD):
-                ub = up_product(wu_q[b], c, "y")
                 ub_f = held.tile([P, CHUNK, PACK], F32, name="ub_f", align_bytes=64)
-                nc.scalar.copy(ub_f[:], ub)
-                nc.gpsimd.tensor_tensor(rounded, ub_f[:], act, MULT)
+                nc.scalar.copy(ub_f[:], up_sums(wu_q[b], c, bank))
+                nc.gpsimd.tensor_tensor(rounded, ub_f[:], acts[b, c], MULT)
             else:
-                nc.vector.tensor_tensor(rounded, up_product(wu_q[b], c, "ub"), act, MULT)
+                nc.vector.tensor_tensor(rounded, up_sums(wu_q[b], c, bank), acts[b, c], MULT)
 
         def quantize_hidden(b, half, codes):
             scales = held.tile([P, HALF], U8, name=f"h_s{b}{half}", align_bytes=64)
-            nc.vector.quantize_mx(out=codes[:].bitcast(FP8X4), scales=scales[:], in_=h_bf[b, half])
+            nc.vector.quantize_mx(out=codes[:].bitcast(FP8X4), scales=scales[:], in_=h_bf[b, half][:])
             h_q[b, half] = codes, scales
 
-        acts = [held.tile([P, CHUNKS, CHUNK, PACK], F32, name="act0", tag="wu0_part0", align_bytes=64)]
-        for c in GROUP0_TURNS[:EARLY_CHUNKS]:
-            hidden(0, c)
-        wg1_bf = reused.tile([P, 2 * GROUP * PACK], BF16, name="wg1_bf", offset=LOW)
-        wg_q[1] = quantize_weight(
-            wg1_parts, "wg1", [("gpsimd", 0, HALF_M), ("scalar", HALF_M, P)], wg1_bf[:, : GROUP * PACK], 1
-        )
-        h_bf[0, 1] = reused.tile([P, HALF * PACK], BF16, name="h_bf01", offset=HIGH)[:]
-        for c in GROUP0_TURNS[EARLY_CHUNKS:]:
-            hidden(0, c)
-        wu1_bf = reused.tile([P, GROUP * PACK], BF16, name="wu1_bf", offset=LOW)
-        wu1_shares = [("gpsimd", 0, HALF_M), ("gpsimd", HALF_M, WU1_SPLIT), ("scalar", WU1_SPLIT, P)]
-        wu_q[1] = quantize_weight(wu1_parts, "wu1", wu1_shares, wu1_bf[:], 1)
-        acts.append(held.tile([P, CHUNKS, CHUNK, PACK], F32, name="act1", align_bytes=64))
-        quantize_hidden(0, 1, held.tile([P, HALF], U32, name="h_c01", align_bytes=64))
-        quantize_hidden(0, 0, reused.tile([P, HALF], U32, name="h_c00", offset=LOW))
+        wg1_bf = reused.tile([P, GROUP * PACK], BF16, name="wg1_bf", offset=AT_WG1_BF)
+        round_places("gpsimd", wg1[:], 0, wg1_bf[:], 0, HALF_M)
+        round_places("scalar", wg1[:], 0, wg1_bf[:], HALF_M, P)
+        for c in range(HALF_CHUNKS):
+            hidden(0, c, c % UP_BANKS)
+        act_late = held.tile([P, CHUNKS - EARLY_SILUS, CHUNK, PACK], F32, name="act_late", tag="wg1", align_bytes=64)
+        for c in range(EARLY_SILUS, CHUNKS):
+            gate_silu(0, c, act_late[:, c - EARLY_SILUS], gate_bank(c))
+        wg_q[1] = quantize_weight("wg1", wg1_bf[:], 1)
+        wu1_bf = reused.tile([P, GROUP * PACK], BF16, name="wu1_bf", offset=AT_WU1_BF)
+        round_places("gpsimd", wu1_gpsimd[:], 0, wu1_bf[:], 0, WU1_SPLIT)
+        round_places("scalar", wu1_scalar[:], WU1_SPLIT, wu1_bf[:], WU1_SPLIT, P)
+        h_bf[0, 1] = reused.tile([P, HALF * PACK], BF16, name="h_bf01", offset=AT_H01)
+        for c in range(HALF_CHUNKS, CHUNKS):
+            hidden(0, c, c % UP_BANKS)
+        wu_q[1] = quantize_weight("wu1", wu1_bf[:], 1)
+        for half in range(2):
+            quantize_hidden(0, half, reused.tile([P, HALF], U32, name=f"h_c0{half}", offset=AT_H_CODES[half]))
 
-        h_bf[1, 1] = reused.tile([P, HALF * PACK], BF16, name="h_bf11", offset=NEXT + ROUNDED_BYTES)[:]
+        h_bf[1, 1] = reused.tile([P, HALF * PACK], BF16, name="h_bf11", offset=AT_H11)
         wd8_d = held.tile([P, N], U32, name="wd8_d", align_bytes=64)
-        wd_sd = reused.tile([P, N], U8, name="wd_sd", offset=NEXT)[:]
+        wd_sd = reused.tile([P, N], U8, name="wd_sd", offset=AT_H01)[:]
         nc.gpsimd.tensor_copy(
             wd_sd.rearrange("p (t a m) -> p a t m", t=PACK, m=16),
             wd_s[:].rearrange("p (a m t) -> p a t m", t=PACK, m=16),
@@ -235,7 +257,7 @@ def tile_list_gmlpt_silu_mix_gateP_kernel(
             half = j0 // HALF
             ms = slice(t * P, (t + 1) * P)
             cols = slice(j0 - half * HALF, j1 - half * HALF)
-            y = psum.tile([P, j1 - j0], F32, name="y", tag=bank, bufs=BANKS[bank])
+            y = psum.tile([P, j1 - j0], F32, name="y", tag=f"bank{bank}")
             nc.tensor.matmul_mx(
                 out=y[:],
                 lhsT=wd8_d[:, ms].bitcast(FP8X4),
@@ -281,22 +303,34 @@ def tile_list_gmlpt_silu_mix_gateP_kernel(
                 out_f[s].rearrange("p t (a j) -> p a t j", j=4),
             )
 
-        for c in GROUP1_TURNS:
-            hidden(1, c)
-            if c == HALF_CHUNKS:
+        act1 = reused.tile([P, CHUNKS, CHUNK, PACK], F32, name="act1", offset=AT_ACT1)
+        gate1 = [gate_bank(CHUNKS + turn) for turn in range(GATE_BANKS)]
+        up1 = [gate1[0], *((CHUNKS + c) % UP_BANKS for c in range(UP_BANKS)), *gate1[1:3]]
+        up1 += up1[3:5]
+        gate1 += up1[: CHUNKS - GATE_BANKS]
+        y_banks = [*gate1[3:5], up1[5], *gate1[GATE_BANKS:], *up1[6:], gate1[3]]
+        for turn in range(GATE_BANKS):
+            gate_silu(1, GROUP1_TURNS[turn], act1[:, turn], gate1[turn])
+        for turn, c in enumerate(GROUP1_TURNS):
+            hidden(1, c, up1[turn])
+            if c == ON_GPSIMD:
                 nc.scalar.copy(
                     wd8_d[:].rearrange("p (t a m) -> p a t m", t=PACK, m=4),
                     wd8_w[:].bitcast(U32).rearrange("p (a m t) -> p a t m", t=PACK, m=4),
                 )
+            late = turn + GATE_BANKS
+            if late < CHUNKS:
+                gate_silu(1, GROUP1_TURNS[late], act1[:, late], gate1[late])
+            if c == HALF_CHUNKS:
                 quantize_hidden(1, 0, held.tile([P, HALF], U32, name="h_c10", align_bytes=64))
-                down_product(0, 0, HALF // 2, "y")
-                down_product(0, HALF // 2, HALF, "y")
+                down_product(0, 0, HALF // 2, y_banks[0])
+                down_product(0, HALF // 2, HALF, y_banks[1])
         for t in range(1, PACK):
-            down_product(t, 0, HALF, "ga")
+            down_product(t, 0, HALF, y_banks[1 + t])
         gate_plane(0, 0)
-        quantize_hidden(1, 1, reused.tile([P, HALF], U32, name="h_c11", offset=LOW))
+        quantize_hidden(1, 1, reused.tile([P, HALF], U32, name="h_c11", offset=AT_H_CODES[0]))
         for t in range(PACK):
-            down_product(t, HALF, J, "ub" if t < BANKS["ub"] else "y")
+            down_product(t, HALF, J, y_banks[1 + PACK + t])
         for t in range(1, PACK):
             gate_plane(0, t)
         round_span(0)

@@ -28,14 +28,52 @@ CHUNKS = J // CHUNK
 HALF = J // 2
 HALF_CHUNKS = CHUNKS // 2
 HALF_M = P // 2
-UP_BANKS = 3
-GATE_BANKS = 5
 
-WORD_PIECES = [(0, CHUNK), (CHUNK, HALF), (HALF, J)]
+WORD_PIECES = [(0, CHUNK), (CHUNK, 3 * CHUNK), (3 * CHUNK, J)]
+WU0_SPLIT = 48
 EARLY_SILUS = 6
 WU1_SPLIT = 80
 ON_GPSIMD = CHUNKS - 1
-GROUP1_TURNS = [ON_GPSIMD, *range(ON_GPSIMD)]
+GROUP1_TURNS = [0, ON_GPSIMD, *range(1, ON_GPSIMD)]
+
+
+def psum_banks():
+    follows = {
+        ("gate", 0, 5): ("gate", 0, 0),
+        ("gate", 0, 6): ("up", 0, 0),
+        ("gate", 0, 7): ("up", 0, 1),
+        **{("up", 0, c): ("gate", 0, c - 2) for c in range(3, 7)},
+        ("up", 0, 7): ("up", 0, 2),
+        ("gate", 1, 0): ("gate", 0, 5),
+        ("gate", 1, ON_GPSIMD): ("up", 0, 3),
+        ("gate", 1, 1): ("gate", 0, 6),
+        ("gate", 1, 2): ("gate", 0, 7),
+        ("gate", 1, 3): ("gate", 1, 0),
+        ("gate", 1, 4): ("gate", 1, ON_GPSIMD),
+        ("gate", 1, 5): ("up", 1, 0),
+        ("gate", 1, 6): ("up", 1, ON_GPSIMD),
+        ("up", 1, 0): ("up", 0, 4),
+        ("up", 1, ON_GPSIMD): ("up", 0, 5),
+        ("up", 1, 1): ("up", 0, 6),
+        ("up", 1, 2): ("up", 0, 7),
+        ("up", 1, 3): ("gate", 1, 1),
+        ("up", 1, 4): ("gate", 1, 2),
+        ("up", 1, 5): ("up", 1, 2),
+        ("up", 1, 6): ("up", 1, 3),
+    }
+    fresh = [("gate", 0, c) for c in range(5)] + [("up", 0, c) for c in range(3)]
+    banks = {sums: bank for bank, sums in enumerate(fresh)}
+    while len(banks) < 4 * CHUNKS:
+        for sums, before in follows.items():
+            if before in banks:
+                banks[sums] = banks[before]
+    return banks
+
+
+BANK = psum_banks()
+LAST_SUMS = [("up", 1, 1), ("gate", 1, 3), ("gate", 1, 4), ("up", 1, 4), ("gate", 1, 5), ("gate", 1, 6)]
+Y_BANKS = [BANK[sums] for sums in LAST_SUMS + [("up", 1, 5), ("up", 1, 6), ("up", 1, 1)]]
+
 SPANS = [(0, HALF), (HALF, J - CHUNK), (J - CHUNK, J)]
 MIDDLE = 1
 
@@ -47,8 +85,10 @@ AT_H01 = AT_WU1_BF + ROUNDED
 AT_H11 = AT_H01 + N
 AT_WU1 = AT_H11 + ROUNDED
 AT_WU1_SCALAR = AT_WU1 + WU1_SPLIT * PACK * PACK * 4
-AT_H_CODES = [AT_WU1, AT_WU1_SCALAR - CODES // 2]
-AT_ACT1 = AT_WU1_SCALAR + CODES // 2
+ALIGN = 64
+AT_H_CODES = [AT_WU1, AT_WU1_SCALAR + ALIGN - CODES]
+AT_ACT_FIRST = AT_WU1_SCALAR + ALIGN
+AT_ACT_REST = AT_ACT_FIRST + GROUP * 4
 
 
 def tile_list_gmlpt_silu_mix_gateP_kernel(
@@ -92,28 +132,26 @@ def tile_list_gmlpt_silu_mix_gateP_kernel(
         wg0_parts.append(load_weight(half_tile("wg0_high"), wg, GROUP // 2, 1))
         tab_w = held.tile([P, T], I32, name="tab_w", align_bytes=64)
         nc.sync.dma_start(tab_w[:], tab_words[0].rearrange("p t i -> p (t i)").bitcast(I32))
-        wu0_parts = [load_weight(half_tile(f"wu0_{k}"), wu, k * GROUP // 2, 1) for k in range(2)]
+        wu0_gpsimd = held.tile([P, PACK, WU0_SPLIT * PACK], F32, name="wu0_gpsimd", align_bytes=64)
+        load_weight(wu0_gpsimd, wu, 0, 1)
+        wu0_vector = held.tile([P, PACK, GROUP - WU0_SPLIT * PACK], F32, name="wu0_vector", align_bytes=64)
+        load_weight(wu0_vector, wu, WU0_SPLIT * PACK, 1)
         wd4_w = reused.tile([P, 2 * N], U8, name="wd4_w", offset=AT_WG1_BF)
         nc.sync.dma_start(wd4_w[:].bitcast(I32), wd4_words[0].bitcast(I32))
         wg1 = held.tile([P, PACK, GROUP], F32, name="wg1", tag="wg1", align_bytes=64)
         load_weight(wg1, wg, GROUP, 1)
+        load_scale_rows(wd_s, 0, wd4_scales)
         wu1_gpsimd = reused.tile([P, PACK, WU1_SPLIT * PACK], F32, name="wu1_gpsimd", offset=AT_WU1)
         load_weight(wu1_gpsimd, wu, GROUP, 1)
         wu1_scalar = reused.tile([P, PACK, GROUP - WU1_SPLIT * PACK], F32, name="wu1_scalar", offset=AT_WU1_SCALAR)
         load_weight(wu1_scalar, wu, GROUP + WU1_SPLIT * PACK, 1)
-        load_scale_rows(wd_s, 0, wd4_scales)
+        load_scale_rows(wd_s, WD8_SCALES_AT, wd8_scales)
         wd8_w = held.tile([P, N], I32, name="wd8_w", align_bytes=64)
         nc.sync.dma_start(wd8_w[:], wd8_words[0].rearrange("p n i -> p (n i)").bitcast(I32))
         gate_rows = []
         for t in range(PACK):
             rows = held.tile([P, T], F32, name=f"gate_rows{t}")
-            plane = gT.rearrange("(p t) c -> p t c", t=PACK)[:, t, :]
-            if t == 0:
-                nc.sync.dma_start(rows[:, : T // 2], plane[:, : T // 2])
-                load_scale_rows(wd_s, WD8_SCALES_AT, wd8_scales)
-                nc.sync.dma_start(rows[:, T // 2 :], plane[:, T // 2 :])
-            else:
-                nc.sync.dma_start(rows[:], plane)
+            nc.sync.dma_start(rows[:], gT.rearrange("(p t) c -> p t c", t=PACK)[:, t, :])
             gate_rows.append(rows)
 
         warm = held.tile([P, 1], F32, name="warm")
@@ -175,20 +213,17 @@ def tile_list_gmlpt_silu_mix_gateP_kernel(
 
         acts = {}
 
-        def gate_bank(turn):
-            return UP_BANKS + turn % GATE_BANKS
-
-        def gate_silu(b, c, act, bank):
+        def gate_silu(b, c, act):
             acts[b, c] = act
-            nc.scalar.activation(act, up_sums(wg_q[b], c, bank), SILU)
+            nc.scalar.activation(act, up_sums(wg_q[b], c, BANK["gate", b, c]), SILU)
 
         act_early = held.tile([P, EARLY_SILUS, CHUNK, PACK], F32, name="act_early", align_bytes=64)
         for c in range(EARLY_SILUS):
-            gate_silu(0, c, act_early[:, c], gate_bank(c))
+            gate_silu(0, c, act_early[:, c])
 
         wu0_bf = held.tile([P, GROUP * PACK], BF16, name="wu0_bf", tag="wu0_bf", align_bytes=64)
-        for k in range(2):
-            round_places("vector", wu0_parts[k][:], k * HALF_M, wu0_bf[:], k * HALF_M, (k + 1) * HALF_M)
+        round_places("gpsimd", wu0_gpsimd[:], 0, wu0_bf[:], 0, WU0_SPLIT)
+        round_places("vector", wu0_vector[:], WU0_SPLIT, wu0_bf[:], WU0_SPLIT, P)
         wu_q[0] = quantize_weight("wu0", wu0_bf[:], 2)
 
         wd4_d = held.tile([P, 2 * N], U8, name="wd4_d", tag="wu0_bf", align_bytes=64)
@@ -202,7 +237,8 @@ def tile_list_gmlpt_silu_mix_gateP_kernel(
         h_bf = {(0, 0): h_bf00, (1, 0): h_bf10}
         h_q = {}
 
-        def hidden(b, c, bank):
+        def hidden(b, c):
+            bank = BANK["up", b, c]
             place = c % HALF_CHUNKS * GROUP
             rounded = h_bf[b, c // HALF_CHUNKS][:, place : place + GROUP].rearrange("p (j t) -> p j t", t=PACK)
             if (b, c) == (1, ON_GPSIMD):
@@ -221,23 +257,22 @@ def tile_list_gmlpt_silu_mix_gateP_kernel(
         round_places("gpsimd", wg1[:], 0, wg1_bf[:], 0, HALF_M)
         round_places("scalar", wg1[:], 0, wg1_bf[:], HALF_M, P)
         for c in range(HALF_CHUNKS):
-            hidden(0, c, c % UP_BANKS)
+            hidden(0, c)
         act_late = held.tile([P, CHUNKS - EARLY_SILUS, CHUNK, PACK], F32, name="act_late", tag="wg1", align_bytes=64)
         for c in range(EARLY_SILUS, CHUNKS):
-            gate_silu(0, c, act_late[:, c - EARLY_SILUS], gate_bank(c))
+            gate_silu(0, c, act_late[:, c - EARLY_SILUS])
         wg_q[1] = quantize_weight("wg1", wg1_bf[:], 1)
         wu1_bf = reused.tile([P, GROUP * PACK], BF16, name="wu1_bf", offset=AT_WU1_BF)
         round_places("gpsimd", wu1_gpsimd[:], 0, wu1_bf[:], 0, WU1_SPLIT)
         round_places("scalar", wu1_scalar[:], WU1_SPLIT, wu1_bf[:], WU1_SPLIT, P)
         h_bf[0, 1] = reused.tile([P, HALF * PACK], BF16, name="h_bf01", offset=AT_H01)
         for c in range(HALF_CHUNKS, CHUNKS):
-            hidden(0, c, c % UP_BANKS)
+            hidden(0, c)
         wu_q[1] = quantize_weight("wu1", wu1_bf[:], 1)
         for half in range(2):
             quantize_hidden(0, half, reused.tile([P, HALF], U32, name=f"h_c0{half}", offset=AT_H_CODES[half]))
 
         h_bf[1, 1] = reused.tile([P, HALF * PACK], BF16, name="h_bf11", offset=AT_H11)
-        wd8_d = held.tile([P, N], U32, name="wd8_d", align_bytes=64)
         wd_sd = reused.tile([P, N], U8, name="wd_sd", offset=AT_H01)[:]
         nc.gpsimd.tensor_copy(
             wd_sd.rearrange("p (t a m) -> p a t m", t=PACK, m=16),
@@ -303,34 +338,31 @@ def tile_list_gmlpt_silu_mix_gateP_kernel(
                 out_f[s].rearrange("p t (a j) -> p a t j", j=4),
             )
 
-        act1 = reused.tile([P, CHUNKS, CHUNK, PACK], F32, name="act1", offset=AT_ACT1)
-        gate1 = [gate_bank(CHUNKS + turn) for turn in range(GATE_BANKS)]
-        up1 = [gate1[0], *((CHUNKS + c) % UP_BANKS for c in range(UP_BANKS)), *gate1[1:3]]
-        up1 += up1[3:5]
-        gate1 += up1[: CHUNKS - GATE_BANKS]
-        y_banks = [*gate1[3:5], up1[5], *gate1[GATE_BANKS:], *up1[6:], gate1[3]]
-        for turn in range(GATE_BANKS):
-            gate_silu(1, GROUP1_TURNS[turn], act1[:, turn], gate1[turn])
-        for turn, c in enumerate(GROUP1_TURNS):
-            hidden(1, c, up1[turn])
+        act_first = reused.tile([P, CHUNK, PACK], F32, name="act_first", offset=AT_ACT_FIRST)
+        act_rest = reused.tile([P, CHUNKS - 1, CHUNK, PACK], F32, name="act_rest", offset=AT_ACT_REST)
+        act1 = [act_first[:], *(act_rest[:, turn] for turn in range(CHUNKS - 1))]
+        for turn in range(EARLY_SILUS):
+            gate_silu(1, GROUP1_TURNS[turn], act1[turn])
+        for c in GROUP1_TURNS:
+            hidden(1, c)
             if c == ON_GPSIMD:
+                wd8_d = reused.tile([P, N], U32, name="wd8_d", offset=AT_ACT_FIRST)
                 nc.scalar.copy(
                     wd8_d[:].rearrange("p (t a m) -> p a t m", t=PACK, m=4),
                     wd8_w[:].bitcast(U32).rearrange("p (a m t) -> p a t m", t=PACK, m=4),
                 )
-            late = turn + GATE_BANKS
-            if late < CHUNKS:
-                gate_silu(1, GROUP1_TURNS[late], act1[:, late], gate1[late])
+                for late in range(EARLY_SILUS, CHUNKS):
+                    gate_silu(1, GROUP1_TURNS[late], act1[late])
             if c == HALF_CHUNKS:
                 quantize_hidden(1, 0, held.tile([P, HALF], U32, name="h_c10", align_bytes=64))
-                down_product(0, 0, HALF // 2, y_banks[0])
-                down_product(0, HALF // 2, HALF, y_banks[1])
+                down_product(0, 0, HALF // 2, Y_BANKS[0])
+                down_product(0, HALF // 2, HALF, Y_BANKS[1])
         for t in range(1, PACK):
-            down_product(t, 0, HALF, y_banks[1 + t])
+            down_product(t, 0, HALF, Y_BANKS[1 + t])
         gate_plane(0, 0)
         quantize_hidden(1, 1, reused.tile([P, HALF], U32, name="h_c11", offset=AT_H_CODES[0]))
         for t in range(PACK):
-            down_product(t, HALF, J, y_banks[1 + PACK + t])
+            down_product(t, HALF, J, Y_BANKS[1 + PACK + t])
         for t in range(1, PACK):
             gate_plane(0, t)
         round_span(0)

@@ -31,7 +31,8 @@ HALF_M = P // 2
 
 WORD_PIECES = [(0, CHUNK), (CHUNK, 3 * CHUNK), (3 * CHUNK, J)]
 WU0_SPLIT = 48
-EARLY_SILUS = 6
+EARLY_SILUS = 5
+AHEAD_OF_COPY = 5
 WU1_SPLIT = 80
 ON_GPSIMD = CHUNKS - 1
 GROUP1_TURNS = [0, ON_GPSIMD, *range(1, ON_GPSIMD)]
@@ -39,25 +40,20 @@ GROUP1_TURNS = [0, ON_GPSIMD, *range(1, ON_GPSIMD)]
 
 def psum_banks():
     follows = {
-        ("gate", 0, 5): ("gate", 0, 0),
-        ("gate", 0, 6): ("up", 0, 0),
-        ("gate", 0, 7): ("up", 0, 1),
-        **{("up", 0, c): ("gate", 0, c - 2) for c in range(3, 7)},
-        ("up", 0, 7): ("up", 0, 2),
+        **{("gate", 0, c): ("up", 0, c - 5) for c in range(5, CHUNKS)},
+        **{("up", 0, c): ("gate", 0, c - 3) for c in range(3, CHUNKS)},
         ("gate", 1, 0): ("gate", 0, 5),
         ("gate", 1, ON_GPSIMD): ("up", 0, 3),
         ("gate", 1, 1): ("gate", 0, 6),
         ("gate", 1, 2): ("gate", 0, 7),
-        ("gate", 1, 3): ("gate", 1, 0),
-        ("gate", 1, 4): ("gate", 1, ON_GPSIMD),
-        ("gate", 1, 5): ("up", 1, 0),
+        **{("gate", 1, c): ("up", 0, c + 2) for c in range(3, 6)},
         ("gate", 1, 6): ("up", 1, ON_GPSIMD),
         ("up", 1, 0): ("up", 0, 4),
-        ("up", 1, ON_GPSIMD): ("up", 0, 5),
-        ("up", 1, 1): ("up", 0, 6),
-        ("up", 1, 2): ("up", 0, 7),
-        ("up", 1, 3): ("gate", 1, 1),
-        ("up", 1, 4): ("gate", 1, 2),
+        ("up", 1, ON_GPSIMD): ("gate", 1, 0),
+        ("up", 1, 1): ("gate", 1, ON_GPSIMD),
+        ("up", 1, 2): ("gate", 1, 1),
+        ("up", 1, 3): ("gate", 1, 2),
+        ("up", 1, 4): ("up", 1, 0),
         ("up", 1, 5): ("up", 1, 2),
         ("up", 1, 6): ("up", 1, 3),
     }
@@ -71,8 +67,8 @@ def psum_banks():
 
 
 BANK = psum_banks()
-LAST_SUMS = [("up", 1, 1), ("gate", 1, 3), ("gate", 1, 4), ("up", 1, 4), ("gate", 1, 5), ("gate", 1, 6)]
-Y_BANKS = [BANK[sums] for sums in LAST_SUMS + [("up", 1, 5), ("up", 1, 6), ("up", 1, 1)]]
+LAST_SUMS = [("gate", 1, 3), ("up", 1, 1), ("gate", 1, 4), ("up", 1, 4), ("gate", 1, 5), ("gate", 1, 6)]
+Y_BANKS = [BANK[sums] for sums in LAST_SUMS + [("up", 1, 5), ("up", 1, 6), ("gate", 1, 3)]]
 
 SPANS = [(0, HALF), (HALF, J - CHUNK), (J - CHUNK, J)]
 MIDDLE = 1
@@ -87,7 +83,8 @@ AT_WU1 = AT_H11 + ROUNDED
 AT_WU1_SCALAR = AT_WU1 + WU1_SPLIT * PACK * PACK * 4
 ALIGN = 64
 AT_H_CODES = [AT_WU1, AT_WU1_SCALAR + ALIGN - CODES]
-AT_ACT_FIRST = AT_WU1_SCALAR + ALIGN
+AT_H00_SCALES = AT_WU1_SCALAR + ALIGN
+AT_ACT_FIRST = AT_H00_SCALES + HALF
 AT_ACT_REST = AT_ACT_FIRST + GROUP * 4
 
 
@@ -132,8 +129,8 @@ def tile_list_gmlpt_silu_mix_gateP_kernel(
         wg0_parts.append(load_weight(half_tile("wg0_high"), wg, GROUP // 2, 1))
         tab_w = held.tile([P, T], I32, name="tab_w", align_bytes=64)
         nc.sync.dma_start(tab_w[:], tab_words[0].rearrange("p t i -> p (t i)").bitcast(I32))
-        wu0_gpsimd = held.tile([P, PACK, WU0_SPLIT * PACK], F32, name="wu0_gpsimd", align_bytes=64)
-        load_weight(wu0_gpsimd, wu, 0, 1)
+        wu0_scalar = held.tile([P, PACK, WU0_SPLIT * PACK], F32, name="wu0_scalar", tag="wu0_scalar", align_bytes=64)
+        load_weight(wu0_scalar, wu, 0, 1)
         wu0_vector = held.tile([P, PACK, GROUP - WU0_SPLIT * PACK], F32, name="wu0_vector", align_bytes=64)
         load_weight(wu0_vector, wu, WU0_SPLIT * PACK, 1)
         wd4_w = reused.tile([P, 2 * N], U8, name="wd4_w", offset=AT_WG1_BF)
@@ -162,15 +159,15 @@ def tile_list_gmlpt_silu_mix_gateP_kernel(
         v_s = held.tile([P, J], U8, name="v_s", align_bytes=64)
         nc.vector.tensor_copy(v_s[:], tab_s[:].indirect(offsets[:]))
 
-        def round_places(engine, part, m_part, rounded, m0, m1):
+        def round_places(engine, part, m_part, rounded, m0, m1, planes=slice(0, PACK)):
             ms = slice(m0 - m_part, m1 - m_part)
             if engine == "gpsimd":
                 dealt = rounded.rearrange("p (t m i) -> p m t i", t=PACK, i=PACK)[:, m0:m1]
                 nc.gpsimd.tensor_scalar(dealt, part.rearrange("p i (m t) -> p m t i", t=PACK)[:, ms], 1.0, 0.0, MULT, ADD)
             else:
-                dealt = rounded.rearrange("p (t m u e) -> p m u t e", t=PACK, u=2, e=2)[:, m0:m1]
+                dealt = rounded.rearrange("p (t m u e) -> p m u t e", t=PACK, u=2, e=2)[:, m0:m1, :, planes]
                 copy = nc.scalar.copy if engine == "scalar" else nc.vector.tensor_copy
-                copy(dealt, part.rearrange("p (u e) (m t) -> p m u t e", e=2, t=PACK)[:, ms])
+                copy(dealt, part.rearrange("p (u e) (m t) -> p m u t e", e=2, t=PACK)[:, ms, :, planes])
 
         def quantize_weight(name, rounded, calls):
             planes = PACK // calls
@@ -217,13 +214,14 @@ def tile_list_gmlpt_silu_mix_gateP_kernel(
             acts[b, c] = act
             nc.scalar.activation(act, up_sums(wg_q[b], c, BANK["gate", b, c]), SILU)
 
-        act_early = held.tile([P, EARLY_SILUS, CHUNK, PACK], F32, name="act_early", align_bytes=64)
+        wu0_bf = held.tile([P, GROUP * PACK], BF16, name="wu0_bf", tag="wu0_bf", align_bytes=64)
+        round_places("scalar", wu0_scalar[:], 0, wu0_bf[:], 0, WU0_SPLIT)
+        act_early = held.tile([P, EARLY_SILUS, CHUNK, PACK], F32, name="act_early", tag="wu0_scalar", align_bytes=64)
         for c in range(EARLY_SILUS):
             gate_silu(0, c, act_early[:, c])
 
-        wu0_bf = held.tile([P, GROUP * PACK], BF16, name="wu0_bf", tag="wu0_bf", align_bytes=64)
-        round_places("gpsimd", wu0_gpsimd[:], 0, wu0_bf[:], 0, WU0_SPLIT)
-        round_places("vector", wu0_vector[:], WU0_SPLIT, wu0_bf[:], WU0_SPLIT, P)
+        for pair in (slice(0, 2), slice(2, PACK)):
+            round_places("vector", wu0_vector[:], WU0_SPLIT, wu0_bf[:], WU0_SPLIT, P, pair)
         wu_q[0] = quantize_weight("wu0", wu0_bf[:], 2)
 
         wd4_d = held.tile([P, 2 * N], U8, name="wd4_d", tag="wu0_bf", align_bytes=64)
@@ -248,9 +246,18 @@ def tile_list_gmlpt_silu_mix_gateP_kernel(
             else:
                 nc.vector.tensor_tensor(rounded, up_sums(wu_q[b], c, bank), acts[b, c], MULT)
 
-        def quantize_hidden(b, half, codes):
-            scales = held.tile([P, HALF], U8, name=f"h_s{b}{half}", align_bytes=64)
-            nc.vector.quantize_mx(out=codes[:].bitcast(FP8X4), scales=scales[:], in_=h_bf[b, half][:])
+        def quantize_hidden(b, half, codes, calls):
+            if (b, half) == (0, 0):
+                scales = reused.tile([P, HALF], U8, name="h_s00", offset=AT_H00_SCALES)
+            else:
+                scales = held.tile([P, HALF], U8, name=f"h_s{b}{half}", align_bytes=64)
+            width = HALF // calls
+            for j in range(0, HALF, width):
+                nc.vector.quantize_mx(
+                    out=codes[:, j : j + width].bitcast(FP8X4),
+                    scales=scales[:, j : j + width],
+                    in_=h_bf[b, half][:, j * PACK : (j + width) * PACK],
+                )
             h_q[b, half] = codes, scales
 
         wg1_bf = reused.tile([P, GROUP * PACK], BF16, name="wg1_bf", offset=AT_WG1_BF)
@@ -270,7 +277,7 @@ def tile_list_gmlpt_silu_mix_gateP_kernel(
             hidden(0, c)
         wu_q[1] = quantize_weight("wu1", wu1_bf[:], 1)
         for half in range(2):
-            quantize_hidden(0, half, reused.tile([P, HALF], U32, name=f"h_c0{half}", offset=AT_H_CODES[half]))
+            quantize_hidden(0, half, reused.tile([P, HALF], U32, name=f"h_c0{half}", offset=AT_H_CODES[half]), 1)
 
         h_bf[1, 1] = reused.tile([P, HALF * PACK], BF16, name="h_bf11", offset=AT_H11)
         wd_sd = reused.tile([P, N], U8, name="wd_sd", offset=AT_H01)[:]
@@ -341,29 +348,29 @@ def tile_list_gmlpt_silu_mix_gateP_kernel(
         act_first = reused.tile([P, CHUNK, PACK], F32, name="act_first", offset=AT_ACT_FIRST)
         act_rest = reused.tile([P, CHUNKS - 1, CHUNK, PACK], F32, name="act_rest", offset=AT_ACT_REST)
         act1 = [act_first[:], *(act_rest[:, turn] for turn in range(CHUNKS - 1))]
-        for turn in range(EARLY_SILUS):
+        for turn in range(AHEAD_OF_COPY):
             gate_silu(1, GROUP1_TURNS[turn], act1[turn])
         for c in GROUP1_TURNS:
             hidden(1, c)
             if c == ON_GPSIMD:
+                gate_silu(1, GROUP1_TURNS[AHEAD_OF_COPY], act1[AHEAD_OF_COPY])
                 wd8_d = reused.tile([P, N], U32, name="wd8_d", offset=AT_ACT_FIRST)
                 nc.scalar.copy(
                     wd8_d[:].rearrange("p (t a m) -> p a t m", t=PACK, m=4),
                     wd8_w[:].bitcast(U32).rearrange("p (a m t) -> p a t m", t=PACK, m=4),
                 )
-                for late in range(EARLY_SILUS, CHUNKS):
+                for late in range(AHEAD_OF_COPY + 1, CHUNKS):
                     gate_silu(1, GROUP1_TURNS[late], act1[late])
             if c == HALF_CHUNKS:
-                quantize_hidden(1, 0, held.tile([P, HALF], U32, name="h_c10", align_bytes=64))
+                quantize_hidden(1, 0, held.tile([P, HALF], U32, name="h_c10", align_bytes=64), 1)
                 down_product(0, 0, HALF // 2, Y_BANKS[0])
                 down_product(0, HALF // 2, HALF, Y_BANKS[1])
+        quantize_hidden(1, 1, held.tile([P, HALF], U32, name="h_c11", align_bytes=64), 2)
         for t in range(1, PACK):
             down_product(t, 0, HALF, Y_BANKS[1 + t])
-        gate_plane(0, 0)
-        quantize_hidden(1, 1, reused.tile([P, HALF], U32, name="h_c11", offset=AT_H_CODES[0]))
         for t in range(PACK):
             down_product(t, HALF, J, Y_BANKS[1 + PACK + t])
-        for t in range(1, PACK):
+        for t in range(PACK):
             gate_plane(0, t)
         round_span(0)
         for j0, j1 in SPANS[1:]:

@@ -26,14 +26,16 @@ WD8_SCALES_AT = 4
 CHUNK = 128
 CHUNKS = J // CHUNK
 HALF = J // 2
+QUARTER = J // 4
 HALF_CHUNKS = CHUNKS // 2
 HALF_M = P // 2
 
 WORD_PIECES = [(0, CHUNK), (CHUNK, 3 * CHUNK), (3 * CHUNK, J)]
 WU0_SPLIT = 48
+WG1_SPLIT = 80
 EARLY_SILUS = 5
 AHEAD_OF_COPY = 5
-WU1_SPLIT = 80
+WU1_SPLIT = 96
 ON_GPSIMD = CHUNKS - 1
 GROUP1_TURNS = [0, ON_GPSIMD, *range(1, ON_GPSIMD)]
 
@@ -74,18 +76,18 @@ SPANS = [(0, HALF), (HALF, J - CHUNK), (J - CHUNK, J)]
 MIDDLE = 1
 
 ROUNDED = GROUP * PACK * 2
-CODES = HALF * 4
 AT_WU1_BF = PACK * HALF * 4
 AT_WG1_BF = AT_WU1_BF + ROUNDED // 2
 AT_H01 = AT_WU1_BF + ROUNDED
 AT_H11 = AT_H01 + N
-AT_WU1 = AT_H11 + ROUNDED
-AT_WU1_SCALAR = AT_WU1 + WU1_SPLIT * PACK * PACK * 4
+ACT = GROUP * 4
 ALIGN = 64
-AT_H_CODES = [AT_WU1, AT_WU1_SCALAR + ALIGN - CODES]
-AT_H00_SCALES = AT_WU1_SCALAR + ALIGN
-AT_ACT_FIRST = AT_H00_SCALES + HALF
-AT_ACT_REST = AT_ACT_FIRST + GROUP * 4
+AT_WG1_GPSIMD = AT_H11 + ROUNDED
+AT_WG1_SCALAR = AT_WG1_GPSIMD + WG1_SPLIT * PACK * PACK * 4
+AT_ACT_LATE = AT_WG1_SCALAR + QUARTER // 2
+AT_ACT1 = AT_ACT_LATE + (CHUNKS - EARLY_SILUS) * ACT
+AT_WU1_SCALAR = AT_ACT1 + CHUNKS * ACT - ALIGN
+AT_WU1_GPSIMD = AT_WU1_SCALAR + (P - WU1_SPLIT) * PACK * PACK * 4
 
 
 def tile_list_gmlpt_silu_mix_gateP_kernel(
@@ -135,10 +137,12 @@ def tile_list_gmlpt_silu_mix_gateP_kernel(
         load_weight(wu0_vector, wu, WU0_SPLIT * PACK, 1)
         wd4_w = reused.tile([P, 2 * N], U8, name="wd4_w", offset=AT_WG1_BF)
         nc.sync.dma_start(wd4_w[:].bitcast(I32), wd4_words[0].bitcast(I32))
-        wg1 = held.tile([P, PACK, GROUP], F32, name="wg1", tag="wg1", align_bytes=64)
-        load_weight(wg1, wg, GROUP, 1)
+        wg1_gpsimd = reused.tile([P, PACK, WG1_SPLIT * PACK], F32, name="wg1_gpsimd", offset=AT_WG1_GPSIMD)
+        load_weight(wg1_gpsimd, wg, GROUP, 1)
+        wg1_scalar = reused.tile([P, PACK, GROUP - WG1_SPLIT * PACK], F32, name="wg1_scalar", offset=AT_WG1_SCALAR)
+        load_weight(wg1_scalar, wg, GROUP + WG1_SPLIT * PACK, 1)
         load_scale_rows(wd_s, 0, wd4_scales)
-        wu1_gpsimd = reused.tile([P, PACK, WU1_SPLIT * PACK], F32, name="wu1_gpsimd", offset=AT_WU1)
+        wu1_gpsimd = reused.tile([P, PACK, WU1_SPLIT * PACK], F32, name="wu1_gpsimd", offset=AT_WU1_GPSIMD)
         load_weight(wu1_gpsimd, wu, GROUP, 1)
         wu1_scalar = reused.tile([P, PACK, GROUP - WU1_SPLIT * PACK], F32, name="wu1_scalar", offset=AT_WU1_SCALAR)
         load_weight(wu1_scalar, wu, GROUP + WU1_SPLIT * PACK, 1)
@@ -233,7 +237,7 @@ def tile_list_gmlpt_silu_mix_gateP_kernel(
         h_bf00 = held.tile([P, HALF * PACK], BF16, name="h_bf00", align_bytes=64)
         h_bf10 = held.tile([P, HALF * PACK], BF16, name="h_bf10", align_bytes=64)
         h_bf = {(0, 0): h_bf00, (1, 0): h_bf10}
-        h_q = {}
+        h_q = [[], []]
 
         def hidden(b, c):
             bank = BANK["up", b, c]
@@ -246,29 +250,29 @@ def tile_list_gmlpt_silu_mix_gateP_kernel(
             else:
                 nc.vector.tensor_tensor(rounded, up_sums(wu_q[b], c, bank), acts[b, c], MULT)
 
-        def quantize_hidden(b, half, codes, calls):
-            if (b, half) == (0, 0):
-                scales = reused.tile([P, HALF], U8, name="h_s00", offset=AT_H00_SCALES)
-            else:
-                scales = held.tile([P, HALF], U8, name=f"h_s{b}{half}", align_bytes=64)
-            width = HALF // calls
-            for j in range(0, HALF, width):
+        def quantize_hidden(b, j0, codes, scales, calls):
+            width = scales.shape[1] // calls
+            for j in range(0, scales.shape[1], width):
+                place = (j0 % HALF + j) * PACK
                 nc.vector.quantize_mx(
                     out=codes[:, j : j + width].bitcast(FP8X4),
                     scales=scales[:, j : j + width],
-                    in_=h_bf[b, half][:, j * PACK : (j + width) * PACK],
+                    in_=h_bf[b, j0 // HALF][:, place : place + width * PACK],
                 )
-            h_q[b, half] = codes, scales
+            h_q[b].append((j0, j0 + scales.shape[1], codes, scales))
 
         wg1_bf = reused.tile([P, GROUP * PACK], BF16, name="wg1_bf", offset=AT_WG1_BF)
-        round_places("gpsimd", wg1[:], 0, wg1_bf[:], 0, HALF_M)
-        round_places("scalar", wg1[:], 0, wg1_bf[:], HALF_M, P)
+        round_places("gpsimd", wg1_gpsimd[:], 0, wg1_bf[:], 0, WG1_SPLIT)
+        round_places("scalar", wg1_scalar[:], WG1_SPLIT, wg1_bf[:], WG1_SPLIT, P)
         for c in range(HALF_CHUNKS):
             hidden(0, c)
-        act_late = held.tile([P, CHUNKS - EARLY_SILUS, CHUNK, PACK], F32, name="act_late", tag="wg1", align_bytes=64)
+        act_late = reused.tile([P, CHUNKS - EARLY_SILUS, CHUNK, PACK], F32, name="act_late", offset=AT_ACT_LATE)
         for c in range(EARLY_SILUS, CHUNKS):
             gate_silu(0, c, act_late[:, c - EARLY_SILUS])
         wg_q[1] = quantize_weight("wg1", wg1_bf[:], 1)
+        codes = held.tile([P, QUARTER], U32, name="h_c_quarter", align_bytes=64)
+        scales = reused.tile([P, QUARTER], U8, name="h_s_quarter", offset=AT_WG1_SCALAR - QUARTER // 2)
+        quantize_hidden(0, 0, codes, scales, 1)
         wu1_bf = reused.tile([P, GROUP * PACK], BF16, name="wu1_bf", offset=AT_WU1_BF)
         round_places("gpsimd", wu1_gpsimd[:], 0, wu1_bf[:], 0, WU1_SPLIT)
         round_places("scalar", wu1_scalar[:], WU1_SPLIT, wu1_bf[:], WU1_SPLIT, P)
@@ -276,8 +280,10 @@ def tile_list_gmlpt_silu_mix_gateP_kernel(
         for c in range(HALF_CHUNKS, CHUNKS):
             hidden(0, c)
         wu_q[1] = quantize_weight("wu1", wu1_bf[:], 1)
-        for half in range(2):
-            quantize_hidden(0, half, reused.tile([P, HALF], U32, name=f"h_c0{half}", offset=AT_H_CODES[half]), 1)
+        for j0, j1 in ((QUARTER, HALF), (HALF, J)):
+            codes = reused.tile([P, j1 - j0], U32, name=f"h_c{j0}", offset=AT_WU1_GPSIMD + (j0 - QUARTER) * 4)
+            scales = reused.tile([P, j1 - j0], U8, name=f"h_s{j0}", offset=AT_WU1_SCALAR + ALIGN + j0 - QUARTER)
+            quantize_hidden(0, j0, codes, scales, 1)
 
         h_bf[1, 1] = reused.tile([P, HALF * PACK], BF16, name="h_bf11", offset=AT_H11)
         wd_sd = reused.tile([P, N], U8, name="wd_sd", offset=AT_H01)[:]
@@ -286,49 +292,62 @@ def tile_list_gmlpt_silu_mix_gateP_kernel(
             wd_s[:].rearrange("p (a m t) -> p a t m", t=PACK, m=16),
         )
 
-        y_f = [
-            reused.tile([P, PACK, HALF], F32, name="y_f0", offset=0, align_bytes=64),
-            held.tile([P, PACK, HALF], F32, name="y_f1"),
-        ]
+        y_first = reused.tile([P, PACK * HALF - CHUNK], F32, name="y_first", offset=0, align_bytes=64)
+        y_apart = held.tile([P, CHUNK], F32, name="y_apart")
+        y_second = held.tile([P, PACK * HALF], F32, name="y_second")
+
+        def y_f(t, j0, j1):
+            if j0 >= HALF:
+                return y_second[:, t * HALF + j0 - HALF : t * HALF + j1 - HALF]
+            if (t, j0) == (PACK - 1, HALF - CHUNK):
+                return y_apart[:]
+            return y_first[:, t * HALF + j0 : t * HALF + j1]
+
+        def pieces(t, j0, j1):
+            if (t, j1) == (PACK - 1, HALF):
+                return [(j0, j1 - CHUNK), (j1 - CHUNK, j1)]
+            return [(j0, j1)]
+
         out_f = [held.tile([P, PACK, HALF], F32, name="out_f0")[:]]
         out_bf = held.tile([P, J * PACK], BF16, name="out_bf", align_bytes=64)
         out_c = held.tile([P, J], U32, name="out_c", align_bytes=64)
         out_s = held.tile([P, J], U8, name="out_s", align_bytes=64)
 
         def down_product(t, j0, j1, bank):
-            half = j0 // HALF
             ms = slice(t * P, (t + 1) * P)
-            cols = slice(j0 - half * HALF, j1 - half * HALF)
             y = psum.tile([P, j1 - j0], F32, name="y", tag=f"bank{bank}")
-            nc.tensor.matmul_mx(
-                out=y[:],
-                lhsT=wd8_d[:, ms].bitcast(FP8X4),
-                lhsT_scale=wd_sd[WD8_SCALES_AT:P, ms],
-                rhs=h_q[0, half][0][:, cols].bitcast(FP8X4),
-                rhs_scale=h_q[0, half][1][:, cols],
-                start=True,
-                stop=False,
-            )
-            nc.tensor.matmul_mx(
-                out=y[:],
-                lhsT=wd4_d[:, 2 * t * P : 2 * (t + 1) * P].bitcast(FP4X4),
-                lhsT_scale=wd_sd[:, ms],
-                rhs=h_q[1, half][0][:, cols].bitcast(FP8X4),
-                rhs_scale=h_q[1, half][1][:, cols],
-                start=False,
-                stop=True,
-            )
-            nc.scalar.copy(y_f[half][:, t, cols], y[:])
+            weights = [
+                (wd8_d[:, ms].bitcast(FP8X4), wd_sd[WD8_SCALES_AT:P, ms]),
+                (wd4_d[:, 2 * t * P : 2 * (t + 1) * P].bitcast(FP4X4), wd_sd[:, ms]),
+            ]
+            passes = [
+                (b, max(j0, q0), min(j1, q1), q0, codes, scales)
+                for b in range(2)
+                for q0, q1, codes, scales in h_q[b]
+                if q0 < j1 and j0 < q1
+            ]
+            for turn, (b, c0, c1, q0, codes, scales) in enumerate(passes):
+                nc.tensor.matmul_mx(
+                    out=y[:, c0 - j0 : c1 - j0],
+                    lhsT=weights[b][0],
+                    lhsT_scale=weights[b][1],
+                    rhs=codes[:, c0 - q0 : c1 - q0].bitcast(FP8X4),
+                    rhs_scale=scales[:, c0 - q0 : c1 - q0],
+                    start=turn == 0,
+                    stop=turn == len(passes) - 1,
+                )
+            for a, b in pieces(t, j0, j1):
+                nc.scalar.copy(y_f(t, a, b), y[:, a - j0 : b - j0])
 
         def gate_plane(s, t):
             j0, j1 = SPANS[s]
-            half = j0 // HALF
-            nc.vector.tensor_tensor(
-                out_f[s][:, t, :],
-                gate_rows[t][:].indirect(offsets[:, j0 // 16 : j1 // 16]),
-                y_f[half][:, t, j0 - half * HALF : j1 - half * HALF],
-                MULT,
-            )
+            for a, b in pieces(t, j0, j1):
+                nc.vector.tensor_tensor(
+                    out_f[s][:, t, a - j0 : b - j0],
+                    gate_rows[t][:].indirect(offsets[:, a // 16 : b // 16]),
+                    y_f(t, a, b),
+                    MULT,
+                )
             if t % 2:
                 pair = slice(t - 1, t + 1)
                 nc.sync.dma_start(out_0.rearrange("(p t) j -> p t j", t=PACK)[:, pair, j0:j1], out_f[s][:, pair, :])
@@ -345,27 +364,27 @@ def tile_list_gmlpt_silu_mix_gateP_kernel(
                 out_f[s].rearrange("p t (a j) -> p a t j", j=4),
             )
 
-        act_first = reused.tile([P, CHUNK, PACK], F32, name="act_first", offset=AT_ACT_FIRST)
-        act_rest = reused.tile([P, CHUNKS - 1, CHUNK, PACK], F32, name="act_rest", offset=AT_ACT_REST)
-        act1 = [act_first[:], *(act_rest[:, turn] for turn in range(CHUNKS - 1))]
+        act1 = reused.tile([P, CHUNKS, CHUNK, PACK], F32, name="act1", offset=AT_ACT1)
         for turn in range(AHEAD_OF_COPY):
-            gate_silu(1, GROUP1_TURNS[turn], act1[turn])
+            gate_silu(1, GROUP1_TURNS[turn], act1[:, turn])
         for c in GROUP1_TURNS:
             hidden(1, c)
             if c == ON_GPSIMD:
-                gate_silu(1, GROUP1_TURNS[AHEAD_OF_COPY], act1[AHEAD_OF_COPY])
-                wd8_d = reused.tile([P, N], U32, name="wd8_d", offset=AT_ACT_FIRST)
+                gate_silu(1, GROUP1_TURNS[AHEAD_OF_COPY], act1[:, AHEAD_OF_COPY])
+                wd8_d = reused.tile([P, N], U32, name="wd8_d", offset=AT_WU1_BF)
                 nc.scalar.copy(
                     wd8_d[:].rearrange("p (t a m) -> p a t m", t=PACK, m=4),
                     wd8_w[:].bitcast(U32).rearrange("p (a m t) -> p a t m", t=PACK, m=4),
                 )
                 for late in range(AHEAD_OF_COPY + 1, CHUNKS):
-                    gate_silu(1, GROUP1_TURNS[late], act1[late])
+                    gate_silu(1, GROUP1_TURNS[late], act1[:, late])
             if c == HALF_CHUNKS:
-                quantize_hidden(1, 0, held.tile([P, HALF], U32, name="h_c10", align_bytes=64), 1)
+                h_c10 = held.tile([P, HALF], U32, name="h_c10", align_bytes=64)
+                quantize_hidden(1, 0, h_c10, held.tile([P, HALF], U8, name="h_s10", align_bytes=64), 1)
                 down_product(0, 0, HALF // 2, Y_BANKS[0])
                 down_product(0, HALF // 2, HALF, Y_BANKS[1])
-        quantize_hidden(1, 1, held.tile([P, HALF], U32, name="h_c11", align_bytes=64), 2)
+        h_c11 = held.tile([P, HALF], U32, name="h_c11", align_bytes=64)
+        quantize_hidden(1, HALF, h_c11, held.tile([P, HALF], U8, name="h_s11", align_bytes=64), 2)
         for t in range(1, PACK):
             down_product(t, 0, HALF, Y_BANKS[1 + t])
         for t in range(PACK):

@@ -30,7 +30,7 @@ QUARTER = J // 4
 HALF_CHUNKS = CHUNKS // 2
 HALF_M = P // 2
 
-WORD_PIECES = [(0, CHUNK), (CHUNK, 3 * CHUNK), (3 * CHUNK, J)]
+WORD_PIECES = [(0, CHUNK), (CHUNK, 3 * CHUNK), (3 * CHUNK, 5 * CHUNK), (5 * CHUNK, J - CHUNK)]
 WU0_SPLIT = 48
 WG1_SPLIT = 80
 EARLY_SILUS = 5
@@ -73,7 +73,7 @@ LAST_SUMS = [("gate", 1, 3), ("up", 1, 1), ("gate", 1, 4), ("up", 1, 4), ("gate"
 Y_BANKS = [BANK[sums] for sums in LAST_SUMS + [("up", 1, 5), ("up", 1, 6), ("gate", 1, 3)]]
 
 SPANS = [(0, HALF), (HALF, J - CHUNK), (J - CHUNK, J)]
-MIDDLE = 1
+MIDDLE, LAST = 1, 2
 
 ROUNDED = GROUP * PACK * 2
 AT_WU1_BF = PACK * HALF * 4
@@ -133,7 +133,7 @@ def tile_list_gmlpt_silu_mix_gateP_kernel(
         nc.sync.dma_start(tab_w[:], tab_words[0].rearrange("p t i -> p (t i)").bitcast(I32))
         wu0_scalar = held.tile([P, PACK, WU0_SPLIT * PACK], F32, name="wu0_scalar", tag="wu0_scalar", align_bytes=64)
         load_weight(wu0_scalar, wu, 0, 1)
-        wu0_vector = held.tile([P, PACK, GROUP - WU0_SPLIT * PACK], F32, name="wu0_vector", align_bytes=64)
+        wu0_vector = held.tile([P, PACK, GROUP - WU0_SPLIT * PACK], F32, name="wu0_vector", tag="wu0_vector", align_bytes=64)
         load_weight(wu0_vector, wu, WU0_SPLIT * PACK, 1)
         wd4_w = reused.tile([P, 2 * N], U8, name="wd4_w", offset=AT_WG1_BF)
         nc.sync.dma_start(wd4_w[:].bitcast(I32), wd4_words[0].bitcast(I32))
@@ -191,11 +191,15 @@ def tile_list_gmlpt_silu_mix_gateP_kernel(
         wg_q[0] = quantize_weight("wg0", wg0_bf[:], 1)
 
         v_w = {}
-        for j0, j1 in WORD_PIECES:
-            words = held.tile([P, j1 - j0], U32, name=f"v_w{j0}", align_bytes=64)
+
+        def gather_words(j0, j1, tag):
+            words = held.tile([P, j1 - j0], U32, name=f"v_w{j0}", tag=tag, align_bytes=64)
             nc.vector.tensor_copy(words[:], tab_w[:].bitcast(U32).indirect(offsets[:, j0 // 16 : j1 // 16]))
             for j in range(j0, j1, CHUNK):
                 v_w[j // CHUNK] = words[:, j - j0 : j - j0 + CHUNK]
+
+        for j0, j1 in WORD_PIECES:
+            gather_words(j0, j1, f"v_w{j0}")
 
         def up_sums(wq, c, bank):
             acc = psum.tile([P, PACK, CHUNK], F32, name="acc", tag=f"bank{bank}")
@@ -227,6 +231,7 @@ def tile_list_gmlpt_silu_mix_gateP_kernel(
         for pair in (slice(0, 2), slice(2, PACK)):
             round_places("vector", wu0_vector[:], WU0_SPLIT, wu0_bf[:], WU0_SPLIT, P, pair)
         wu_q[0] = quantize_weight("wu0", wu0_bf[:], 2)
+        gather_words(J - CHUNK, J, "wu0_vector")
 
         wd4_d = held.tile([P, 2 * N], U8, name="wd4_d", tag="wu0_bf", align_bytes=64)
         nc.vector.tensor_copy(
@@ -279,7 +284,7 @@ def tile_list_gmlpt_silu_mix_gateP_kernel(
         h_bf[0, 1] = reused.tile([P, HALF * PACK], BF16, name="h_bf01", offset=AT_H01)
         for c in range(HALF_CHUNKS, CHUNKS):
             hidden(0, c)
-        wu_q[1] = quantize_weight("wu1", wu1_bf[:], 1)
+        wu_q[1] = quantize_weight("wu1", wu1_bf[:], 2)
         for j0, j1 in ((QUARTER, HALF), (HALF, J)):
             codes = reused.tile([P, j1 - j0], U32, name=f"h_c{j0}", offset=AT_WU1_GPSIMD + (j0 - QUARTER) * 4)
             scales = reused.tile([P, j1 - j0], U8, name=f"h_s{j0}", offset=AT_WU1_SCALAR + ALIGN + j0 - QUARTER)
@@ -348,8 +353,9 @@ def tile_list_gmlpt_silu_mix_gateP_kernel(
                     y_f(t, a, b),
                     MULT,
                 )
-            if t % 2:
-                pair = slice(t - 1, t + 1)
+            stored = PACK if s == LAST else 2
+            if (t + 1) % stored == 0:
+                pair = slice(t + 1 - stored, t + 1)
                 nc.sync.dma_start(out_0.rearrange("(p t) j -> p t j", t=PACK)[:, pair, j0:j1], out_f[s][:, pair, :])
                 if s == MIDDLE:
                     nc.scalar.copy(
@@ -403,6 +409,7 @@ def tile_list_gmlpt_silu_mix_gateP_kernel(
             nc.vector.quantize_mx(
                 out=out_c[:, j0:j1].bitcast(FP8X4), scales=out_s[:, j0:j1], in_=out_bf[:, j0 * PACK : j1 * PACK]
             )
+        for j0, j1 in ((0, HALF), (HALF, J)):
             nc.sync.dma_start(
                 out_1[0].rearrange("p j i -> p (j i)").bitcast(I32)[:, j0:j1], out_c[:, j0:j1].bitcast(I32)
             )

@@ -30,10 +30,11 @@ QUARTER = J // 4
 HALF_CHUNKS = CHUNKS // 2
 HALF_M = P // 2
 
-WORD_PIECES = [(0, CHUNK), (CHUNK, 3 * CHUNK), (3 * CHUNK, 5 * CHUNK), (5 * CHUNK, J - CHUNK)]
-WU0_SPLIT = 48
+WORD_PIECES = [(0, CHUNK), (CHUNK, HALF), (HALF + QUARTER, J)]
+LATE_WORDS = (HALF, HALF + QUARTER)
+WU0_SPLIT, WU0_LAST = 48, 80
 WG1_SPLIT = 80
-EARLY_SILUS = 5
+EARLY_SILUS = 4
 AHEAD_OF_COPY = 5
 WU1_SPLIT = 96
 ON_GPSIMD = CHUNKS - 1
@@ -79,7 +80,8 @@ ROUNDED = GROUP * PACK * 2
 AT_WU1_BF = PACK * HALF * 4
 AT_WG1_BF = AT_WU1_BF + ROUNDED // 2
 AT_H01 = AT_WU1_BF + ROUNDED
-AT_H11 = AT_H01 + N
+AT_WD8_DEALT = AT_H01 + P
+AT_H11 = AT_WD8_DEALT + N * 4
 ACT = GROUP * 4
 ALIGN = 64
 AT_WG1_GPSIMD = AT_H11 + ROUNDED
@@ -129,14 +131,14 @@ def tile_list_gmlpt_silu_mix_gateP_kernel(
         nc.gpsimd.memset(wd_s[:].bitcast(I32), 0)
 
         wg0_parts.append(load_weight(half_tile("wg0_high"), wg, GROUP // 2, 1))
-        tab_w = held.tile([P, T], I32, name="tab_w", align_bytes=64)
+        tab_w = reused.tile([P, T], I32, name="tab_w", offset=AT_WU1_BF)
         nc.sync.dma_start(tab_w[:], tab_words[0].rearrange("p t i -> p (t i)").bitcast(I32))
         wu0_scalar = held.tile([P, PACK, WU0_SPLIT * PACK], F32, name="wu0_scalar", tag="wu0_scalar", align_bytes=64)
         load_weight(wu0_scalar, wu, 0, 1)
-        wu0_vector = held.tile([P, PACK, GROUP - WU0_SPLIT * PACK], F32, name="wu0_vector", tag="wu0_vector", align_bytes=64)
-        load_weight(wu0_vector, wu, WU0_SPLIT * PACK, 1)
-        wd4_w = reused.tile([P, 2 * N], U8, name="wd4_w", offset=AT_WG1_BF)
-        nc.sync.dma_start(wd4_w[:].bitcast(I32), wd4_words[0].bitcast(I32))
+        wu0_second = held.tile([P, PACK, (WU0_LAST - WU0_SPLIT) * PACK], F32, name="wu0_second", align_bytes=64)
+        load_weight(wu0_second, wu, WU0_SPLIT * PACK, 1)
+        wu0_last = held.tile([P, PACK, GROUP - WU0_LAST * PACK], F32, name="wu0_last", tag="wu0_last", align_bytes=64)
+        load_weight(wu0_last, wu, WU0_LAST * PACK, 1)
         wg1_gpsimd = reused.tile([P, PACK, WG1_SPLIT * PACK], F32, name="wg1_gpsimd", offset=AT_WG1_GPSIMD)
         load_weight(wg1_gpsimd, wg, GROUP, 1)
         wg1_scalar = reused.tile([P, PACK, GROUP - WG1_SPLIT * PACK], F32, name="wg1_scalar", offset=AT_WG1_SCALAR)
@@ -146,6 +148,8 @@ def tile_list_gmlpt_silu_mix_gateP_kernel(
         load_weight(wu1_gpsimd, wu, GROUP, 1)
         wu1_scalar = reused.tile([P, PACK, GROUP - WU1_SPLIT * PACK], F32, name="wu1_scalar", offset=AT_WU1_SCALAR)
         load_weight(wu1_scalar, wu, GROUP + WU1_SPLIT * PACK, 1)
+        wd4_w = held.tile([P, 2 * N], U8, name="wd4_w", align_bytes=64)
+        nc.sync.dma_start(wd4_w[:].bitcast(I32), wd4_words[0].bitcast(I32))
         load_scale_rows(wd_s, WD8_SCALES_AT, wd8_scales)
         wd8_w = held.tile([P, N], I32, name="wd8_w", align_bytes=64)
         nc.sync.dma_start(wd8_w[:], wd8_words[0].rearrange("p n i -> p (n i)").bitcast(I32))
@@ -222,25 +226,20 @@ def tile_list_gmlpt_silu_mix_gateP_kernel(
             acts[b, c] = act
             nc.scalar.activation(act, up_sums(wg_q[b], c, BANK["gate", b, c]), SILU)
 
-        wu0_bf = held.tile([P, GROUP * PACK], BF16, name="wu0_bf", tag="wu0_bf", align_bytes=64)
+        wu0_bf = held.tile([P, GROUP * PACK], BF16, name="wu0_bf", align_bytes=64)
         round_places("scalar", wu0_scalar[:], 0, wu0_bf[:], 0, WU0_SPLIT)
         act_early = held.tile([P, EARLY_SILUS, CHUNK, PACK], F32, name="act_early", tag="wu0_scalar", align_bytes=64)
         for c in range(EARLY_SILUS):
             gate_silu(0, c, act_early[:, c])
 
+        round_places("vector", wu0_second[:], WU0_SPLIT, wu0_bf[:], WU0_SPLIT, WU0_LAST)
         for pair in (slice(0, 2), slice(2, PACK)):
-            round_places("vector", wu0_vector[:], WU0_SPLIT, wu0_bf[:], WU0_SPLIT, P, pair)
+            round_places("vector", wu0_last[:], WU0_LAST, wu0_bf[:], WU0_LAST, P, pair)
         wu_q[0] = quantize_weight("wu0", wu0_bf[:], 2)
-        gather_words(J - CHUNK, J, "wu0_vector")
-
-        wd4_d = held.tile([P, 2 * N], U8, name="wd4_d", tag="wu0_bf", align_bytes=64)
-        nc.vector.tensor_copy(
-            wd4_d[:].bitcast(U16).rearrange("p (t a m) -> p a t m", t=PACK, m=8),
-            wd4_w[:].bitcast(U16).rearrange("p (a m t) -> p a t m", t=PACK, m=8),
-        )
+        gather_words(*LATE_WORDS, "wu0_last")
 
         h_bf00 = held.tile([P, HALF * PACK], BF16, name="h_bf00", align_bytes=64)
-        h_bf10 = held.tile([P, HALF * PACK], BF16, name="h_bf10", align_bytes=64)
+        h_bf10 = held.tile([P, HALF * PACK], BF16, name="h_bf10", tag="h_bf10", align_bytes=64)
         h_bf = {(0, 0): h_bf00, (1, 0): h_bf10}
         h_q = [[], []]
 
@@ -290,12 +289,18 @@ def tile_list_gmlpt_silu_mix_gateP_kernel(
             scales = reused.tile([P, j1 - j0], U8, name=f"h_s{j0}", offset=AT_WU1_SCALAR + ALIGN + j0 - QUARTER)
             quantize_hidden(0, j0, codes, scales, 1)
 
+        def deal(copy, dealt, source, t0, t1, run):
+            copy(
+                dealt.rearrange("p (t a m) -> p a t m", t=t1 - t0, m=run),
+                source.rearrange("p (a m t) -> p a t m", t=PACK, m=run)[:, :, t0:t1],
+            )
+
         h_bf[1, 1] = reused.tile([P, HALF * PACK], BF16, name="h_bf11", offset=AT_H11)
-        wd_sd = reused.tile([P, N], U8, name="wd_sd", offset=AT_H01)[:]
-        nc.gpsimd.tensor_copy(
-            wd_sd.rearrange("p (t a m) -> p a t m", t=PACK, m=16),
-            wd_s[:].rearrange("p (a m t) -> p a t m", t=PACK, m=16),
-        )
+        wd_sd = [reused.tile([P, P], U8, name="wd_sd_first", offset=AT_H01)[:]]
+        deal(nc.gpsimd.tensor_copy, wd_sd[0], wd_s[:], 0, 1, 16)
+        wd8_d = reused.tile([P, N], I32, name="wd8_d", offset=AT_WD8_DEALT)
+        deal(nc.gpsimd.tensor_copy, wd8_d[:], wd8_w[:], 0, PACK, 4)
+        wd4_d = []
 
         y_first = reused.tile([P, PACK * HALF - CHUNK], F32, name="y_first", offset=0, align_bytes=64)
         y_apart = held.tile([P, CHUNK], F32, name="y_apart")
@@ -319,11 +324,10 @@ def tile_list_gmlpt_silu_mix_gateP_kernel(
         out_s = held.tile([P, J], U8, name="out_s", align_bytes=64)
 
         def down_product(t, j0, j1, bank):
-            ms = slice(t * P, (t + 1) * P)
             y = psum.tile([P, j1 - j0], F32, name="y", tag=f"bank{bank}")
             weights = [
-                (wd8_d[:, ms].bitcast(FP8X4), wd_sd[WD8_SCALES_AT:P, ms]),
-                (wd4_d[:, 2 * t * P : 2 * (t + 1) * P].bitcast(FP4X4), wd_sd[:, ms]),
+                (wd8_d[:, t * P : (t + 1) * P].bitcast(FP8X4), wd_sd[t][WD8_SCALES_AT:P, :]),
+                (wd4_d[t].bitcast(FP4X4), wd_sd[t]),
             ]
             passes = [
                 (b, max(j0, q0), min(j1, q1), q0, codes, scales)
@@ -353,7 +357,7 @@ def tile_list_gmlpt_silu_mix_gateP_kernel(
                     y_f(t, a, b),
                     MULT,
                 )
-            stored = PACK if s == LAST else 2
+            stored = 2 if s == MIDDLE else PACK
             if (t + 1) % stored == 0:
                 pair = slice(t + 1 - stored, t + 1)
                 nc.sync.dma_start(out_0.rearrange("(p t) j -> p t j", t=PACK)[:, pair, j0:j1], out_f[s][:, pair, :])
@@ -377,16 +381,19 @@ def tile_list_gmlpt_silu_mix_gateP_kernel(
             hidden(1, c)
             if c == ON_GPSIMD:
                 gate_silu(1, GROUP1_TURNS[AHEAD_OF_COPY], act1[:, AHEAD_OF_COPY])
-                wd8_d = reused.tile([P, N], U32, name="wd8_d", offset=AT_WU1_BF)
-                nc.scalar.copy(
-                    wd8_d[:].rearrange("p (t a m) -> p a t m", t=PACK, m=4),
-                    wd8_w[:].bitcast(U32).rearrange("p (a m t) -> p a t m", t=PACK, m=4),
-                )
+                wd4_first = reused.tile([P, 2 * P], U8, name="wd4_first", offset=AT_WU1_BF)
+                deal(nc.scalar.copy, wd4_first[:].bitcast(U16), wd4_w[:].bitcast(U16), 0, 1, 8)
                 for late in range(AHEAD_OF_COPY + 1, CHUNKS):
                     gate_silu(1, GROUP1_TURNS[late], act1[:, late])
+                wd4_rest = reused.tile([P, 2 * (N - P)], U8, name="wd4_rest", offset=AT_WU1_BF + 2 * P)
+                deal(nc.scalar.copy, wd4_rest[:].bitcast(U16), wd4_w[:].bitcast(U16), 1, PACK, 8)
+                wd4_d += [wd4_first[:]] + [wd4_rest[:, 2 * t * P : 2 * (t + 1) * P] for t in range(PACK - 1)]
             if c == HALF_CHUNKS:
                 h_c10 = held.tile([P, HALF], U32, name="h_c10", align_bytes=64)
                 quantize_hidden(1, 0, h_c10, held.tile([P, HALF], U8, name="h_s10", align_bytes=64), 1)
+                wd_sd_rest = held.tile([P, N - P], U8, name="wd_sd_rest", tag="h_bf10", align_bytes=64)
+                deal(nc.gpsimd.tensor_copy, wd_sd_rest[:], wd_s[:], 1, PACK, 16)
+                wd_sd += [wd_sd_rest[:, t * P : (t + 1) * P] for t in range(PACK - 1)]
                 down_product(0, 0, HALF // 2, Y_BANKS[0])
                 down_product(0, HALF // 2, HALF, Y_BANKS[1])
         h_c11 = held.tile([P, HALF], U32, name="h_c11", align_bytes=64)

@@ -32,7 +32,7 @@ HALF_M = P // 2
 
 WORD_PIECES = [(0, CHUNK), (CHUNK, HALF), (HALF + QUARTER, J)]
 LATE_WORDS = (HALF, HALF + QUARTER)
-WU0_SPLIT, WU0_LAST = 48, 80
+WU0_SPLIT, WU0_LAST = 56, 96
 WG1_SPLIT = 80
 EARLY_SILUS = 4
 AHEAD_OF_COPY = 5

from contextlib import ExitStack

import concourse.mybir as mybir

K, R, N, T, J = 512, 1024, 512, 2048, 1024
FLOPS = 2 * K * R * J * 2 + 2 * R * N * J

F32 = mybir.dt.float32
BF16 = mybir.dt.bfloat16
I32 = mybir.dt.int32
U32 = mybir.dt.uint32
U16 = mybir.dt.uint16
U8 = mybir.dt.uint8
FP8X4 = mybir.dt.float8_e4m3fn_x4
FP4X4 = mybir.dt.float4_e2m1fn_x4
MULT = mybir.AluOpType.mult
ADD = mybir.AluOpType.add
SILU = mybir.ActivationFunctionType.Silu

P = 128
PACK = 4
GROUP = P * PACK
QUADRANT = 32
SCALE_ROWS = GROUP // 32
WD8_SCALES_AT = 4
CHUNK = 128
CHUNKS = J // CHUNK
HALF = J // 2
QUARTER = J // 4
HALF_CHUNKS = CHUNKS // 2
HALF_M = P // 2

WORD_PIECES = [(0, CHUNK), (CHUNK, HALF), (HALF + QUARTER, J)]
LATE_WORDS = (HALF, HALF + QUARTER)
WU0_SPLIT, WU0_LAST = 56, 96
WG1_SPLIT = 80
EARLY_SILUS = 4
AHEAD_OF_COPY = 5
WU1_SPLIT = 96
ON_GPSIMD = CHUNKS - 1
GROUP1_TURNS = [0, ON_GPSIMD, *range(1, ON_GPSIMD)]


def psum_banks():
    follows = {
        **{("gate", 0, c): ("up", 0, c - 5) for c in range(5, CHUNKS)},
        **{("up", 0, c): ("gate", 0, c - 3) for c in range(3, CHUNKS)},
        ("gate", 1, 0): ("gate", 0, 5),
        ("gate", 1, ON_GPSIMD): ("up", 0, 3),
        ("gate", 1, 1): ("gate", 0, 6),
        ("gate", 1, 2): ("gate", 0, 7),
        **{("gate", 1, c): ("up", 0, c + 2) for c in range(3, 6)},
        ("gate", 1, 6): ("up", 1, ON_GPSIMD),
        ("up", 1, 0): ("up", 0, 4),
        ("up", 1, ON_GPSIMD): ("gate", 1, 0),
        ("up", 1, 1): ("gate", 1, ON_GPSIMD),
        ("up", 1, 2): ("gate", 1, 1),
        ("up", 1, 3): ("gate", 1, 2),
        ("up", 1, 4): ("up", 1, 0),
        ("up", 1, 5): ("up", 1, 2),
        ("up", 1, 6): ("up", 1, 3),
    }
    fresh = [("gate", 0, c) for c in range(5)] + [("up", 0, c) for c in range(3)]
    banks = {sums: bank for bank, sums in enumerate(fresh)}
    while len(banks) < 4 * CHUNKS:
        for sums, before in follows.items():
            if before in banks:
                banks[sums] = banks[before]
    return banks


BANK = psum_banks()
LAST_SUMS = [("gate", 1, 3), ("up", 1, 1), ("gate", 1, 4), ("up", 1, 4), ("gate", 1, 5), ("gate", 1, 6)]
Y_BANKS = [BANK[sums] for sums in LAST_SUMS + [("up", 1, 5), ("up", 1, 6), ("gate", 1, 3)]]

SPANS = [(0, HALF), (HALF, J - CHUNK), (J - CHUNK, J)]
MIDDLE, LAST = 1, 2

ROUNDED = GROUP * PACK * 2
AT_WU1_BF = PACK * HALF * 4
AT_WG1_BF = AT_WU1_BF + ROUNDED // 2
AT_H01 = AT_WU1_BF + ROUNDED
AT_WD8_DEALT = AT_H01 + P
AT_H11 = AT_WD8_DEALT + N * 4
ACT = GROUP * 4
ALIGN = 64
AT_WG1_GPSIMD = AT_H11 + ROUNDED
AT_WG1_SCALAR = AT_WG1_GPSIMD + WG1_SPLIT * PACK * PACK * 4
AT_ACT_LATE = AT_WG1_SCALAR + QUARTER // 2
AT_ACT1 = AT_ACT_LATE + (CHUNKS - EARLY_SILUS) * ACT
AT_WU1_SCALAR = AT_ACT1 + CHUNKS * ACT - ALIGN
AT_WU1_GPSIMD = AT_WU1_SCALAR + (P - WU1_SPLIT) * PACK * PACK * 4


def tile_list_gmlpt_silu_mix_gateP_kernel(
    tc, tab_words, tab_scales, wg, wu, wd8_words, wd8_scales, wd4_words, wd4_scales, gT, offs, out_0, out_1, out_2
):
    nc = tc.nc
    with ExitStack() as ctx:
        held = ctx.enter_context(tc.tile_pool(name="held", bufs=1))
        reused = ctx.enter_context(tc.tile_pool(name="reused", bufs=1))
        psum = ctx.enter_context(tc.psum_pool(name="psum", bufs=1))

        offsets = held.tile([P, J // 16], U16, name="offsets")
        nc.sync.dma_start(offsets[:], offs)

        def load_weight(part, w, c0, pieces):
            rows = w.rearrange("(p i) r -> p i r", i=PACK)[:, :, c0 : c0 + part.shape[2]]
            for u in range(pieces):
                some = slice(u * PACK // pieces, (u + 1) * PACK // pieces)
                nc.sync.dma_start(part[:, some], rows[:, some])
            return part

        def half_tile(name):
            return held.tile([P, PACK, GROUP // 2], F32, name=name, align_bytes=64)

        def scale_rows(tile, first, r):
            return tile[first + r : P : QUADRANT, :].bitcast(I32)

        def load_scale_rows(tile, first, scales):
            for r in range(PACK):
                nc.sync.dma_start(scale_rows(tile, first, r), scales[0].bitcast(I32)[r:SCALE_ROWS:PACK, :])

        wg0_parts = [load_weight(half_tile("wg0_low"), wg, 0, 2)]

        tab_s = held.tile([P, T], U8, name="tab_s", align_bytes=64)
        nc.gpsimd.memset(tab_s[:].bitcast(I32), 0)
        load_scale_rows(tab_s, 0, tab_scales)

        wd_s = held.tile([P, N], U8, name="wd_s", align_bytes=64)
        nc.gpsimd.memset(wd_s[:].bitcast(I32), 0)

        wg0_parts.append(load_weight(half_tile("wg0_high"), wg, GROUP // 2, 1))
        tab_w = reused.tile([P, T], I32, name="tab_w", offset=AT_WU1_BF)
        nc.sync.dma_start(tab_w[:], tab_words[0].rearrange("p t i -> p (t i)").bitcast(I32))
        wu0_scalar = held.tile([P, PACK, WU0_SPLIT * PACK], F32, name="wu0_scalar", tag="wu0_scalar", align_bytes=64)
        load_weight(wu0_scalar, wu, 0, 1)
        wu0_second = held.tile([P, PACK, (WU0_LAST - WU0_SPLIT) * PACK], F32, name="wu0_second", align_bytes=64)
        load_weight(wu0_second, wu, WU0_SPLIT * PACK, 1)
        wu0_last = held.tile([P, PACK, GROUP - WU0_LAST * PACK], F32, name="wu0_last", tag="wu0_last", align_bytes=64)
        load_weight(wu0_last, wu, WU0_LAST * PACK, 1)
        wg1_gpsimd = reused.tile([P, PACK, WG1_SPLIT * PACK], F32, name="wg1_gpsimd", offset=AT_WG1_GPSIMD)
        load_weight(wg1_gpsimd, wg, GROUP, 1)
        wg1_scalar = reused.tile([P, PACK, GROUP - WG1_SPLIT * PACK], F32, name="wg1_scalar", offset=AT_WG1_SCALAR)
        load_weight(wg1_scalar, wg, GROUP + WG1_SPLIT * PACK, 1)
        load_scale_rows(wd_s, 0, wd4_scales)
        wu1_gpsimd = reused.tile([P, PACK, WU1_SPLIT * PACK], F32, name="wu1_gpsimd", offset=AT_WU1_GPSIMD)
        load_weight(wu1_gpsimd, wu, GROUP, 1)
        wu1_scalar = reused.tile([P, PACK, GROUP - WU1_SPLIT * PACK], F32, name="wu1_scalar", offset=AT_WU1_SCALAR)
        load_weight(wu1_scalar, wu, GROUP + WU1_SPLIT * PACK, 1)
        wd4_w = held.tile([P, 2 * N], U8, name="wd4_w", align_bytes=64)
        nc.sync.dma_start(wd4_w[:].bitcast(I32), wd4_words[0].bitcast(I32))
        load_scale_rows(wd_s, WD8_SCALES_AT, wd8_scales)
        wd8_w = held.tile([P, N], I32, name="wd8_w", align_bytes=64)
        nc.sync.dma_start(wd8_w[:], wd8_words[0].rearrange("p n i -> p (n i)").bitcast(I32))
        gate_rows = []
        for t in range(PACK):
            rows = held.tile([P, T], F32, name=f"gate_rows{t}")
            nc.sync.dma_start(rows[:], gT.rearrange("(p t) c -> p t c", t=PACK)[:, t, :])
            gate_rows.append(rows)

        warm = held.tile([P, 1], F32, name="warm")
        nc.vector.memset(warm[:], 0.0)
        warm_out = held.tile([P, 1], F32, name="warm_out")
        nc.scalar.activation(warm_out[:], warm[:], SILU)

        v_s = held.tile([P, J], U8, name="v_s", align_bytes=64)
        nc.vector.tensor_copy(v_s[:], tab_s[:].indirect(offsets[:]))

        def round_places(engine, part, m_part, rounded, m0, m1, planes=slice(0, PACK)):
            ms = slice(m0 - m_part, m1 - m_part)
            if engine == "gpsimd":
                dealt = rounded.rearrange("p (t m i) -> p m t i", t=PACK, i=PACK)[:, m0:m1]
                nc.gpsimd.tensor_scalar(dealt, part.rearrange("p i (m t) -> p m t i", t=PACK)[:, ms], 1.0, 0.0, MULT, ADD)
            else:
                dealt = rounded.rearrange("p (t m u e) -> p m u t e", t=PACK, u=2, e=2)[:, m0:m1, :, planes]
                copy = nc.scalar.copy if engine == "scalar" else nc.vector.tensor_copy
                copy(dealt, part.rearrange("p (u e) (m t) -> p m u t e", e=2, t=PACK)[:, ms, :, planes])

        def quantize_weight(name, rounded, calls):
            planes = PACK // calls
            quantised = []
            for u in range(calls):
                codes = held.tile([P, planes * P], U32, name=f"{name}_{u}_c", align_bytes=64)
                scales = held.tile([P, planes * P], U8, name=f"{name}_{u}_s", align_bytes=64)
                values = rounded[:, u * planes * GROUP : (u + 1) * planes * GROUP]
                nc.vector.quantize_mx(out=codes[:].bitcast(FP8X4), scales=scales[:], in_=values)
                quantised += [(codes[:, t * P : (t + 1) * P], scales[:, t * P : (t + 1) * P]) for t in range(planes)]
            return quantised

        wg_q, wu_q = {}, {}
        wg0_bf = held.tile([P, GROUP * PACK], BF16, name="wg0_bf", align_bytes=64)
        for k in range(2):
            round_places("scalar", wg0_parts[k][:], k * HALF_M, wg0_bf[:], k * HALF_M, (k + 1) * HALF_M)
        wg_q[0] = quantize_weight("wg0", wg0_bf[:], 1)

        v_w = {}

        def gather_words(j0, j1, tag):
            words = held.tile([P, j1 - j0], U32, name=f"v_w{j0}", tag=tag, align_bytes=64)
            nc.vector.tensor_copy(words[:], tab_w[:].bitcast(U32).indirect(offsets[:, j0 // 16 : j1 // 16]))
            for j in range(j0, j1, CHUNK):
                v_w[j // CHUNK] = words[:, j - j0 : j - j0 + CHUNK]

        for j0, j1 in WORD_PIECES:
            gather_words(j0, j1, f"v_w{j0}")

        def up_sums(wq, c, bank):
            acc = psum.tile([P, PACK, CHUNK], F32, name="acc", tag=f"bank{bank}")
            for t in range(PACK):
                codes, scales = wq[t]
                nc.tensor.matmul_mx(
                    out=acc[:, t, :],
                    lhsT=codes.bitcast(FP8X4),
                    lhsT_scale=scales,
                    rhs=v_w[c].bitcast(FP8X4),
                    rhs_scale=v_s[:, c * CHUNK : (c + 1) * CHUNK],
                    start=True,
                    stop=True,
                )
            return acc[:].rearrange("p t j -> p j t")

        acts = {}

        def gate_silu(b, c, act):
            acts[b, c] = act
            nc.scalar.activation(act, up_sums(wg_q[b], c, BANK["gate", b, c]), SILU)

        wu0_bf = held.tile([P, GROUP * PACK], BF16, name="wu0_bf", align_bytes=64)
        round_places("scalar", wu0_scalar[:], 0, wu0_bf[:], 0, WU0_SPLIT)
        act_early = held.tile([P, EARLY_SILUS, CHUNK, PACK], F32, name="act_early", tag="wu0_scalar", align_bytes=64)
        for c in range(EARLY_SILUS):
            gate_silu(0, c, act_early[:, c])

        round_places("vector", wu0_second[:], WU0_SPLIT, wu0_bf[:], WU0_SPLIT, WU0_LAST)
        for pair in (slice(0, 2), slice(2, PACK)):
            round_places("vector", wu0_last[:], WU0_LAST, wu0_bf[:], WU0_LAST, P, pair)
        wu_q[0] = quantize_weight("wu0", wu0_bf[:], 2)
        gather_words(*LATE_WORDS, "wu0_last")

        h_bf00 = held.tile([P, HALF * PACK], BF16, name="h_bf00", align_bytes=64)
        h_bf10 = held.tile([P, HALF * PACK], BF16, name="h_bf10", tag="h_bf10", align_bytes=64)
        h_bf = {(0, 0): h_bf00, (1, 0): h_bf10}
        h_q = [[], []]

        def hidden(b, c):
            bank = BANK["up", b, c]
            place = c % HALF_CHUNKS * GROUP
            rounded = h_bf[b, c // HALF_CHUNKS][:, place : place + GROUP].rearrange("p (j t) -> p j t", t=PACK)
            if (b, c) == (1, ON_GPSIMD):
                ub_f = held.tile([P, CHUNK, PACK], F32, name="ub_f", align_bytes=64)
                nc.scalar.copy(ub_f[:], up_sums(wu_q[b], c, bank))
                nc.gpsimd.tensor_tensor(rounded, ub_f[:], acts[b, c], MULT)
            else:
                nc.vector.tensor_tensor(rounded, up_sums(wu_q[b], c, bank), acts[b, c], MULT)

        def quantize_hidden(b, j0, codes, scales, calls):
            width = scales.shape[1] // calls
            for j in range(0, scales.shape[1], width):
                place = (j0 % HALF + j) * PACK
                nc.vector.quantize_mx(
                    out=codes[:, j : j + width].bitcast(FP8X4),
                    scales=scales[:, j : j + width],
                    in_=h_bf[b, j0 // HALF][:, place : place + width * PACK],
                )
            h_q[b].append((j0, j0 + scales.shape[1], codes, scales))

        wg1_bf = reused.tile([P, GROUP * PACK], BF16, name="wg1_bf", offset=AT_WG1_BF)
        round_places("gpsimd", wg1_gpsimd[:], 0, wg1_bf[:], 0, WG1_SPLIT)
        round_places("scalar", wg1_scalar[:], WG1_SPLIT, wg1_bf[:], WG1_SPLIT, P)
        for c in range(HALF_CHUNKS):
            hidden(0, c)
        act_late = reused.tile([P, CHUNKS - EARLY_SILUS, CHUNK, PACK], F32, name="act_late", offset=AT_ACT_LATE)
        for c in range(EARLY_SILUS, CHUNKS):
            gate_silu(0, c, act_late[:, c - EARLY_SILUS])
        wg_q[1] = quantize_weight("wg1", wg1_bf[:], 1)
        codes = held.tile([P, QUARTER], U32, name="h_c_quarter", align_bytes=64)
        scales = reused.tile([P, QUARTER], U8, name="h_s_quarter", offset=AT_WG1_SCALAR - QUARTER // 2)
        quantize_hidden(0, 0, codes, scales, 1)
        wu1_bf = reused.tile([P, GROUP * PACK], BF16, name="wu1_bf", offset=AT_WU1_BF)
        round_places("gpsimd", wu1_gpsimd[:], 0, wu1_bf[:], 0, WU1_SPLIT)
        round_places("scalar", wu1_scalar[:], WU1_SPLIT, wu1_bf[:], WU1_SPLIT, P)
        h_bf[0, 1] = reused.tile([P, HALF * PACK], BF16, name="h_bf01", offset=AT_H01)
        for c in range(HALF_CHUNKS, CHUNKS):
            hidden(0, c)
        wu_q[1] = quantize_weight("wu1", wu1_bf[:], 2)
        for j0, j1 in ((QUARTER, HALF), (HALF, J)):
            codes = reused.tile([P, j1 - j0], U32, name=f"h_c{j0}", offset=AT_WU1_GPSIMD + (j0 - QUARTER) * 4)
            scales = reused.tile([P, j1 - j0], U8, name=f"h_s{j0}", offset=AT_WU1_SCALAR + ALIGN + j0 - QUARTER)
            quantize_hidden(0, j0, codes, scales, 1)

        def deal(copy, dealt, source, t0, t1, run):
            copy(
                dealt.rearrange("p (t a m) -> p a t m", t=t1 - t0, m=run),
                source.rearrange("p (a m t) -> p a t m", t=PACK, m=run)[:, :, t0:t1],
            )

        h_bf[1, 1] = reused.tile([P, HALF * PACK], BF16, name="h_bf11", offset=AT_H11)
        wd_sd = [reused.tile([P, P], U8, name="wd_sd_first", offset=AT_H01)[:]]
        deal(nc.gpsimd.tensor_copy, wd_sd[0], wd_s[:], 0, 1, 16)
        wd8_d = reused.tile([P, N], I32, name="wd8_d", offset=AT_WD8_DEALT)
        deal(nc.gpsimd.tensor_copy, wd8_d[:], wd8_w[:], 0, PACK, 4)
        wd4_d = []

        y_first = reused.tile([P, PACK * HALF - CHUNK], F32, name="y_first", offset=0, align_bytes=64)
        y_apart = held.tile([P, CHUNK], F32, name="y_apart")
        y_second = held.tile([P, PACK * HALF], F32, name="y_second")

        def y_f(t, j0, j1):
            if j0 >= HALF:
                return y_second[:, t * HALF + j0 - HALF : t * HALF + j1 - HALF]
            if (t, j0) == (PACK - 1, HALF - CHUNK):
                return y_apart[:]
            return y_first[:, t * HALF + j0 : t * HALF + j1]

        def pieces(t, j0, j1):
            if (t, j1) == (PACK - 1, HALF):
                return [(j0, j1 - CHUNK), (j1 - CHUNK, j1)]
            return [(j0, j1)]

        out_f = [held.tile([P, PACK, HALF], F32, name="out_f0")[:]]
        out_bf = held.tile([P, J * PACK], BF16, name="out_bf", align_bytes=64)
        out_c = held.tile([P, J], U32, name="out_c", align_bytes=64)
        out_s = held.tile([P, J], U8, name="out_s", align_bytes=64)

        def down_product(t, j0, j1, bank):
            y = psum.tile([P, j1 - j0], F32, name="y", tag=f"bank{bank}")
            weights = [
                (wd8_d[:, t * P : (t + 1) * P].bitcast(FP8X4), wd_sd[t][WD8_SCALES_AT:P, :]),
                (wd4_d[t].bitcast(FP4X4), wd_sd[t]),
            ]
            passes = [
                (b, max(j0, q0), min(j1, q1), q0, codes, scales)
                for b in range(2)
                for q0, q1, codes, scales in h_q[b]
                if q0 < j1 and j0 < q1
            ]
            for turn, (b, c0, c1, q0, codes, scales) in enumerate(passes):
                nc.tensor.matmul_mx(
                    out=y[:, c0 - j0 : c1 - j0],
                    lhsT=weights[b][0],
                    lhsT_scale=weights[b][1],
                    rhs=codes[:, c0 - q0 : c1 - q0].bitcast(FP8X4),
                    rhs_scale=scales[:, c0 - q0 : c1 - q0],
                    start=turn == 0,
                    stop=turn == len(passes) - 1,
                )
            for a, b in pieces(t, j0, j1):
                nc.scalar.copy(y_f(t, a, b), y[:, a - j0 : b - j0])

        def gate_plane(s, t):
            j0, j1 = SPANS[s]
            for a, b in pieces(t, j0, j1):
                nc.vector.tensor_tensor(
                    out_f[s][:, t, a - j0 : b - j0],
                    gate_rows[t][:].indirect(offsets[:, a // 16 : b // 16]),
                    y_f(t, a, b),
                    MULT,
                )
            stored = 2 if s == MIDDLE else PACK
            if (t + 1) % stored == 0:
                pair = slice(t + 1 - stored, t + 1)
                nc.sync.dma_start(out_0.rearrange("(p t) j -> p t j", t=PACK)[:, pair, j0:j1], out_f[s][:, pair, :])
                if s == MIDDLE:
                    nc.scalar.copy(
                        out_bf[:, j0 * PACK : j1 * PACK].rearrange("p (j t) -> p j t", t=PACK)[:, :, pair],
                        out_f[s][:, pair, :].rearrange("p t j -> p j t"),
                    )

        def round_span(s):
            j0, j1 = SPANS[s]
            nc.scalar.copy(
                out_bf[:, j0 * PACK : j1 * PACK].rearrange("p (a j t) -> p a t j", t=PACK, j=4),
                out_f[s].rearrange("p t (a j) -> p a t j", j=4),
            )

        act1 = reused.tile([P, CHUNKS, CHUNK, PACK], F32, name="act1", offset=AT_ACT1)
        for turn in range(AHEAD_OF_COPY):
            gate_silu(1, GROUP1_TURNS[turn], act1[:, turn])
        for c in GROUP1_TURNS:
            hidden(1, c)
            if c == ON_GPSIMD:
                gate_silu(1, GROUP1_TURNS[AHEAD_OF_COPY], act1[:, AHEAD_OF_COPY])
                wd4_first = reused.tile([P, 2 * P], U8, name="wd4_first", offset=AT_WU1_BF)
                deal(nc.scalar.copy, wd4_first[:].bitcast(U16), wd4_w[:].bitcast(U16), 0, 1, 8)
                for late in range(AHEAD_OF_COPY + 1, CHUNKS):
                    gate_silu(1, GROUP1_TURNS[late], act1[:, late])
                wd4_rest = reused.tile([P, 2 * (N - P)], U8, name="wd4_rest", offset=AT_WU1_BF + 2 * P)
                deal(nc.scalar.copy, wd4_rest[:].bitcast(U16), wd4_w[:].bitcast(U16), 1, PACK, 8)
                wd4_d += [wd4_first[:]] + [wd4_rest[:, 2 * t * P : 2 * (t + 1) * P] for t in range(PACK - 1)]
            if c == HALF_CHUNKS:
                h_c10 = held.tile([P, HALF], U32, name="h_c10", align_bytes=64)
                quantize_hidden(1, 0, h_c10, held.tile([P, HALF], U8, name="h_s10", align_bytes=64), 1)
                wd_sd_rest = held.tile([P, N - P], U8, name="wd_sd_rest", tag="h_bf10", align_bytes=64)
                deal(nc.gpsimd.tensor_copy, wd_sd_rest[:], wd_s[:], 1, PACK, 16)
                wd_sd += [wd_sd_rest[:, t * P : (t + 1) * P] for t in range(PACK - 1)]
                down_product(0, 0, HALF // 2, Y_BANKS[0])
                down_product(0, HALF // 2, HALF, Y_BANKS[1])
        h_c11 = held.tile([P, HALF], U32, name="h_c11", align_bytes=64)
        quantize_hidden(1, HALF, h_c11, held.tile([P, HALF], U8, name="h_s11", align_bytes=64), 2)
        for t in range(1, PACK):
            down_product(t, 0, HALF, Y_BANKS[1 + t])
        for t in range(PACK):
            down_product(t, HALF, J, Y_BANKS[1 + PACK + t])
        for t in range(PACK):
            gate_plane(0, t)
        round_span(0)
        for j0, j1 in SPANS[1:]:
            late = reused.tile([P, PACK, j1 - j0], F32, name=f"out_f{j0}", offset=(j0 - HALF) * PACK * 4)
            out_f.append(late[:])
        for s in range(1, len(SPANS)):
            for t in range(PACK):
                gate_plane(s, t)
        round_span(len(SPANS) - 1)
        for j0, j1 in SPANS:
            nc.vector.quantize_mx(
                out=out_c[:, j0:j1].bitcast(FP8X4), scales=out_s[:, j0:j1], in_=out_bf[:, j0 * PACK : j1 * PACK]
            )
        for j0, j1 in ((0, HALF), (HALF, J)):
            nc.sync.dma_start(
                out_1[0].rearrange("p j i -> p (j i)").bitcast(I32)[:, j0:j1], out_c[:, j0:j1].bitcast(I32)
            )
        for r in range(PACK):
            queue = nc.scalar if r % 2 else nc.sync
            queue.dma_start(out_2[0].bitcast(I32)[r:SCALE_ROWS:PACK, :], scale_rows(out_s, 0, r))
